import numpy as np, ml_dtypes
CORES = [1,5,17,21,33,37,49,53]
N = 8
import mx_ref
BF = ml_dtypes.bfloat16
def gentries(a):
    return np.ascontiguousarray(a.reshape(8, 16, -1).transpose(0, 2, 1)).reshape(8, -1)
def gtable(e):
    e = np.asarray(e); return np.ascontiguousarray(e.reshape(8, -1, 16).transpose(0, 2, 1)).reshape(128, -1).astype(np.int32)
def gcols(t, e):
    v = np.concatenate([t.reshape(8, 16, -1, 4), np.zeros((8, 16, 1, 4), BF)], axis=2)
    return np.ascontiguousarray(np.stack([v[g][:, e[g]] for g in range(8)])).reshape(128, -1)
def gpick(z, e):
    return np.concatenate([z[16 * g:16 * g + 16][:, e[g]] for g in range(8)])
def tile(rs):
    return np.stack(rs, axis=2).reshape(128, -1).astype(BF)
def pick(q, e):
    c = np.concatenate([q[0].reshape(128, -1, 4), np.zeros((128, 1, 4), np.uint8)], axis=1); s = np.concatenate([q[1], np.ones((16, 1), np.uint8)], axis=1)
    return (np.ascontiguousarray(c[:, e].reshape(128, -1)), np.ascontiguousarray(s[:, e]))
def join(*qs):
    return (np.concatenate([q[0] for q in qs], axis=1), np.concatenate([q[1] for q in qs], axis=1))
def put(q, e, v):
    c, s = q[0].reshape(128, -1, 4).copy(), q[1].copy(); c[:, e] = v[0].reshape(128, -1, 4); s[:, e] = v[1]
    return (c.reshape(128, -1), s)
def pk(c, s):
    return (np.ascontiguousarray(c), mx_ref.live(s))
def emit(q):
    return q[0], q[1]
def packed(v, rng):
    q = [mx_ref.quantize(np.ascontiguousarray(v[r])) for r in range(N)]
    return np.stack([a for a, b in q]), np.stack([mx_ref.plane(b, rng) for a, b in q])
def values_of_codes():
    e, c = np.zeros((128, 128, 4), np.float32), np.zeros((128, 2, 4), np.uint8)
    e[np.arange(128), np.arange(128), 0] = 1
    c[:127, :, 0] = np.arange(256).reshape(2, 128).T[:127]
    return mx_ref.matmul(mx_ref.quantize(e.reshape(128, 512).astype(BF)), (c.reshape(128, 8), np.full((16, 2), 127, np.uint8))).T.reshape(-1).astype(np.float64)
CODE_VALUE, SCALE_VALUE = values_of_codes(), 2.0 ** (np.arange(256) - 127.0)
def decode(q):
    return (CODE_VALUE[q[0]].reshape(16, 8, -1, 4) * SCALE_VALUE[q[1]][:, None, :, None] + 0.0).reshape(128, -1).astype(np.float32)
def f(rng, *shape):
    return mx_ref.flush((rng.standard_normal(shape, dtype=np.float32) * np.exp2(rng.integers(-2, 3, shape[:-1] + (1,)))).astype(BF))
def wide(rng, *shape, cols=0):
    v = rng.standard_normal(shape, dtype=np.float32) * np.exp2(rng.integers(-12, 13, shape)).astype(np.float32)
    if cols: v *= np.repeat(np.exp2(rng.integers(-cols, cols + 1, shape[:-2] + (1, shape[-1] // 4))) * (rng.random(shape[:-2] + (1, shape[-1] // 4)) > 0.0625), 4, axis=-1).astype(np.float32)
    return mx_ref.flush(v.astype(BF))
C = 320
STEP = [1, 2, 4]
def numbers_of(rng):
    return {"x": np.array(f(rng, N, 128, 4 * C)), "u": np.array(f(rng, N, 128, 512)), "v": np.array(f(rng, N, 128, 512))}
def drawn(rng):
    e = np.tile(np.arange(C), (N, 8, 1))
    p, k, s, m = rng.permuted(e, axis=2), rng.permuted(e, axis=2), rng.permuted(e, axis=2), np.zeros_like(e)
    np.put_along_axis(m, s[:, :, ::2], s[:, :, 1::2], 2)
    np.put_along_axis(m, s[:, :, 1::2], s[:, :, ::2], 2)
    return p, k, m
def stored(p, k, m):
    return {"pg": np.stack([gtable(p[r]) for r in range(N)]), "kg": np.stack([gtable(k[r]) for r in range(N)]), "mg": np.stack([gtable(m[r]) for r in range(N)])}
def layers(rng):
    return np.array(f(rng, N, 128, 2048)).reshape(N, 8, 16, 4, 8, 16, 4)
def weights(rng, w):
    c, s = packed(np.ascontiguousarray(w).reshape(N, 128, 2048), rng)
    return {"wc": c, "ws": s}
def setup_inputs(rng):
    return {**numbers_of(rng), **stored(*drawn(rng)), **weights(rng, layers(rng))}
def setup_inputs_ties(rng):
    d = numbers_of(rng)
    o = rng.permutation(N)
    s = rng.integers(-1, 2, (N, 2, 8, C))
    s[o[0]] = 0
    s[o[1]] = 1
    s[o[2], 0] = np.where(np.arange(C) % 2 == 1, 1, rng.integers(-1, 1, (8, C)))
    x = d["x"].astype(np.float32).reshape(N, 8, 16, C, 4)
    u = d["u"].astype(np.float32).reshape(N, 128, 128, 4)
    for i in range(2):
        x[:, :, i] = 0
        x[:, :, i, :, 0] = s[:, i]
        u[:, :, i::16] = 0
        for h in range(0, 128, 16): u[:, h + i, h + i, 0] = 1
    p, k, m = drawn(rng)
    p[o[2]] = k[o[2]] = np.arange(C)
    m[o[2]] = np.arange(C) ^ 1
    w = layers(rng)
    w[:, :, :, :, :, :8] = 0
    return {"x": x.reshape(N, 128, 4 * C).astype(BF), "u": u.reshape(N, 128, 512).astype(BF), "v": d["v"], **stored(p, k, m), **weights(rng, w)}
def setup_inputs_near(rng):
    d = numbers_of(rng)
    o = rng.permutation(N)
    k = np.where(o % 2 == 0, 2.0 ** -30, 1.0)
    x = np.zeros((N, 8, 16, C, 4))
    s = rng.integers(-1, 2, (N, 2, 8, C)) * k[:, None, None, None]
    for i in range(2):
        x[:, :, 2 * i, :, 0] = 1.125 * s[:, i]
        x[:, :, 2 * i + 1, :, 0] = -1.25 * s[:, i]
    x[:, :, 9, :, 0] = rng.choice([-1.0, 1.0], (N, 8, C)) * 2.0 ** -17
    x[:, :, 10:] = rng.choice([-1.0, 1.0], (N, 8, 6, C, 4)) * (1 + 0.125 * rng.integers(0, 8, (N, 8, 6, C, 4))) * np.exp2(-12.0 - rng.integers(0, 4, (N, 8, 6, C, 4)))
    u = d["u"].astype(np.float32).reshape(N, 128, 128, 4)
    u[:, :, ::16] = 0
    u[:, :, 1::16] = 0
    w = layers(rng)
    w[:, :, :8] = 0
    w[:, :, :, :, :, :10] = 0
    for r in range(N):
        for g in rng.permutation(8)[:4]: x[r, g, 0, rng.integers(C), 0] = 2.0 ** 30 * rng.choice([-1.0, 1.0])
        if o[r] == 0:
            x[r, :, :8] = 0
            x[r, :, 0, :, 0] = 2.0 ** -30
        for g in range(8):
            h = 16 * g
            if o[r] == 0:
                u[r, h + 4, h, 0] = 2.0 ** -30
                u[r, h + 4, h + 1, 0] = -2.0 ** -30
                w[r, g, 8, 0, g, 4, 0] = 2.0 ** -8
                w[r, g, 9, 0, g, 4, 0] = 2.0 ** -22
            else:
                for i in range(2):
                    u[r, h + 2 * i, h + i, 0] = 1.125 * k[r]
                    u[r, h + 2 * i + 1, h + i, 0] = k[r]
    return {"x": x.astype(np.float32).reshape(N, 128, 4 * C).astype(BF), "u": u.reshape(N, 128, 512).astype(BF), "v": d["v"], **stored(*drawn(rng)), **weights(rng, w)}
def setup_inputs_odd(rng):
    d = numbers_of(rng)
    x = (1.0 + (2 * rng.integers(0, 64, (N, 16, 8, C, 4)) + 1) * 2.0 ** -7) * np.exp2(-rng.integers(0, 7, (N, 16, 8, C, 4)).astype(np.float64)) * rng.choice([-1.0, 1.0], (N, 16, 8, C, 4))
    x[:, ::2, 0, :, 0] = 1.96875 * 2.0 ** 8 * rng.choice([-1.0, 1.0], (8, 1))
    x[:, 1::2, 0, :, 0] = 1.96875 * 2.0 ** 8 * rng.choice([-1.0, 1.0], (N, 8, C))
    u = d["u"].astype(np.float32).reshape(N, 16, 8, 128, 4)
    u[:, :, 0, ::16] = 0
    u[:, :, :, 1::16] = 0
    h = rng.permutation(8) % 4
    for g in range(8):
        x[:, 2 * g, 1, :, 0] = (8 + rng.integers(0, 2, (N, C))) * 2.0 ** (int(h[g]) - 9)
        x[:, 2 * g, 2, :, 0] = -2.0 ** (int(h[g]) - 6)
        u[:, 2 * g, 1:3, 16 * g + 1, 0] = 1
    w = layers(rng)
    for i in (0, 8):
        w[:, :, i] = 0
        w[:, :, :, :, :, i] = 0
    w[:, :, :, 0, :, 1:3] = 0
    for g in range(8): w[:, g, 0, 0, g, 0, 0] = -0.5
    p, k, m = drawn(rng)
    t = int(rng.integers(N))
    p[t] = m[t] = np.arange(C)
    k[t] = rng.permutation(C)
    return {"x": x.astype(np.float32).reshape(N, 128, 4 * C).astype(BF), "u": u.reshape(N, 128, 512).astype(BF), "v": d["v"], **stored(p, k, m), **weights(rng, w)}
def setup_inputs_ends(rng):
    d = numbers_of(rng)
    o, ep, ek, em = [rng.permutation(N) % 4 for i in range(4)]
    s = rng.choice([-1.0, 1.0], (N, 128, C, 4))
    s[o == 0] = -1
    s[o == 1] = rng.choice([-1.0, 1.0], (N, 1, C, 1))[o == 1]
    x = s * (0.90 + 0.02 * rng.random((N, 128, C, 4))) * 2.0 ** 30
    tiny = (1 + 0.125 * rng.integers(0, 8, (N, 128, C, 4))) * 2.0 ** -30
    x[o == 3] = (s * tiny)[o == 3]
    x[:, 8:16] = tiny[:, 8:16]
    u = d["u"].astype(np.float32).reshape(N, 128, 128, 4)
    for r in range(N):
        h = rng.permutation(8)
        size = 2.0 ** -30 if o[r] == 3 else 2.0 ** 30
        u[r, :, ::16] = ((h % 2 * 2 - 1) * size)[None, :, None]
        u[r, :, 1::16] = ((h // 2 % 2 * 2 - 1) * size)[None, :, None]
    v = rng.choice([-1.0, 1.0], (N, 128, 512)) * np.where(o % 2 == 0, 2.0 ** 30, 2.0 ** -30)[:, None, None]
    p, k, m = drawn(rng)
    line = np.arange(C)
    p[ep == 0] = line
    p[ep == 1] = (line + 1) % C
    p[ep == 2] = C - 1 - line
    k[ek == 0] = line
    k[ek == 1] = C - 1 - line
    k[ek == 2] = (line + C - 1) % C
    m[em == 0] = line
    m[em == 1] = C - 1 - line
    m[em == 2] = line ^ 1
    w = np.zeros((N, 128, 4, 128, 4), np.float32)
    i = np.arange(128)
    for b in range(4): w[:, i, b, i, b] = np.where((i >= 8) & (i < 16), np.where(o == 3, 2.0 ** 8, 2.0 ** -8)[:, None], -0.25)
    return {"x": x.astype(np.float32).reshape(N, 128, 4 * C).astype(BF), "u": u.reshape(N, 128, 512).astype(BF), "v": v.astype(np.float32).astype(BF), **stored(p, k, m), **weights(rng, w.astype(BF))}
def setup_inputs_spread(rng):
    d = setup_inputs(rng)
    d["x"] = wide(rng, N, 128, 4 * C, cols=6)
    return d
def check_inputs(d):
    b = []
    for k in ("x", "u", "v"):
        a = np.abs(d[k].astype(np.float32))
        if not (np.isfinite(a).all() and ((a == 0) | (a >= 2.0 ** -30) & (a <= 2.0 ** 30)).all()): b.append("a value of " + k)
    none, least, most = [emit(mx_ref.quantize(np.full((128, 16), k, np.float32).astype(BF)))[1][0, 0] for k in (0.0, 2.0 ** -8, 2.0 ** 8)]
    top = emit(mx_ref.quantize(np.full((128, 16), 1.9921875, np.float32).astype(BF)))[0][0, 0] & 0x7F
    line = np.arange(C)
    for r in range(N):
        for k in ("pg", "kg"):
            if not (np.sort(gentries(d[k][r]), axis=1) == line).all(): b.append(k + ": no permutation")
        m = gentries(d["mg"][r])
        if not ((m >= 0) & (m < C)).all(): b.append("an entry of mg")
        elif not (np.take_along_axis(m, m, 1) == line).all(): b.append("mg: a mate's mate")
        if ((d["wc"][r] == 0x7F) | (d["wc"][r] == 0xFF)).any(): b.append("wc: a code that is no number")
        if ((d["wc"][r] & 0x7F) > top).any(): b.append("wc: a code that quantize_mx does not give")
        s = mx_ref.live(d["ws"][r])
        if ((s != none) & ((s < least) | (s > most))).any(): b.append("ws: a scale out of range")
    return b
def reference(x, u, v, pg, kg, mg, wc, ws):
    qu = [mx_ref.quantize(u[r]) for r in range(N)]
    lay = [pk(wc[r], ws[r]) for r in range(N)]
    p, k, m = [[gentries(a[r]).astype(np.int64) for r in range(N)] for a in (pg, kg, mg)]
    now = [x[r] for r in range(N)]
    for step in STEP:
        own, land, mosaic = [], [], []
        for r in range(N):
            q = mx_ref.quantize(now[r])
            s = mx_ref.matmul(qu[r], q)
            first = (s[::16] > 0).astype(np.int64)
            e = first + 2 * (s[1::16] > 0).astype(np.int64)
            at = np.zeros((8, C), np.int64)
            for g in range(8):
                power = np.ones(C, np.int64) if g == 0 else e[g - 1][at[g - 1]]
                a = k[r][g]
                for i in range(3): a = np.where(i < power, p[r][g][a], a)
                at[g] = a
            bit = np.take_along_axis(first, at, 1)
            p[r] = np.where(bit != np.take_along_axis(bit, m[r], 1), np.take_along_axis(p[r], m[r], 1), p[r])
            land.append(at)
            own.append(decode(q))
            mosaic.append(mx_ref.quantize(gcols(own[r].astype(BF), at)))
        made = []
        for r in range(N):
            h = [mx_ref.matmul(pick(lay[r], np.arange(128 * b, 128 * b + 128)), mosaic[r ^ step]) * np.float32(0.03125) for b in range(4)]
            made.append(tile([own[r][:, b::4] + gpick(h[b], land[r]) for b in range(4)]))
        now = made
    y, pl = np.zeros((N, 128, C), np.float32), np.zeros((N, 8, 2 * C), np.float32)
    oc, osc = np.zeros((N, 128, 4 * C), np.uint8), np.zeros((N, 16, C), np.uint8)
    for r in range(N):
        q = mx_ref.quantize(now[r])
        y[r] = mx_ref.matmul(mx_ref.quantize(v[r]), q)
        pl[r] = np.concatenate([land[r], p[r]], axis=1)
        oc[r], osc[r] = emit(q)
    return {"y": y, "pl": pl, "oc": oc, "osc": osc}

@@ -1,0 +1,448 @@
+import numpy as np
+from concourse.bass import DstId, RemoteDMATransfer
+from concourse.mybir import dt, AluOpType, AxisListType, ActivationFunctionType
+
+C = 320
+STEPS = [1, 2, 4]
+HALF = 160
+BLK = 112
+BIG = 1.0e29
+TW = 172
+
+SCRATCH = {}
+SEMAPHORES = ["vs", "ss", "ts", "gs", "lsem"]
+
+
+def _sb(name, cols, d):
+    SCRATCH[name] = ("sbuf", [128, cols], d)
+
+
+for _k in range(4):
+    _sb("x%d" % _k, 4 * C, "bfloat16")
+    _sb("qx%d" % _k, C, "float8_e4m3fn_x4")
+    _sb("sx%d" % _k, C, "uint8")
+for _k in range(3):
+    _sb("rq%d" % _k, C, "float8_e4m3fn_x4")
+    _sb("rs%d" % _k, C, "uint8")
+    _sb("al%d" % _k, 20, "uint16")
+    _sb("rl%d" % _k, 20, "uint16")
+    SEMAPHORES += ["aq%d" % _k, "ar%d" % _k]
+for _k in range(2):
+    _sb("pw%d" % _k, C, "bfloat16")
+for _n, _c, _d in [
+    ("ut", 512, "bfloat16"), ("vt", 512, "bfloat16"), ("zt", 4 * C, "bfloat16"),
+    ("gt", 4 * 352, "bfloat16"), ("st", 600, "bfloat16"), ("kt", 720, "bfloat16"), ("et", 2048, "bfloat16"), ("rt", 2048, "bfloat16"),
+    ("pint", C, "int32"), ("kg32", 20, "int32"), ("mg32", 20, "int32"),
+    ("ip", 1, "int32"), ("si", 4, "int32"), ("sc", 16, "float32"),
+    ("i16c", C, "bfloat16"), ("flat", C, "float32"), ("i20", 20, "int32"), ("iu", 24, "int32"), ("bt", 84, "float32"),
+    ("jw", 20, "float32"), ("mj", 20, "float32"), ("ro", 20, "uint16"), ("ml", 20, "uint16"), ("ul", 24, "uint16"),
+    ("dm", C, "bfloat16"), ("rm", C, "bfloat16"), ("mk", 84, "float32"), ("ident", 128, "bfloat16"),
+    ("oh", 48, "float32"), ("rw", 68, "float32"), ("pr", 48, "float32"), ("jk", 48, "float32"), ("al", 8, "float32"),
+    ("cw", 12, "float32"), ("co", 12, "float32"), ("cds", 4, "float32"), ("xc", 2, "float32"), ("gm", TW, "float32"),
+    ("tk", TW, "float32"), ("ti", TW, "int32"), ("pd", 147, "int32"),
+    ("tb1", C, "float32"), ("tb", C, "bfloat16"), ("sg", C, "bfloat16"), ("vb", C, "bfloat16"), ("ym", C, "bfloat16"), ("ysc", C, "bfloat16"),
+    ("lm", C, "bfloat16"), ("lsc", 3 * C, "bfloat16"), ("lg", 80, "uint16"), ("lw", 80, "float32"),
+    ("ind", 80, "float32"), ("im", 80, "float32"), ("ia", 40, "float32"), ("af", 20, "float32"),
+    ("xb", 60, "float32"), ("df", 20, "float32"), ("sf", 40, "float32"), ("sl", 20, "uint16"),
+    ("fo", 4 * C, "bfloat16"), ("fp", 4 * C, "bfloat16"), ("hs", 4 * C, "float32"), ("yo", C, "float32"), ("plo", 2 * C, "float32"),
+]:
+    _sb(_n, _c, _d)
+for _n, _c in [("qu", 128), ("up", 384), ("qv", 128), ("wq", 512), ("qe", 512), ("qr", 512), ("qk", 180), ("qg", 240), ("qh", 128), ("qs", 150), ("qz", C)]:
+    _sb(_n, _c, "float8_e4m3fn_x4")
+    _sb(_n + "s", _c, "uint8")
+for _k in range(8):
+    SCRATCH["b%d" % _k] = ("psum", [128, 512], "float32")
+LOADS = ["dx", "du", "dp", "dk", "dm", "dw", "dws", "dv", "oy", "oc", "os", "op"]
+LOADS = ["d_" + _n for _n in LOADS]
+SEMAPHORES += LOADS
+
+A = AluOpType
+ACT = ActivationFunctionType
+
+
+def rank_program(g, core, T, topo):
+    rank = T.rank_of(core)
+    if rank is None:
+        return
+    queues = {"v": (g.vector, "vs"), "s": (g.scalar, "ss"), "t": (g.tensor, "ts"), "g": (g, "gs"), "y": (g.sync, None)}
+    cnt, seen, lastw, readers = {}, {}, {}, {}
+
+    def need(qn, reads, writes, free=()):
+        out = {}
+        for k in list(reads) + list(writes):
+            for s, v in lastw.get(k, []):
+                if k in writes and k in free:
+                    continue
+                out[s] = max(out.get(s, 0), v)
+        for k in writes:
+            for s, v in readers.get(k, []):
+                out[s] = max(out.get(s, 0), v)
+        for s, v in out.items():
+            if seen.get((qn, s), 0) < v:
+                queues[qn][0].wait_ge(T.sem[s], v)
+                seen[(qn, s)] = v
+
+    def done(reads, writes, s, v, free=()):
+        for k in reads:
+            readers.setdefault(k, []).append((s, v))
+        for k in writes:
+            if k in free:
+                lastw.setdefault(k, []).append((s, v))
+            else:
+                lastw[k] = [(s, v)]
+                readers[k] = []
+
+    def op(qn, fn, reads, writes, free=()):
+        need(qn, reads, writes, free)
+        s = queues[qn][1]
+        cnt[s] = cnt.get(s, 0) + 1
+        fn().then_inc(T.sem[s], 1)
+        done(reads, writes, s, cnt[s], free)
+
+    def dma(qn, s, out, in_, reads, writes, free=()):
+        need(qn, reads, writes, free)
+        cnt[s] = cnt.get(s, 0) + 16
+        queues[qn][0].dma_start(out, in_).then_inc(T.sem[s], 16)
+        done(reads, writes, s, cnt[s], free)
+
+    def V(fn, reads, writes, free=()):
+        op("v", fn, reads, writes, free)
+
+    def ts(out, i, s1, s2, *ops):
+        return lambda: g.vector.tensor_scalar(out, i, s1, s2, *ops)
+
+    def tt(out, a, b, o):
+        return lambda: g.vector.tensor_tensor(out, a, b, o)
+
+    def cp(out, i):
+        return lambda: g.vector.tensor_copy(out, i)
+
+    def ms(ap, c):
+        return lambda: g.vector.memset(ap, c)
+
+    def act(out, i, f, **kw):
+        return lambda: g.scalar.activation(out, i, f, **kw)
+
+    def quant(q, src, tiles, n):
+        V(lambda: g.vector.quantize_mx(T[q][:, 0:n], T[(q + "s") if q[:2] != "qx" else "sx" + q[2:]][:, 0:n], T[src][:, 0:4 * n]), tiles, [q])
+
+    def mm(bank, n, w, ws, wa, x, xs, xa, reads, start=True, stop=True):
+        op("t", lambda: g.tensor.matmul_mx(T[bank][:, 0:n], T[w][:, wa:wa + 128], T[ws][:, wa:wa + 128], T[x][:, xa:xa + n], T[xs][:, xa:xa + n], start, stop),
+           reads, [bank], [] if start else [bank])
+
+    dma("y", "d_dx", T.x0[:], T.x[:], [], ["x0"])
+    dma("s", "d_du", T.ut[:], T.u[:], [], ["ut"])
+    for r in range(16):
+        dma("y" if r % 2 else "s", "d_dp", T.pint[r::16, :], T.pg[:], [], ["pint"], ["pint"])
+    dma("s", "d_dk", T.kg32[:], T.kg[:], [], ["kg32"])
+    dma("y", "d_dm", T.mg32[:], T.mg[:], [], ["mg32"])
+    dma("y", "d_dw", T.wq[:].bitcast(dt.uint8), T.wc[:], [], ["wq"])
+    dma("y", "d_dws", T.wqs[:], T.ws[:], [], ["wqs"])
+    dma("y", "d_dv", T.vt[:], T.v[:], [], ["vt"])
+
+    def iota(out, pattern, base, cm, reads, key):
+        op("g", lambda: g.iota(out, pattern, base, cm, allow_small_or_imprecise_dtypes=True), reads, [key])
+
+    iota(T.ip[:], [[0, 1]], 0, 1, [], "ip")
+    iota(T.iu[:], [[0, 3], [16, 8]], 0, 0, [], "iu")
+    iota(T.flat[:], [[1, C]], 0, 0, [], "flat")
+    iota(T.i16c[:], [[0, 20], [1, 16]], 0, 0, [], "i16c")
+    iota(T.i20[:], [[1, 20]], 0, 0, [], "i20")
+    iota(T.jk[:], [[0, 3], [1, 16]], 0, 0, [], "jk")
+    iota(T.rw[:, 0:48], [[0, 48]], 0, 0, [], "rwz")
+    iota(T.rw[:, 48:62], [[0, 14]], 1, 0, [], "rwo")
+    iota(T.rw[:, 62:66], [[1, 4]], -1, 0, [], "rwp")
+    RWA, RWB = ["rwz"], ["rwo", "rwp"]
+    for col, val in ((0, 1), (4, 3), (10, 3), (17, 1), (21, 3), (27, 3), (32, 15), (36, 3840), (37, -15), (42, 240), (43, 15)):
+        iota(T.rw[:, col:col + 1], [[0, 1]], val, 0, ["rwz"], "rw%d" % col)
+        RWA.append("rw%d" % col)
+    for col, val in ((49, 2), (50, 4), (51, 8), (52, 4), (53, 2), (56, 16), (57, 256), (58, 4096), (59, 256), (60, 16)):
+        iota(T.rw[:, col:col + 1], [[0, 1]], val, 0, ["rwo"], "rw%d" % col)
+        RWB.append("rw%d" % col)
+    iota(T.bt[:], [[0, 7], [1, 12]], 0, 0, [], "bt")
+    iota(T.gm[:, 84:88], [[0, 4]], 0, 0, [], "gmz")
+
+    V(ms(T.et[:], 0.0), [], ["etz"])
+    one = {n: T.sc[:, i:i + 1] for i, n in enumerate(("rf", "gf", "of", "pf", "b10", "b4", "r20", "zf", "e1", "ef", "h1", "h2", "hf", "g4"))}
+    V(ts(T.si[:, 0:1], T.ip[:], 15, None, A.bitwise_and), ["ip"], ["si0"])
+    V(ts(T.si[:, 1:2], T.ip[:], 4, None, A.arith_shift_right), ["ip"], ["si1"])
+    V(cp(one["pf"], T.ip[:]), ["ip"], ["pf"])
+    V(ts(T.si[:, 2:3], T.si[:, 1:2], 1, None, A.bitwise_and), ["si1"], ["si2"])
+    V(cp(T.sc[:, 0:3], T.si[:, 0:3]), ["si0", "si1", "si2"], ["rf"])
+    V(ts(one["b10"], one["rf"], 10.0, None, A.is_ge), ["rf"], ["b10"])
+    V(ts(one["b4"], one["rf"], 4.0, None, A.is_ge), ["rf"], ["b4"])
+    V(ts(one["r20"], one["rf"], 20.0, None, A.mult), ["rf"], ["r20"])
+    V(cp(T.ul[:, 16:24], T.iu[:, 16:24]), ["iu"], ["ul2"])
+    V(ts(T.ul[:, 0:8], T.iu[:, 0:8], one["b10"], None, A.add), ["iu", "b10"], ["ul0"])
+    V(ts(T.ul[:, 8:16], T.iu[:, 8:16], one["b4"], None, A.add), ["iu", "b4"], ["ul1"])
+    V(ts(T.ident[:], T.flat[:, 0:128], one["pf"], None, A.is_equal), ["flat", "pf"], ["ident"])
+    V(ts(T.dm[:], T.i16c[:], one["rf"], None, A.is_equal), ["i16c", "rf"], ["dm"])
+    V(ts(T.rm[:], T.i16c[:], 1.0, None, A.min), ["i16c"], ["rm"])
+    V(ts(T.ro[:], T.i20[:], one["r20"], None, A.add), ["i20", "r20"], ["ro"])
+
+    def S(out, i, f, reads, key, **kw):
+        op("s", act(out, i, f, **kw), reads, [key])
+
+    S(T.kt[:], T.et[:, 0:720], ACT.Copy, ["etz"], "ktz")
+    S(one["zf"], one["gf"], ACT.Relu, ["rf"], "zf", scale=-1.0, bias=1.0)
+    S(one["h1"], one["gf"], ACT.Relu, ["rf"], "h1", bias=-3.0)
+    S(one["g4"], one["gf"], ACT.Identity, ["rf"], "g4", bias=-4.0)
+    S(one["e1"], one["zf"], ACT.Identity, ["zf"], "e1", scale=-1.0, bias=1.0)
+    S(one["h2"], one["h1"], ACT.Sign, ["h1"], "h2")
+    S(one["ef"], one["of"], ACT.Identity, ["rf", "e1"], "ef", scale=-1.0, bias=one["e1"])
+    S(one["hf"], one["h2"], ACT.Identity, ["rf", "h2"], "hf", scale=8.0, bias=one["gf"])
+
+    S(T.gt[:, 4 * C:], T.et[:, 0:128], ACT.Copy, ["etz"], "gtz")
+    S(T.st[:], T.et[:, 0:600], ACT.Copy, ["etz"], "stz")
+
+    quant("qx0", "x0", ["x0"], C)
+    quant("qu", "ut", ["ut"], 128)
+    ULK = ["ul0", "ul1", "ul2"]
+    V(cp(T.up[:].bitcast(dt.uint32), T.qu[:].bitcast(dt.uint32).indirect(T.ul[:])), ["qu"] + ULK, ["up"])
+    op("s", act(T.ups[:], T.qus[:].indirect(T.ul[:]), ACT.Copy), ["qu"] + ULK, ["ups"])
+    V(ts(T.oh[:], T.jk[:], one["rf"], None, A.is_equal), ["jk", "rf"], ["oh"])
+    V(tt(T.pr[:], T.oh[:], T.rw[:, 0:48], A.mult), ["oh"] + RWA, ["pr"])
+    for i in range(3):
+        S(T.jk[:, 16 * i:16 * i + 16], T.pr[:, 16 * i:16 * i + 16], ACT.Copy, ["pr", "oh"], "alp%d" % i, accum_out=T.al[:, i:i + 1])
+    for i, (src, f) in enumerate(((0, "zf"), (0, "ef"), (1, "ef"), (2, "of"))):
+        S(T.al[:, 3 + i:4 + i], T.al[:, src:src + 1], ACT.Copy, ["alp%d" % src, "rf" if f == "of" else f], "alp%d" % (3 + i), scale=one[f])
+    S(T.cw[:, 0:2], T.rw[:, 58:60], ACT.Copy, RWB + ["alp4"], "cw0", scale=T.al[:, 4:5])
+    S(T.cw[:, 2:4], T.rw[:, 60:62], ACT.Copy, RWB + ["alp5"], "cw1", scale=T.al[:, 5:6])
+    S(T.cw[:, 4:8], T.rw[:, 51:55], ACT.Copy, RWB + ["alp6"], "cw2", scale=T.al[:, 6:7])
+    for b in range(4):
+        S(T.et[:, 512 * b + b:512 * (b + 1):4], T.ident[:], ACT.Copy, ["ident", "etz", "ktz", "stz", "gtz"], "et%d" % b)
+    ETK = ["et%d" % b for b in range(4)]
+    ETK.append("etz")
+
+    partner = [rank ^ s for s in STEPS]
+
+    def send(k, pairs, sem):
+        dst = T.cores[partner[k]]
+        rid, pid, _ = topo.addr(dst)
+        eng = topo.engines(core, dst)[:8]
+        m = sum(1 << e for e in eng)
+        for out, in_ in pairs:
+            g.remote_dma(out, in_, T.sem[sem], T.sem.lsem, pid, rid, m)
+            cnt["lsem"] = cnt.get("lsem", 0) + len(eng)
+            cnt[sem] = cnt.get(sem, 0) + len(eng)
+
+    def send_state(k):
+        need("g", ["qx%d" % k], [])
+        send(k, [(T["rq%d" % k][:].bitcast(dt.uint8), T["qx%d" % k][:].bitcast(dt.uint8)), (T["rs%d" % k][:], T["sx%d" % k][:])], "aq%d" % k)
+        done([], ["rq%d" % k], "aq%d" % k, cnt["aq%d" % k])
+
+    def send_list(k):
+        need("g", ["al%d" % k], [])
+        send(k, [(T["rl%d" % k][:], T["al%d" % k][:])], "ar%d" % k)
+        done([], ["rl%d" % k], "ar%d" % k, cnt["ar%d" % k])
+
+    def signs_mm(k):
+        q, s = "qx%d" % k, "sx%d" % k
+        mm("b0", C, "up", "ups", 0, q, s, 0, ["up", "ups", q])
+        mm("b1", C, "up", "ups", 128, q, s, 0, ["up", "ups", q])
+
+    def signs_table():
+        V(ts(T.tb1[:], T.b0[:, 0:C], 0.0, BIG, A.is_le, A.mult), ["b0"], ["tb1"])
+        V(tt(T.tb[:], T.b1[:, 0:C], T.tb1[:], A.is_gt), ["b1", "tb1"], ["tb"])
+
+    def unpack_mm(codes, scales, key):
+        for b in range(4):
+            mm("b%d" % (4 + b), C, "qe", "qes", 128 * b, codes, scales, 0, ["qe", key])
+
+    def unpack_copy(dst):
+        for b in range(4):
+            op("s", act(T[dst][:, C * b:C * (b + 1)], T["b%d" % (4 + b)][:, 0:C], ACT.Copy), ["b%d" % (4 + b)], ["%s%d" % (dst, b)])
+
+    send_state(0)
+    signs_mm(0)
+
+    for b in range(3):
+        V(cp(T.lg[:, 7 * b:7 * b + (7 if b < 2 else 6)], T.kg32[:, b::3]), ["kg32"], ["lg0%d" % b])
+    LG0 = ["lg00", "lg01", "lg02"]
+    V(ts(T.pw0[:], T.pint[:].indirect(T.ro[:]), -float(HALF), None, A.add), ["pint", "ro"], ["pw0"])
+
+    def candidates(n, k):
+        src = LG0 if n == 1 else ["lg%d" % (n - 1)]
+        pw = "pw%d" % (k % 2)
+        V(tt(T.lm[:], T[pw][:].indirect(T.lg[:, 20 * (n - 1):20 * n]), T.dm[:], A.mult), [pw, "dm"] + src, ["lm"])
+        lo, hi = C * (n - 1), C * n
+        V(lambda: g.vector.tensor_tensor_scan(T.lsc[:, lo:hi], T.rm[:], T.lm[:], 0.0, A.mult, A.add), ["rm", "lm"], ["lsc%d" % n])
+        V(ts(T.lg[:, 20 * n:20 * (n + 1)], T.lsc[:, lo + 15:hi:16], float(HALF), None, A.add), ["lsc%d" % n], ["lg%d" % n])
+
+    def candidates_own(n):
+        lo, hi = C * (n - 1), C * n
+        for b in range(3):
+            S(T.lw[:, 20 * n + b:20 * (n + 1):3], T.lsc[:, lo + 112 * b + 15:min(hi, lo + 112 * (b + 1)):16], ACT.Identity, ["lsc%d" % n], "lw%d%d" % (n, b), bias=float(HALF))
+
+    candidates(1, 0)
+    candidates_own(1)
+    V(tt(T.cw[:, 8:12], T.cw[:, 0:4], T.cw[:, 4:8], A.add), ["cw0", "cw1", "cw2"], ["cw"])
+    V(ts(T.gm[:, 0:84], T.bt[:], one["hf"], None, A.is_equal), ["bt", "hf"], ["gm0"])
+    V(ts(T.gm[:, 88:172], T.bt[:], one["g4"], None, A.is_equal), ["bt", "g4"], ["gm1"])
+    V(tt(T.cw[:, 9:10], T.cw[:, 9:10], T.al[:, 3:4], A.add), ["cw", "alp3"], ["cw"])
+    for n in range(4):
+        S(T.kt[:, 32 + n:32 + 4 * TW:4], T.gm[:], ACT.Copy, ["gm0", "gm1", "gmz", "cw", "ktz"], "kt%d" % n, scale=T.cw[:, 8 + n:9 + n])
+    for i, (lo, f) in enumerate(((48, "of"), (55, "ef"), (62, "zf"))):
+        S(T.co[:, 4 * i:4 * i + 4], T.rw[:, lo:lo + 4], ACT.Copy, RWB + ["rf" if f == "of" else f], "co%d" % i, scale=one[f])
+    S(T.xc[:, 0:1], one["of"], ACT.Copy, ["rf"], "xc0", scale=14.0, bias=2.0)
+    S(T.xc[:, 1:2], one["of"], ACT.Copy, ["rf"], "xc1", scale=4088.0, bias=8.0)
+    candidates(2, 0)
+    candidates_own(2)
+    signs_table()
+    candidates(3, 0)
+
+    def gather_signs():
+        for n in range(4):
+            rd = ["tb"] + (LG0 if n == 0 else ["lg%d" % n])
+            out, src = T.gt[:, n:4 * C:4], T.tb[:].indirect(T.lg[:, 20 * n:20 * (n + 1)])
+            if n in (0, 2):
+                V(cp(out, src), rd, ["gt%d" % n])
+            else:
+                op("s", act(out, src, ACT.Copy), rd, ["gt%d" % n])
+
+    iota(T.tk[:], [[0, TW]], 4369, 0, [], "tka")
+    op("g", lambda: g.affine_select(T.tk[:], T.tk[:], [[0, TW // 2], [1, 2]], A.not_equal, 15.0, -1, 0), ["tka"], ["tkb"])
+    iota(T.tk[:, 0:84:4], [[0, 21]], 1, 0, ["tkb"], "tk")
+    iota(T.mk[:], [[1, 7], [0, 12]], 0, 0, [], "mka")
+    iota(T.mk[:, 80:84], [[0, 4]], -1, 0, ["mka"], "mkb")
+    iota(T.rt[:], [[0, 2048]], 0, 0, [], "rtz")
+    quant("qk", "kt", ["ktz"] + ["kt%d" % n for n in range(4)], 180)
+    LWK = ["lw00"] + ["lw%d%d" % (n, b) for n in range(1, 4) for b in range(3)]
+
+    def constants_a():
+        quant("qe", "et", ETK, 512)
+        V(ts(T.mk[:], T.mk[:], one["gf"], None, A.is_equal), ["mkb", "rf"], ["mk"])
+        unpack_mm("qx0", "sx0", "qx0")
+
+    def constants_b():
+        keys = ["rtz"]
+        for own in range(2):
+            for gg in range(8):
+                to = gg + 1 - own
+                if to > 7:
+                    continue
+                o = 1024 * own + 512 * (gg // 4) + 64 * to + gg % 4
+                keys.append("rt%d%d" % (own, gg))
+                S(T.rt[:, o:o + 61:4], T.dm[:, 0:16], ACT.Copy, ["dm", "rtz"], keys[-1])
+        V(tt(T.cds[:], T.co[:, 0:4], T.co[:, 4:8], A.add), ["co0", "co1"], ["cdh"])
+        V(tt(T.cds[:], T.cds[:], T.co[:, 8:12], A.add), ["cdh", "co2"], ["cds"])
+        quant("qr", "rt", keys, 512)
+
+    def part(gg):
+        return T.ti[:, 88 * (gg // 4) + gg % 4:88 * (gg // 4) + 84:4]
+
+    def chain(first):
+        for b in range(3):
+            q = "qg" if b < 2 else "qh"
+            mm("b3", TW, q, q + "s", BLK * (b % 2), "qk", "qks", 8 - 4 * b, [q, "qk"], b == 0, b == 2)
+        if first:
+            constants_a()
+        V(tt(T.ti[:], T.b3[:, 0:TW], T.tk[:], A.add), ["b3", "tk"], ["ti"] + ["ti%d" % q for q in range(8)])
+        for gg in range(1, 8):
+            pd = T.pd[:, 21 * (gg - 1):21 * gg]
+            V(tt(pd, part(gg), part(gg - 1), A.mult), ["ti%d" % gg, "ti%d" % (gg - 1)], ["pd%d" % gg])
+            sh, mask = (3, 0x1111) if gg % 2 else (12, 15)
+            V(ts(part(gg), pd, sh, mask, A.arith_shift_right, A.bitwise_and), ["pd%d" % gg], ["ti%d" % gg])
+            if gg % 4 == 3:
+                o = 88 * (gg // 4)
+                V(tt(T.st[:, o:o + 84], T.ti[:, o:o + 84], T.mk[:], A.mult), ["mk", "stz"] + ["ti%d" % q for q in range(gg - 3, gg + 1)], ["st%d" % gg])
+        if first:
+            constants_b()
+        quant("qs", "st", ["stz", "st3", "st7"], 150)
+        if first:
+            V(cp(T.lw[:, 0:20], T.kg32[:]), ["kg32"], ["lw00"])
+            V(ts(T.jw[:], T.i20[:], 16.0, one["rf"], A.mult, A.add), ["i20", "rf"], ["jw"])
+            V(cp(T.ml[:], T.mg32[:]), ["mg32"], ["ml"])
+            V(tt(T.mj[:], T.mg32[:], T.jw[:], A.subtract), ["mg32", "jw"], ["mj"])
+            unpack_copy("fo")
+
+    def back(bank, own):
+        for h in range(2):
+            mm(bank, 128, "qr", "qrs", 256 * own + 128 * h, "qs", "qss", 22 * h, ["qr", "qs"], h == 0, h == 1)
+
+    def select(k):
+        for n in range(4):
+            V(ts(T.ind[:, 20 * n:20 * n + 20], T.b0[:, 0:20], T.cds[:, n:n + 1], None, A.is_equal), ["b0", "cds"], ["ind%d" % n])
+        V(tt(T.im[:], T.ind[:], T.lw[:], A.mult), ["ind%d" % n for n in range(4)] + LWK, ["im"])
+        V(tt(T.ia[:], T.im[:, 0:40], T.im[:, 40:80], A.add), ["im"], ["ia"])
+        V(tt(T.af[:], T.ia[:, 0:20], T.ia[:, 20:40], A.add), ["ia"], ["af"])
+        V(cp(T["al%d" % k][:], T.af[:]), ["af"], ["al%d" % k])
+
+    def exchange(k):
+        a = "al%d" % k
+        op("s", act(T.vb[:], T.sg[:].indirect(T[a][:]), ACT.Relu), ["sg", a], ["vb"])
+        V(ts(T.xb[:, 0:20], T.b1[:, 0:20], T.xc[:, 0:1], None, A.is_equal), ["b1", "xc0"], ["xb0"])
+        V(ts(T.xb[:, 20:40], T.b1[:, 0:20], T.xc[:, 1:2], None, A.is_equal), ["b1", "xc1"], ["xb1"])
+        V(tt(T.xb[:, 40:60], T.xb[:, 0:20], T.xb[:, 20:40], A.add), ["xb0", "xb1"], ["xb2"])
+        V(tt(T.ym[:], T.vb[:].indirect(T.ml[:]), T.dm[:], A.mult), ["vb", "ml", "dm"], ["ym"])
+        V(lambda: g.vector.tensor_tensor_scan(T.ysc[:], T.rm[:], T.ym[:], 0.0, A.mult, A.add), ["rm", "ym"], ["ysc"])
+        V(tt(T.df[:], T.ysc[:, 15::16], T.xb[:, 40:60], A.not_equal), ["ysc", "xb2"], ["df"])
+        V(tt(T.sf[:, 0:20], T.df[:], T.mj[:], A.mult), ["df", "mj"], ["sf0"])
+        V(tt(T.sf[:, 20:40], T.sf[:, 0:20], T.jw[:], A.add), ["sf0", "jw"], ["sf1"])
+        V(cp(T.sl[:], T.sf[:, 20:40]), ["sf1"], ["sl"])
+        old, new = "pw%d" % (k % 2), "pw%d" % (1 - k % 2)
+        op("s", act(T[new][:], T[old][:].indirect(T.sl[:]), ACT.Copy), [old, "sl"], [new])
+
+    for k in range(3):
+        qx, sx, last = "qx%d" % k, "sx%d" % k, k == 2
+        if k:
+            quant(qx, "x%d" % k, ["x%d_%d" % (k, b) for b in range(4)], C)
+            send_state(k)
+            signs_mm(k)
+            unpack_mm(qx, sx, qx)
+            candidates(3, k)
+            signs_table()
+        mm("b2", C, "up", "ups", 256, qx, sx, 0, ["up", "ups", qx])
+        gather_signs()
+        candidates_own(3)
+        op("s", act(T.sg[:], T.b2[:, 0:C], ACT.Sign), ["b2"], ["sg"])
+        if k:
+            unpack_copy("fo")
+        for q, lo, hi in (("qg", 0, 240), ("qh", 224, 352)):
+            V(lambda q=q, lo=lo, hi=hi: g.vector.quantize_mx(T[q][:], T[q + "s"][:], T.gt[:, 4 * lo:4 * hi]), ["gtz"] + ["gt%d" % n for n in range(4)], [q])
+        chain(k == 0)
+        unpack_mm("rq%d" % k, "rs%d" % k, "rq%d" % k)
+        unpack_copy("fp")
+        back("b0", 0)
+        back("b1", 1)
+        select(k)
+        send_list(k)
+        exchange(k)
+        if not last:
+            candidates(1, k + 1)
+        for t in range(4):
+            out, src = T.zt[:, t:4 * C:4], T.fp[:, C * t:C * (t + 1)].indirect(T["rl%d" % k][:])
+            rd = ["fp%d" % t, "rl%d" % k]
+            if t == 0:
+                V(cp(out, src), rd, ["zt%d" % t])
+            else:
+                op("s", act(out, src, ACT.Copy), rd, ["zt%d" % t])
+        if not last:
+            candidates_own(1)
+        quant("qz", "zt", ["zt%d" % t for t in range(4)], C)
+        for b in range(4):
+            mm("b%d" % (4 + b), C, "wq", "wqs", 128 * b, "qz", "qzs", 0, ["wq", "wqs", "qz"])
+        for b in range(4):
+            op("s", act(T.hs[:, C * b:C * (b + 1)], T["b%d" % (4 + b)][:, 0:C], ACT.Copy, scale=0.03125), ["b%d" % (4 + b)], ["hs%d" % b])
+        if not last:
+            candidates(2, k + 1)
+            candidates_own(2)
+        for b in range(4):
+            V(tt(T["x%d" % (k + 1)][:, b::4], T.hs[:, C * b:C * (b + 1)].indirect(T["al%d" % k][:]), T.fo[:, C * b:C * (b + 1)], A.add),
+              ["hs%d" % b, "al%d" % k, "fo%d" % b], ["x%d_%d" % (k + 1, b)])
+
+    quant("qv", "vt", ["vt"], 128)
+    op("s", act(T.plo[:, 0:C], T.flat[:].indirect(T.al2[:]), ACT.Copy), ["flat", "al2"], ["plo0"])
+    op("s", act(T.plo[:, C:2 * C], T.pw1[:], ACT.Copy, bias=float(HALF)), ["pw1"], ["plo1"])
+    quant("qx3", "x3", ["x3_%d" % b for b in range(4)], C)
+    for h in range(2):
+        mm("b%d" % h, C // 2, "qv", "qvs", 0, "qx3", "sx3", C // 2 * h, ["qv", "qx3"])
+    dma("y", "d_op", T.pl[:], T.plo[0::16, :], ["plo0", "plo1"], [])
+    dma("y", "d_oc", T.oc[:], T.qx3[:].bitcast(dt.uint8), ["qx3"], [])
+    for i in range(4):
+        dma("y", "d_os", T.osc[4 * i:4 * i + 4, :], T.sx3[32 * i:32 * i + 4, :], ["qx3"], [])
+    V(cp(T.yo[:, 0:C // 2], T.b0[:, 0:C // 2]), ["b0"], ["yo0"])
+    op("s", act(T.yo[:, C // 2:C], T.b1[:, 0:C // 2], ACT.Copy), ["b1"], ["yo1"])
+    dma("s", "d_oy", T.y[:], T.yo[:], ["yo0", "yo1"], [])
+    for s, v in cnt.items():
+        g.wait_ge(T.sem[s], v)

@@ -5,9 +5,8 @@ from concourse.mybir import dt, AluOpType, AxisListType, ActivationFunctionType
 C = 320
 STEPS = [1, 2, 4]
 HALF = 160
-BLK = 112
-BIG = 1.0e29
-TW = 172
+VIEW = [0, 128, 192]
+BIG, TINY = 2.0 ** 96, 2.0 ** -100
 
 SCRATCH = {}
 SEMAPHORES = ["vs", "ss", "ts", "gs", "lsem"]
@@ -31,28 +30,29 @@ for _k in range(2):
     _sb("pw%d" % _k, C, "bfloat16")
 for _n, _c, _d in [
     ("ut", 512, "bfloat16"), ("vt", 512, "bfloat16"), ("zt", 4 * C, "bfloat16"),
-    ("gt", 4 * 352, "bfloat16"), ("st", 600, "bfloat16"), ("kt", 720, "bfloat16"), ("et", 2048, "bfloat16"), ("rt", 2048, "bfloat16"),
-    ("pint", C, "int32"), ("kg32", 20, "int32"), ("mg32", 20, "int32"),
-    ("ip", 1, "int32"), ("si", 4, "int32"), ("sc", 16, "float32"),
-    ("i16c", C, "bfloat16"), ("flat", C, "float32"), ("i20", 20, "int32"), ("iu", 24, "int32"), ("bt", 84, "float32"),
-    ("jw", 20, "float32"), ("mj", 20, "float32"), ("ro", 20, "uint16"), ("ml", 20, "uint16"), ("ul", 24, "uint16"),
-    ("dm", C, "bfloat16"), ("rm", C, "bfloat16"), ("mk", 84, "float32"), ("ident", 128, "bfloat16"),
-    ("oh", 48, "float32"), ("rw", 68, "float32"), ("pr", 48, "float32"), ("jk", 48, "float32"), ("al", 8, "float32"),
-    ("cw", 12, "float32"), ("co", 12, "float32"), ("cds", 4, "float32"), ("xc", 2, "float32"), ("gm", TW, "float32"),
-    ("tk", TW, "float32"), ("ti", TW, "int32"), ("pd", 147, "int32"),
-    ("tb1", C, "float32"), ("tb", C, "bfloat16"), ("sg", C, "bfloat16"), ("vb", C, "bfloat16"), ("ym", C, "bfloat16"), ("ysc", C, "bfloat16"),
-    ("lm", C, "bfloat16"), ("lsc", 3 * C, "bfloat16"), ("lg", 80, "uint16"), ("lw", 80, "float32"),
-    ("ind", 80, "float32"), ("im", 80, "float32"), ("ia", 40, "float32"), ("af", 20, "float32"),
-    ("xb", 60, "float32"), ("df", 20, "float32"), ("sf", 40, "float32"), ("sl", 20, "uint16"),
-    ("fo", 4 * C, "bfloat16"), ("fp", 4 * C, "bfloat16"), ("hs", 4 * C, "float32"), ("yo", C, "float32"), ("plo", 2 * C, "float32"),
+    ("gt", 4 * C, "bfloat16"), ("st", 656, "bfloat16"), ("kt", 544, "bfloat16"), ("et", 2048, "bfloat16"), ("rt", 1024, "bfloat16"),
+    ("pint", C, "int32"), ("l32", 60, "int32"), ("pl16", 20, "uint16"), ("p2", C, "bfloat16"),
+    ("ip", 1, "int32"), ("si", 4, "int32"), ("sc", 24, "float32"),
+    ("i16c", C, "bfloat16"), ("flat", C, "float32"), ("i20", 20, "int32"), ("iu", 16, "int32"),
+    ("jw", 40, "float32"), ("mj", 20, "float32"), ("ro", 20, "uint16"), ("ml", 20, "uint16"), ("ul", 16, "uint16"),
+    ("dm", C, "bfloat16"), ("rm", C, "bfloat16"), ("kw", C, "bfloat16"), ("kd", C, "bfloat16"), ("ident", 128, "bfloat16"),
+    ("ra", 16, "float32"), ("pr", 32, "float32"), ("eq", 32, "float32"), ("pa", 16, "float32"), ("pb", 16, "float32"), ("on", 12, "float32"),
+    ("rowt", 32, "float32"), ("rsc", 32, "float32"), ("scl", 2, "uint16"),
+    ("tk", 96, "float32"), ("ti", 96, "float32"), ("hk", 36, "float32"), ("pk", 36, "float32"),
+    ("pd", 80, "int32"), ("bi", 36, "int32"), ("sv", 32, "int32"),
+    ("tb1", C, "bfloat16"), ("tb", C, "bfloat16"), ("vb", C, "bfloat16"), ("ym", C, "bfloat16"), ("ysc", 2 * C, "bfloat16"),
+    ("lm", C, "bfloat16"), ("lf", 2 * C, "bfloat16"), ("lsb", C, "bfloat16"), ("lsc", C, "float32"), ("lg", 80, "uint16"), ("lw", 80, "float32"),
+    ("mt", 80, "float32"), ("dd", 80, "float32"), ("af", 80, "float32"),
+    ("sf", 60, "float32"), ("sl", 20, "uint16"),
+    ("fo", 4 * C, "bfloat16"), ("fp", 4 * C, "bfloat16"), ("hs", 4 * C, "float32"), ("ks", C, "float32"), ("yo", C, "float32"), ("plo", 2 * C, "float32"),
 ]:
     _sb(_n, _c, _d)
-for _n, _c in [("qu", 128), ("up", 384), ("qv", 128), ("wq", 512), ("qe", 512), ("qr", 512), ("qk", 180), ("qg", 240), ("qh", 128), ("qs", 150), ("qz", C)]:
+for _n, _c in [("qu", 128), ("up", 256), ("qv", 128), ("wq", 512), ("qe", 512), ("qr", 256), ("qk", 136), ("qg", C), ("qs", 148), ("qz", C)]:
     _sb(_n, _c, "float8_e4m3fn_x4")
     _sb(_n + "s", _c, "uint8")
 for _k in range(8):
     SCRATCH["b%d" % _k] = ("psum", [128, 512], "float32")
-LOADS = ["dx", "du", "dp", "dk", "dm", "dw", "dws", "dv", "oy", "oc", "os", "op"]
+LOADS = ["dx", "du", "dp", "dk", "dm", "dg", "dw", "dws", "dv", "oy", "oc", "os", "op"]
 LOADS = ["d_" + _n for _n in LOADS]
 SEMAPHORES += LOADS
 
@@ -120,99 +120,84 @@ def rank_program(g, core, T, topo):
     def ms(ap, c):
         return lambda: g.vector.memset(ap, c)
 
-    def act(out, i, f, **kw):
-        return lambda: g.scalar.activation(out, i, f, **kw)
+    def scan(out, a, b, o0, o1):
+        return lambda: g.vector.tensor_tensor_scan(out, a, b, 0.0, o0, o1)
 
-    def quant(q, src, tiles, n):
-        V(lambda: g.vector.quantize_mx(T[q][:, 0:n], T[(q + "s") if q[:2] != "qx" else "sx" + q[2:]][:, 0:n], T[src][:, 0:4 * n]), tiles, [q])
+    def S(out, i, f, reads, writes, **kw):
+        op("s", lambda: g.scalar.activation(out, i, f, **kw), reads, [writes] if isinstance(writes, str) else writes)
+
+    def quant(q, src, tiles, lo, hi, key=None):
+        sc = (q + "s") if q[:2] != "qx" else "sx" + q[2:]
+        V(lambda: g.vector.quantize_mx(T[q][:, lo:hi], T[sc][:, lo:hi], T[src][:, 4 * lo:4 * hi]), tiles, [key or q])
 
     def mm(bank, n, w, ws, wa, x, xs, xa, reads, start=True, stop=True):
         op("t", lambda: g.tensor.matmul_mx(T[bank][:, 0:n], T[w][:, wa:wa + 128], T[ws][:, wa:wa + 128], T[x][:, xa:xa + n], T[xs][:, xa:xa + n], start, stop),
            reads, [bank], [] if start else [bank])
 
-    dma("y", "d_dx", T.x0[:], T.x[:], [], ["x0"])
-    dma("s", "d_du", T.ut[:], T.u[:], [], ["ut"])
+    def iota(out, pattern, base, reads, key, cm=0):
+        op("g", lambda: g.iota(out, pattern, base, cm, allow_small_or_imprecise_dtypes=True), reads, [key])
+
     for r in range(16):
         dma("y" if r % 2 else "s", "d_dp", T.pint[r::16, :], T.pg[:], [], ["pint"], ["pint"])
-    dma("s", "d_dk", T.kg32[:], T.kg[:], [], ["kg32"])
-    dma("y", "d_dm", T.mg32[:], T.mg[:], [], ["mg32"])
+    dma("s", "d_dg", T.l32[:, 20:40], T.pg[:], [], ["pg32"])
+    dma("y", "d_dk", T.l32[:, 0:20], T.kg[:], [], ["kg32"])
+    dma("s", "d_du", T.ut[:], T.u[:], [], ["ut"])
+    dma("y", "d_dx", T.x0[:], T.x[:], [], ["x0"])
+    dma("y", "d_dm", T.l32[:, 40:60], T.mg[:], [], ["mg32"])
     dma("y", "d_dw", T.wq[:].bitcast(dt.uint8), T.wc[:], [], ["wq"])
     dma("y", "d_dws", T.wqs[:], T.ws[:], [], ["wqs"])
     dma("y", "d_dv", T.vt[:], T.v[:], [], ["vt"])
+    kg32, pg32, mg32 = T.l32[:, 0:20], T.l32[:, 20:40], T.l32[:, 40:60]
 
-    def iota(out, pattern, base, cm, reads, key):
-        op("g", lambda: g.iota(out, pattern, base, cm, allow_small_or_imprecise_dtypes=True), reads, [key])
+    iota(T.ip[:], [[0, 1]], 0, [], "ip", 1)
+    iota(T.i20[:], [[1, 20]], 0, [], "i20")
+    iota(T.flat[:, 0:128], [[1, 128]], 0, [], "flat")
+    iota(T.i16c[:], [[0, 20], [1, 16]], 0, [], "i16c")
+    iota(T.iu[:], [[0, 2], [16, 8]], 0, [], "iu")
+    def pieces(key, parts):
+        for out, pattern, base in parts:
+            op("g", lambda: g.iota(out, pattern, base, 0, allow_small_or_imprecise_dtypes=True), [], [key], [key])
 
-    iota(T.ip[:], [[0, 1]], 0, 1, [], "ip")
-    iota(T.iu[:], [[0, 3], [16, 8]], 0, 0, [], "iu")
-    iota(T.flat[:], [[1, C]], 0, 0, [], "flat")
-    iota(T.i16c[:], [[0, 20], [1, 16]], 0, 0, [], "i16c")
-    iota(T.i20[:], [[1, 20]], 0, 0, [], "i20")
-    iota(T.jk[:], [[0, 3], [1, 16]], 0, 0, [], "jk")
-    iota(T.rw[:, 0:48], [[0, 48]], 0, 0, [], "rwz")
-    iota(T.rw[:, 48:62], [[0, 14]], 1, 0, [], "rwo")
-    iota(T.rw[:, 62:66], [[1, 4]], -1, 0, [], "rwp")
-    RWA, RWB = ["rwz"], ["rwo", "rwp"]
-    for col, val in ((0, 1), (4, 3), (10, 3), (17, 1), (21, 3), (27, 3), (32, 15), (36, 3840), (37, -15), (42, 240), (43, 15)):
-        iota(T.rw[:, col:col + 1], [[0, 1]], val, 0, ["rwz"], "rw%d" % col)
-        RWA.append("rw%d" % col)
-    for col, val in ((49, 2), (50, 4), (51, 8), (52, 4), (53, 2), (56, 16), (57, 256), (58, 4096), (59, 256), (60, 16)):
-        iota(T.rw[:, col:col + 1], [[0, 1]], val, 0, ["rwo"], "rw%d" % col)
-        RWB.append("rw%d" % col)
-    iota(T.bt[:], [[0, 7], [1, 12]], 0, 0, [], "bt")
-    iota(T.gm[:, 84:88], [[0, 4]], 0, 0, [], "gmz")
+    pieces("ra", [(T.ra[:, 0:2], [[-15, 2]], 15), (T.ra[:, 2:4], [[-3855, 2]], 3840), (T.ra[:, 4:6], [[-225, 2]], 240), (T.ra[:, 6:16], [[0, 10]], 0)])
+    pieces("on", [(T.on[:, 0:4], [[0, 4]], 1)])
+    pieces("pa", [(T.pa[:, 0::2], [[0, 4], [-6, 2]], 8), (T.pa[:, 1::2], [[0, 4], [-3, 2]], 4)])
+    PA = ["pa"]
+    pieces("tk", [(T.tk[:, 0:36:2], [[0, 9], [4368, 2]], 1), (T.tk[:, 1:36:2], [[0, 18]], 15), (T.tk[:, 36:60], [[0, 24]], 1),
+                  (T.tk[:, 60:84], [[-4354, 2], [0, 12]], 4369), (T.tk[:, 84:96], [[0, 12]], 4369)])
+    pieces("hk", [(T.hk[:, 0::2], [[0, 9], [16, 2]], 0), (T.hk[:, 1::2], [[0, 18]], 16)])
+    pieces("rowt", [(T.rowt[:, 0:24:3], [[80, 2], [1, 4]], 0), (T.rowt[:, 1:24:3], [[80, 2], [1, 4]], 32),
+                    (T.rowt[:, 2:24:3], [[80, 2], [1, 4]], 48), (T.rowt[:, 24:32], [[1, 8]], 608)])
 
     V(ms(T.et[:], 0.0), [], ["etz"])
-    one = {n: T.sc[:, i:i + 1] for i, n in enumerate(("rf", "gf", "of", "pf", "b10", "b4", "r20", "zf", "e1", "ef", "h1", "h2", "hf", "g4"))}
+    names = ("rf", "gf", "of", "pf", "ge2", "r20", "lt4", "thr", "fix", "fx2", "ev", "lt6", "b3", "b", "lo", "a", "hi", "t0", "t1", "t2", "t3", "g4")
+    one = {n: T.sc[:, i:i + 1] for i, n in enumerate(names)}
     V(ts(T.si[:, 0:1], T.ip[:], 15, None, A.bitwise_and), ["ip"], ["si0"])
     V(ts(T.si[:, 1:2], T.ip[:], 4, None, A.arith_shift_right), ["ip"], ["si1"])
+    V(ts(T.si[:, 2:3], T.ip[:], 1, None, A.bitwise_and), ["ip"], ["si2"])
     V(cp(one["pf"], T.ip[:]), ["ip"], ["pf"])
-    V(ts(T.si[:, 2:3], T.si[:, 1:2], 1, None, A.bitwise_and), ["si1"], ["si2"])
     V(cp(T.sc[:, 0:3], T.si[:, 0:3]), ["si0", "si1", "si2"], ["rf"])
-    V(ts(one["b10"], one["rf"], 10.0, None, A.is_ge), ["rf"], ["b10"])
-    V(ts(one["b4"], one["rf"], 4.0, None, A.is_ge), ["rf"], ["b4"])
-    V(ts(one["r20"], one["rf"], 20.0, None, A.mult), ["rf"], ["r20"])
-    V(cp(T.ul[:, 16:24], T.iu[:, 16:24]), ["iu"], ["ul2"])
-    V(ts(T.ul[:, 0:8], T.iu[:, 0:8], one["b10"], None, A.add), ["iu", "b10"], ["ul0"])
-    V(ts(T.ul[:, 8:16], T.iu[:, 8:16], one["b4"], None, A.add), ["iu", "b4"], ["ul1"])
     V(ts(T.ident[:], T.flat[:, 0:128], one["pf"], None, A.is_equal), ["flat", "pf"], ["ident"])
+    V(ts(one["r20"], one["rf"], 20.0, None, A.mult), ["rf"], ["r20"])
+    V(ts(one["ge2"], one["rf"], 2.0, None, A.is_ge), ["rf"], ["ge2"])
+    V(ts(one["lt4"], one["rf"], 4.0, BIG, A.is_lt, A.mult), ["rf"], ["lt4"])
+    V(ts(T.ro[:], T.i20[:], one["r20"], None, A.add), ["i20", "r20"], ["ro"])
     V(ts(T.dm[:], T.i16c[:], one["rf"], None, A.is_equal), ["i16c", "rf"], ["dm"])
     V(ts(T.rm[:], T.i16c[:], 1.0, None, A.min), ["i16c"], ["rm"])
-    V(ts(T.ro[:], T.i20[:], one["r20"], None, A.add), ["i20", "r20"], ["ro"])
+    V(ts(one["thr"], one["lt4"], TINY, None, A.max), ["lt4"], ["thr"])
+    V(cp(T.ul[:, 0:8], T.iu[:, 0:8]), ["iu"], ["ul0"])
+    V(ts(T.ul[:, 8:16], T.iu[:, 8:16], one["ge2"], None, A.add), ["iu", "ge2"], ["ul1"])
+    V(ts(one["lt6"], one["rf"], 6.0, None, A.is_lt), ["rf"], ["lt6"])
+    V(ts(T.eq[:, 0:8], T.flat[:, 0:8], one["gf"], None, A.is_equal), ["flat", "rf"], ["eq"])
+    V(ts(T.kw[:], T.dm[:], 8704.0, -512.0, A.mult, A.add), ["dm"], ["kw"])
 
-    def S(out, i, f, reads, key, **kw):
-        op("s", act(out, i, f, **kw), reads, [key])
-
-    S(T.kt[:], T.et[:, 0:720], ACT.Copy, ["etz"], "ktz")
-    S(one["zf"], one["gf"], ACT.Relu, ["rf"], "zf", scale=-1.0, bias=1.0)
-    S(one["h1"], one["gf"], ACT.Relu, ["rf"], "h1", bias=-3.0)
-    S(one["g4"], one["gf"], ACT.Identity, ["rf"], "g4", bias=-4.0)
-    S(one["e1"], one["zf"], ACT.Identity, ["zf"], "e1", scale=-1.0, bias=1.0)
-    S(one["h2"], one["h1"], ACT.Sign, ["h1"], "h2")
-    S(one["ef"], one["of"], ACT.Identity, ["rf", "e1"], "ef", scale=-1.0, bias=one["e1"])
-    S(one["hf"], one["h2"], ACT.Identity, ["rf", "h2"], "hf", scale=8.0, bias=one["gf"])
-
-    S(T.gt[:, 4 * C:], T.et[:, 0:128], ACT.Copy, ["etz"], "gtz")
-    S(T.st[:], T.et[:, 0:600], ACT.Copy, ["etz"], "stz")
-
-    quant("qx0", "x0", ["x0"], C)
-    quant("qu", "ut", ["ut"], 128)
-    ULK = ["ul0", "ul1", "ul2"]
-    V(cp(T.up[:].bitcast(dt.uint32), T.qu[:].bitcast(dt.uint32).indirect(T.ul[:])), ["qu"] + ULK, ["up"])
-    op("s", act(T.ups[:], T.qus[:].indirect(T.ul[:]), ACT.Copy), ["qu"] + ULK, ["ups"])
-    V(ts(T.oh[:], T.jk[:], one["rf"], None, A.is_equal), ["jk", "rf"], ["oh"])
-    V(tt(T.pr[:], T.oh[:], T.rw[:, 0:48], A.mult), ["oh"] + RWA, ["pr"])
-    for i in range(3):
-        S(T.jk[:, 16 * i:16 * i + 16], T.pr[:, 16 * i:16 * i + 16], ACT.Copy, ["pr", "oh"], "alp%d" % i, accum_out=T.al[:, i:i + 1])
-    for i, (src, f) in enumerate(((0, "zf"), (0, "ef"), (1, "ef"), (2, "of"))):
-        S(T.al[:, 3 + i:4 + i], T.al[:, src:src + 1], ACT.Copy, ["alp%d" % src, "rf" if f == "of" else f], "alp%d" % (3 + i), scale=one[f])
-    S(T.cw[:, 0:2], T.rw[:, 58:60], ACT.Copy, RWB + ["alp4"], "cw0", scale=T.al[:, 4:5])
-    S(T.cw[:, 2:4], T.rw[:, 60:62], ACT.Copy, RWB + ["alp5"], "cw1", scale=T.al[:, 5:6])
-    S(T.cw[:, 4:8], T.rw[:, 51:55], ACT.Copy, RWB + ["alp6"], "cw2", scale=T.al[:, 6:7])
+    S(T.kt[:], T.et[:, 0:544], ACT.Copy, ["etz"], "ktz")
     for b in range(4):
-        S(T.et[:, 512 * b + b:512 * (b + 1):4], T.ident[:], ACT.Copy, ["ident", "etz", "ktz", "stz", "gtz"], "et%d" % b)
-    ETK = ["et%d" % b for b in range(4)]
-    ETK.append("etz")
+        S(T.et[:, 512 * b + b:512 * (b + 1):4], T.ident[:], ACT.Copy, ["ident", "etz", "ktz"], "et%d" % b)
+    ETK = ["et%d" % b for b in range(4)] + ["etz"]
+    S(one["fix"], one["rf"], ACT.Copy, ["rf"], "fix", scale=-512.0, bias=7680.0 + HALF)
+    for h in range(2):
+        op("s", lambda: g.scalar.activation(T.rt[:, 512 * h:512 * (h + 1)], T.kt[:, 0:512], ACT.Copy), ["ktz"], ["rtz"], ["rtz"])
+    quant("qe", "et", ETK, 0, 512)
 
     partner = [rank ^ s for s in STEPS]
 
@@ -242,207 +227,254 @@ def rank_program(g, core, T, topo):
         mm("b1", C, "up", "ups", 128, q, s, 0, ["up", "ups", q])
 
     def signs_table():
-        V(ts(T.tb1[:], T.b0[:, 0:C], 0.0, BIG, A.is_le, A.mult), ["b0"], ["tb1"])
+        V(ts(T.tb1[:], T.b0[:, 0:C], 0.0, one["thr"], A.is_le, A.mult), ["b0", "thr"], ["tb1"])
         V(tt(T.tb[:], T.b1[:, 0:C], T.tb1[:], A.is_gt), ["b1", "tb1"], ["tb"])
 
-    def unpack_mm(codes, scales, key):
-        for b in range(4):
-            mm("b%d" % (4 + b), C, "qe", "qes", 128 * b, codes, scales, 0, ["qe", key])
+    def unpack_mm(codes, scales, key, parts, banks):
+        for b, bank in zip(parts, banks):
+            mm(bank, C, "qe", "qes", 128 * b, codes, scales, 0, ["qe", key])
 
-    def unpack_copy(dst):
-        for b in range(4):
-            op("s", act(T[dst][:, C * b:C * (b + 1)], T["b%d" % (4 + b)][:, 0:C], ACT.Copy), ["b%d" % (4 + b)], ["%s%d" % (dst, b)])
+    def unpack_copy(dst, parts):
+        for b in parts:
+            S(T[dst][:, C * b:C * (b + 1)], T["b%d" % (4 + b)][:, 0:C], ACT.Copy, ["b%d" % (4 + b)], "%s%d" % (dst, b))
 
-    send_state(0)
-    signs_mm(0)
+    def lgn(n):
+        return T.lg[:, 20 * n:20 * n + 20]
 
-    for b in range(3):
-        V(cp(T.lg[:, 7 * b:7 * b + (7 if b < 2 else 6)], T.kg32[:, b::3]), ["kg32"], ["lg0%d" % b])
-    LG0 = ["lg00", "lg01", "lg02"]
+    def cand_v(n, table, src):
+        V(tt(T.lm[:], T[table][:].indirect(lgn(src)), T.dm[:], A.mult), [table, "dm", "lg%d" % src], ["lm"])
+
+    def wrap_v(n):
+        V(scan(T.lsb[:], T.rm[:], T.lm[:], A.mult, A.add), ["rm", "lm"], ["lsb"])
+        V(ts(lgn(n), T.lsb[:, 15::16], float(HALF), None, A.add), ["lsb"], ["lg%d" % n])
+
+    def cand_s(n, table, src):
+        S(T.lf[:, C * (n % 2):C * (n % 2 + 1)], T[table][:].indirect(lgn(src)), ACT.Copy, [table, "lg%d" % src], "lf%d" % (n % 2))
+
+    def wrap_s(n):
+        V(scan(T.lsc[:], T.kw[:], T.lf[:, C * (n % 2):C * (n % 2 + 1)], A.add, A.min), ["kw", "lf%d" % (n % 2)], ["lsc"])
+        V(ts(lgn(n), T.lsc[:, 15::16], one["fix"], None, A.add), ["lsc", "fix"], ["lg%d" % n])
+
+    def gather(out, window, lst, rd, key, q, f=ACT.Copy):
+        if q == "v":
+            V(cp(out, window.indirect(lst)), rd, [key])
+        else:
+            S(out, window.indirect(lst), f, rd, key)
+
+    def signs_at(n, q):
+        gather(T.gt[:, n:4 * C:4], T.tb[:], lgn(n), ["tb", "lg%d" % n], "gt%d" % n, q)
+
     V(ts(T.pw0[:], T.pint[:].indirect(T.ro[:]), -float(HALF), None, A.add), ["pint", "ro"], ["pw0"])
-
-    def candidates(n, k):
-        src = LG0 if n == 1 else ["lg%d" % (n - 1)]
-        pw = "pw%d" % (k % 2)
-        V(tt(T.lm[:], T[pw][:].indirect(T.lg[:, 20 * (n - 1):20 * n]), T.dm[:], A.mult), [pw, "dm"] + src, ["lm"])
-        lo, hi = C * (n - 1), C * n
-        V(lambda: g.vector.tensor_tensor_scan(T.lsc[:, lo:hi], T.rm[:], T.lm[:], 0.0, A.mult, A.add), ["rm", "lm"], ["lsc%d" % n])
-        V(ts(T.lg[:, 20 * n:20 * (n + 1)], T.lsc[:, lo + 15:hi:16], float(HALF), None, A.add), ["lsc%d" % n], ["lg%d" % n])
-
-    def candidates_own(n):
-        lo, hi = C * (n - 1), C * n
-        for b in range(3):
-            S(T.lw[:, 20 * n + b:20 * (n + 1):3], T.lsc[:, lo + 112 * b + 15:min(hi, lo + 112 * (b + 1)):16], ACT.Identity, ["lsc%d" % n], "lw%d%d" % (n, b), bias=float(HALF))
-
-    candidates(1, 0)
-    candidates_own(1)
-    V(tt(T.cw[:, 8:12], T.cw[:, 0:4], T.cw[:, 4:8], A.add), ["cw0", "cw1", "cw2"], ["cw"])
-    V(ts(T.gm[:, 0:84], T.bt[:], one["hf"], None, A.is_equal), ["bt", "hf"], ["gm0"])
-    V(ts(T.gm[:, 88:172], T.bt[:], one["g4"], None, A.is_equal), ["bt", "g4"], ["gm1"])
-    V(tt(T.cw[:, 9:10], T.cw[:, 9:10], T.al[:, 3:4], A.add), ["cw", "alp3"], ["cw"])
-    for n in range(4):
-        S(T.kt[:, 32 + n:32 + 4 * TW:4], T.gm[:], ACT.Copy, ["gm0", "gm1", "gmz", "cw", "ktz"], "kt%d" % n, scale=T.cw[:, 8 + n:9 + n])
-    for i, (lo, f) in enumerate(((48, "of"), (55, "ef"), (62, "zf"))):
-        S(T.co[:, 4 * i:4 * i + 4], T.rw[:, lo:lo + 4], ACT.Copy, RWB + ["rf" if f == "of" else f], "co%d" % i, scale=one[f])
-    S(T.xc[:, 0:1], one["of"], ACT.Copy, ["rf"], "xc0", scale=14.0, bias=2.0)
-    S(T.xc[:, 1:2], one["of"], ACT.Copy, ["rf"], "xc1", scale=4088.0, bias=8.0)
-    candidates(2, 0)
-    candidates_own(2)
+    V(cp(T.pl16[:], pg32), ["pg32"], ["pl16"])
+    V(cp(lgn(0), kg32), ["kg32"], ["lg0"])
+    S(T.p2[:], T.pw0[:].indirect(T.pl16[:]), ACT.Copy, ["pw0", "pl16"], "p2")
+    quant("qu", "ut", ["ut"], 0, 128)
+    cand_v(1, "pw0", 0)
+    quant("qx0", "x0", ["x0"], 0, C)
+    send_state(0)
+    wrap_v(1)
+    ULK = ["ul0", "ul1"]
+    S(T.ups[:], T.qus[:].indirect(T.ul[:]), ACT.Copy, ["qu"] + ULK, "ups")
+    V(cp(T.up[:].bitcast(dt.uint32), T.qu[:].bitcast(dt.uint32).indirect(T.ul[:])), ["qu"] + ULK, ["up"])
+    signs_mm(0)
+    cand_s(2, "p2", 0)
+    cand_s(3, "p2", 1)
+    V(tt(T.pr[:, 0:16], T.dm[:, 0:16], T.ra[:], A.mult), ["dm", "ra"], ["pr"])
+    wrap_s(2)
     signs_table()
-    candidates(3, 0)
+    wrap_s(3)
+    iota(T.st[:], [[0, 656]], 0, [], "st")
+    iota(T.flat[:, 128:C], [[1, C - 128]], 128, [], "flat2")
 
-    def gather_signs():
+    def tables_tile():
+        S(T.pr[:, 16:32], T.pr[:, 0:16], ACT.Copy, ["pr"], "a", accum_out=one["a"])
+        S(one["b3"], one["ge2"], ACT.Copy, ["ge2"], "b3", scale=2.0, bias=1.0)
+        S(one["ev"], one["of"], ACT.Copy, ["rf"], "ev", scale=-1.0, bias=1.0)
+        S(T.on[:, 8:12], T.on[:, 0:4], ACT.Copy, ["on", "rf"], "od4", scale=one["of"])
+        S(one["b"], one["b3"], ACT.Copy, ["b3", "lt6"], "b", scale=one["lt6"])
+        S(T.on[:, 4:8], T.on[:, 0:4], ACT.Copy, ["on", "ev"], "ev4", scale=one["ev"])
+        S(T.eq[:, 8:16], T.eq[:, 0:8], ACT.Copy, ["eq", "a"], "ag", scale=one["a"])
+        S(one["lo"], one["b"], ACT.Copy, ["b", "ev"], "lo", scale=one["ev"])
+        S(T.eq[:, 16:24], T.eq[:, 0:8], ACT.Copy, ["eq", "b"], "bg", scale=one["b"])
         for n in range(4):
-            rd = ["tb"] + (LG0 if n == 0 else ["lg%d" % n])
-            out, src = T.gt[:, n:4 * C:4], T.tb[:].indirect(T.lg[:, 20 * n:20 * (n + 1)])
-            if n in (0, 2):
-                V(cp(out, src), rd, ["gt%d" % n])
-            else:
-                op("s", act(out, src, ACT.Copy), rd, ["gt%d" % n])
+            S(T.pb[:, n::4], T.on[:, 4:8] if n < 2 else T.on[:, 8:12], ACT.Copy, ["ev4", "od4"], "pb%d" % n, scale=float(16 ** (3 - n)))
+        PB = ["pb%d" % n for n in range(4)]
+        S(T.eq[:, 24:32], T.eq[:, 0:8], ACT.Copy, ["eq", "lo"], "lg", scale=one["lo"])
+        ag, bg, lg = [[T.eq[:, o + i:o + i + 1] for i in range(8)] for o in (8, 16, 24)]
+        fills = [(T.kt[:, 36:40], T.pa[:, 0:4], ag[1]), (T.kt[:, 44:48], T.pa[:, 0:4], ag[3]), (T.kt[:, 40:44], T.pb[:, 0:4], bg[2]), (T.kt[:, 33:34], T.on[:, 0:1], lg[0]),
+                 (T.kt[:, 176:196:5], T.on[:, 0:4], ag[4]), (T.kt[:, 224:244:5], T.on[:, 0:4], lg[4]),
+                 (T.kt[:, 272:288], T.pb[:], bg[5]), (T.kt[:, 320:336], T.pa[:], ag[5]), (T.kt[:, 368:384], T.pb[:], bg[6])]
+        for i, (out, src, f) in enumerate(fills):
+            S(out, src, ACT.Copy, PA + PB + ["on", "ag", "bg", "lg", "ktz", "rtz"], "kt%d" % i, scale=f)
+        for i in (1, 2):
+            S(T.kt[:, 32 + 48 * i:48 + 48 * i], T.kt[:, 32:48], ACT.Copy, ["kt0", "kt1", "kt2", "kt3", "ktz"], "kt%d" % (8 + i))
+        return ["ktz"] + ["kt%d" % i for i in range(11)]
 
-    iota(T.tk[:], [[0, TW]], 4369, 0, [], "tka")
-    op("g", lambda: g.affine_select(T.tk[:], T.tk[:], [[0, TW // 2], [1, 2]], A.not_equal, 15.0, -1, 0), ["tka"], ["tkb"])
-    iota(T.tk[:, 0:84:4], [[0, 21]], 1, 0, ["tkb"], "tk")
-    iota(T.mk[:], [[1, 7], [0, 12]], 0, 0, [], "mka")
-    iota(T.mk[:, 80:84], [[0, 4]], -1, 0, ["mka"], "mkb")
-    iota(T.rt[:], [[0, 2048]], 0, 0, [], "rtz")
-    quant("qk", "kt", ["ktz"] + ["kt%d" % n for n in range(4)], 180)
-    LWK = ["lw00"] + ["lw%d%d" % (n, b) for n in range(1, 4) for b in range(3)]
+    KTK = tables_tile()
 
-    def constants_a():
-        quant("qe", "et", ETK, 512)
-        V(ts(T.mk[:], T.mk[:], one["gf"], None, A.is_equal), ["mkb", "rf"], ["mk"])
-        unpack_mm("qx0", "sx0", "qx0")
-
-    def constants_b():
+    def way_back_constants():
         keys = ["rtz"]
-        for own in range(2):
-            for gg in range(8):
-                to = gg + 1 - own
-                if to > 7:
-                    continue
-                o = 1024 * own + 512 * (gg // 4) + 64 * to + gg % 4
-                keys.append("rt%d%d" % (own, gg))
-                S(T.rt[:, o:o + 61:4], T.dm[:, 0:16], ACT.Copy, ["dm", "rtz"], keys[-1])
-        V(tt(T.cds[:], T.co[:, 0:4], T.co[:, 4:8], A.add), ["co0", "co1"], ["cdh"])
-        V(tt(T.cds[:], T.cds[:], T.co[:, 8:12], A.add), ["cdh", "co2"], ["cds"])
-        quant("qr", "rt", keys, 512)
+        S(T.rowt[0:64, 2:24:3], T.flat[0:64, 0:8], ACT.Copy, ["flat"], "rowt", bias=600.0)
+        S(one["g4"], one["gf"], ACT.Copy, ["rf"], "g4", scale=4.0)
+        for gg in range(7):
+            o = 512 * (gg // 4) + 64 * (gg + 1) + gg % 4
+            keys.append("rt%d" % gg)
+            S(T.rt[:, o:o + 61:4], T.dm[:, 0:16], ACT.Copy, ["dm", "rtz"], keys[-1])
+        S(one["hi"], T.eq[:, 2:3], ACT.Identity, ["eq"], "hi", bias=T.eq[:, 4:5])
+        S(one["t0"], T.eq[:, 0:1], ACT.Copy, ["eq"], "t0", scale=-2.0, bias=2.0)
+        S(one["t1"], one["hi"], ACT.Copy, ["hi"], "t1", scale=4088.0, bias=8.0)
+        S(one["t2"], one["hi"], ACT.Copy, ["hi"], "t2", scale=252.0, bias=4.0)
+        S(one["t3"], one["hi"], ACT.Identity, ["hi", "t0"], "t3", scale=14.0, bias=one["t0"])
+        return keys
 
-    def part(gg):
-        return T.ti[:, 88 * (gg // 4) + gg % 4:88 * (gg // 4) + 84:4]
+    def differences(first):
+        lo = 0 if first else 20
+        V(cp(T.lw[:, lo:80], T.lg[:, lo:80]), ["lg%d" % n for n in range(4)], ["lw"])
+        if first:
+            V(cp(T.dd[:, 3::4], T.lg[:, 0:20]), ["lg0"], ["dd3"])
+        for i in range(3):
+            V(tt(T.dd[:, i::4], T.lw[:, 20 * (3 - i):20 * (4 - i)], T.lw[:, 20 * (2 - i):20 * (3 - i)], A.subtract), ["lw"], ["dd%d" % i])
 
-    def chain(first):
-        for b in range(3):
-            q = "qg" if b < 2 else "qh"
-            mm("b3", TW, q, q + "s", BLK * (b % 2), "qk", "qks", 8 - 4 * b, [q, "qk"], b == 0, b == 2)
-        if first:
-            constants_a()
-        V(tt(T.ti[:], T.b3[:, 0:TW], T.tk[:], A.add), ["b3", "tk"], ["ti"] + ["ti%d" % q for q in range(8)])
-        for gg in range(1, 8):
-            pd = T.pd[:, 21 * (gg - 1):21 * gg]
-            V(tt(pd, part(gg), part(gg - 1), A.mult), ["ti%d" % gg, "ti%d" % (gg - 1)], ["pd%d" % gg])
-            sh, mask = (3, 0x1111) if gg % 2 else (12, 15)
-            V(ts(part(gg), pd, sh, mask, A.arith_shift_right, A.bitwise_and), ["pd%d" % gg], ["ti%d" % gg])
-            if gg % 4 == 3:
-                o = 88 * (gg // 4)
-                V(tt(T.st[:, o:o + 84], T.ti[:, o:o + 84], T.mk[:], A.mult), ["mk", "stz"] + ["ti%d" % q for q in range(gg - 3, gg + 1)], ["st%d" % gg])
-        if first:
-            constants_b()
-        quant("qs", "st", ["stz", "st3", "st7"], 150)
-        if first:
-            V(cp(T.lw[:, 0:20], T.kg32[:]), ["kg32"], ["lw00"])
-            V(ts(T.jw[:], T.i20[:], 16.0, one["rf"], A.mult, A.add), ["i20", "rf"], ["jw"])
-            V(cp(T.ml[:], T.mg32[:]), ["mg32"], ["ml"])
-            V(tt(T.mj[:], T.mg32[:], T.jw[:], A.subtract), ["mg32", "jw"], ["mj"])
-            unpack_copy("fo")
+    def chain(k, freed, fill):
+        V(tt(T.ti[:], T.b2[:, 0:96], T.tk[:], A.add), ["b2", "tk"], ["tia", "tib", "t5", "t6"])
+        freed()
+        UP, DOWN = (3, 0x1111), (12, 15)
 
-    def back(bank, own):
+        def times(out, table, state, rd, key):
+            V(tt(out, table, state, A.mult), rd, [key])
+
+        def pick(out, src, kind, rd, wr):
+            V(ts(out, src, kind[0], kind[1], A.arith_shift_right, A.bitwise_and), rd, wr)
+
+        times(T.pd[:, 0:9], T.ti[:, 1:36:4], T.ti[:, 0:36:4], ["tia"], "pd1")
+        times(T.pd[:, 40:64], T.ti[:, 60:84], T.ti[:, 36:60], ["tib", "t5"], "pe1")
+        pick(T.sv[:, 3:12], T.pd[:, 0:9], UP, ["pd1"], ["s1", "s2", "s3"])
+        pick(T.bi[:, 24:36], T.pd[:, 52:64], UP, ["pe1"], ["bh"])
+        times(T.pd[:, 9:18], T.ti[:, 2:36:4], T.sv[:, 3:12], ["tia", "s1", "s2", "s3"], "pd2")
+        times(T.pd[:, 64:76], T.ti[:, 84:96], T.bi[:, 24:36], ["t6", "bh"], "pe2")
+        pick(T.sv[:, 6:15], T.pd[:, 9:18], DOWN, ["pd2"], ["s2", "s3", "s4"])
+        pick(T.bi[:, 0:12], T.pd[:, 40:52], DOWN, ["pe1"], ["b5l"])
+        pick(T.bi[:, 12:24], T.pd[:, 64:76], DOWN, ["pe2"], ["b6l"])
+        times(T.pd[:, 18:27], T.ti[:, 3:36:4], T.sv[:, 6:15], ["tia", "s2", "s3", "s4"], "pd3")
+        V(cp(T.ti[:, 60:84], T.bi[:, 0:24]), ["b5l", "b6l"], ["t5"])
+        pick(T.sv[:, 9:18], T.pd[:, 18:27], UP, ["pd3"], ["s3", "s4", "s5"])
+        V(scan(T.pk[:], T.hk[:], T.ti[:, 48:84], A.mult, A.add), ["hk", "tib", "t5"], ["pk"])
+        V(cp(T.sv[:, 0:3], T.ti[:, 0:12:4]), ["tia"], ["s0"])
+        times(T.pd[:, 27:36], T.pk[:, 3::4], T.sv[:, 9:18], ["pk", "s3", "s4", "s5"], "pd4")
+        fill()
+        pick(T.sv[:, 12:21], T.pd[:, 27:36], DOWN, ["pd4"], ["s4", "s5", "s6"])
+        V(cp(T.st[:].indirect(T.scl[:]), T.sv[:]), ["s%d" % i for i in range(8)] + ["scl"], ["st"])
+        quant("qs", "st", ["st"], 0, 148)
         for h in range(2):
-            mm(bank, 128, "qr", "qrs", 256 * own + 128 * h, "qs", "qss", 22 * h, ["qr", "qs"], h == 0, h == 1)
+            mm("b3", 128, "qr", "qrs", 128 * h, "qs", "qss", 20 * h, ["qr", "qs"], h == 0, h == 1)
 
     def select(k):
-        for n in range(4):
-            V(ts(T.ind[:, 20 * n:20 * n + 20], T.b0[:, 0:20], T.cds[:, n:n + 1], None, A.is_equal), ["b0", "cds"], ["ind%d" % n])
-        V(tt(T.im[:], T.ind[:], T.lw[:], A.mult), ["ind%d" % n for n in range(4)] + LWK, ["im"])
-        V(tt(T.ia[:], T.im[:, 0:40], T.im[:, 40:80], A.add), ["im"], ["ia"])
-        V(tt(T.af[:], T.ia[:, 0:20], T.ia[:, 20:40], A.add), ["ia"], ["af"])
-        V(cp(T["al%d" % k][:], T.af[:]), ["af"], ["al%d" % k])
+        for i in (1, 2, 3):
+            V(ts(T.mt[:, i::4], T.b3[:, 0:20], one["t%d" % i], None, A.is_ge), ["b3", "t%d" % i], ["mt%d" % i])
+        V(scan(T.af[:], T.mt[:], T.dd[:], A.mult, A.add), ["mt%d" % i for i in range(4)] + ["dd%d" % i for i in range(4)], ["af"])
+        V(cp(T["al%d" % k][:], T.af[:, 3::4]), ["af"], ["al%d" % k])
 
-    def exchange(k):
+    def sigma(k):
         a = "al%d" % k
-        op("s", act(T.vb[:], T.sg[:].indirect(T[a][:]), ACT.Relu), ["sg", a], ["vb"])
-        V(ts(T.xb[:, 0:20], T.b1[:, 0:20], T.xc[:, 0:1], None, A.is_equal), ["b1", "xc0"], ["xb0"])
-        V(ts(T.xb[:, 20:40], T.b1[:, 0:20], T.xc[:, 1:2], None, A.is_equal), ["b1", "xc1"], ["xb1"])
-        V(tt(T.xb[:, 40:60], T.xb[:, 0:20], T.xb[:, 20:40], A.add), ["xb0", "xb1"], ["xb2"])
-        V(tt(T.ym[:], T.vb[:].indirect(T.ml[:]), T.dm[:], A.mult), ["vb", "ml", "dm"], ["ym"])
-        V(lambda: g.vector.tensor_tensor_scan(T.ysc[:], T.rm[:], T.ym[:], 0.0, A.mult, A.add), ["rm", "ym"], ["ysc"])
-        V(tt(T.df[:], T.ysc[:, 15::16], T.xb[:, 40:60], A.not_equal), ["ysc", "xb2"], ["df"])
-        V(tt(T.sf[:, 0:20], T.df[:], T.mj[:], A.mult), ["df", "mj"], ["sf0"])
-        V(tt(T.sf[:, 20:40], T.sf[:, 0:20], T.jw[:], A.add), ["sf0", "jw"], ["sf1"])
+        V(ts(T.vb[:, 0:HALF], T.tb1[:].indirect(T[a][:, 0:10]), 0.0, None, A.is_gt), ["tb1", a], ["vb0"])
+        S(T.vb[:, HALF:C], T.tb1[:].indirect(T[a][:, 10:20]), ACT.Sign, ["tb1", a], "vb1")
+        for h in range(2):
+            gather(T.ym[:, HALF * h:HALF * (h + 1)], T.vb[:], T.ml[:, 10 * h:10 * h + 10], ["vb0", "vb1", "ml"], "ym%d" % h, "vs"[h])
+        V(scan(T.ysc[:, 0:C], T.kd[:], T.vb[:], A.add, A.min), ["kd", "vb0", "vb1"], ["ysc0"])
+        V(scan(T.ysc[:, C:2 * C], T.kd[:], T.ym[:], A.add, A.min), ["kd", "ym0", "ym1"], ["ysc1"])
+        V(tt(T.sf[:, 40:60], T.ysc[:, 15:C:16], T.ysc[:, C + 15::16], A.not_equal), ["ysc0", "ysc1"], ["df"])
+        V(tt(T.sf[:, 0:20], T.sf[:, 40:60], T.mj[:], A.mult), ["df", "mj"], ["sf0"])
+        V(tt(T.sf[:, 20:40], T.sf[:, 0:20], T.jw[:, 0:20], A.add), ["sf0", "jw"], ["sf1"])
         V(cp(T.sl[:], T.sf[:, 20:40]), ["sf1"], ["sl"])
+
+    def new_p(k):
         old, new = "pw%d" % (k % 2), "pw%d" % (1 - k % 2)
-        op("s", act(T[new][:], T[old][:].indirect(T.sl[:]), ACT.Copy), [old, "sl"], [new])
+        S(T[new][:], T[old][:].indirect(T.sl[:]), ACT.Copy, [old, "sl"], new)
 
     for k in range(3):
-        qx, sx, last = "qx%d" % k, "sx%d" % k, k == 2
+        qx, sx, first, last = "qx%d" % k, "sx%d" % k, k == 0, k == 2
+        pw = "pw%d" % (k % 2)
         if k:
-            quant(qx, "x%d" % k, ["x%d_%d" % (k, b) for b in range(4)], C)
+            cand_s(2, pw, 1)
+            quant(qx, "x%d" % k, ["x%d_%d" % (k, b) for b in range(4)], 0, C)
             send_state(k)
             signs_mm(k)
-            unpack_mm(qx, sx, qx)
-            candidates(3, k)
+            wrap_s(2)
+            cand_s(3, pw, 2)
             signs_table()
-        mm("b2", C, "up", "ups", 256, qx, sx, 0, ["up", "ups", qx])
-        gather_signs()
-        candidates_own(3)
-        op("s", act(T.sg[:], T.b2[:, 0:C], ACT.Sign), ["b2"], ["sg"])
-        if k:
-            unpack_copy("fo")
-        for q, lo, hi in (("qg", 0, 240), ("qh", 224, 352)):
-            V(lambda q=q, lo=lo, hi=hi: g.vector.quantize_mx(T[q][:], T[q + "s"][:], T.gt[:, 4 * lo:4 * hi]), ["gtz"] + ["gt%d" % n for n in range(4)], [q])
-        chain(k == 0)
-        unpack_mm("rq%d" % k, "rs%d" % k, "rq%d" % k)
-        unpack_copy("fp")
-        back("b0", 0)
-        back("b1", 1)
+            signs_at(1, "s")
+            wrap_s(3)
+            signs_at(2, "s")
+            signs_at(0, "v")
+            signs_at(3, "v")
+        else:
+            signs_at(0, "v")
+            signs_at(1, "s")
+            signs_at(2, "s")
+            signs_at(3, "v")
+        unpack_mm(qx, sx, qx, [0, 1, 2], ["b4", "b5", "b6"])
+        GT = ["gt%d" % n for n in range(4)]
+        if first:
+            quant("qk", "kt", KTK, 0, 136)
+        quant("qg", "gt", GT, 0, 128, "qga")
+        quant("qg", "gt", GT, 128, C, "qgb")
+        for b in range(3):
+            mm("b2", 128, "qg", "qgs", VIEW[b], "qk", "qks", 8 - 4 * b, ["qga" if b == 0 else "qgb", "qk"], b == 0, b == 2)
+        own_last = lambda: unpack_mm(qx, sx, qx, [3], ["b2"])
+        if first:
+            RTK = way_back_constants()
+            V(tt(T.pr[:], T.dm[:, 0:32], T.rowt[:], A.mult), ["dm", "rowt", "a"], ["pr", "prs"])
+            V(scan(T.rsc[:], T.rm[:, 0:32], T.pr[:], A.mult, A.add), ["rm", "prs"], ["rsc"])
+            V(ms(T.sv[:, 21:32], 0), [], ["s7"])
+            V(ts(T.scl[:], T.rsc[:, 15::16], one["g4"], None, A.add), ["rsc", "g4"], ["scl"])
+        else:
+            differences(False)
+        unpack_copy("fo", [0, 1, 2])
+        chain(k, own_last, (lambda: quant("qr", "rt", RTK, 0, 256)) if first else (lambda: None))
+        if first:
+            V(ms(T.mt[:, 0::4], 0.0), [], ["mt0"])
+            differences(True)
+        unpack_mm("rq%d" % k, "rs%d" % k, "rq%d" % k, [0, 1, 2, 3], ["b4", "b5", "b6", "b7"])
         select(k)
         send_list(k)
-        exchange(k)
-        if not last:
-            candidates(1, k + 1)
+        if first:
+            V(ts(T.jw[:, 0:20], T.i20[:], 16.0, one["rf"], A.mult, A.add), ["i20", "rf"], ["jw"])
+            V(cp(T.ml[:], mg32), ["mg32"], ["ml"])
+            V(tt(T.mj[:], mg32, T.jw[:, 0:20], A.subtract), ["mg32", "jw"], ["mj"])
+            V(ts(T.kd[:], T.dm[:], 34.0, -2.0, A.mult, A.add), ["dm"], ["kd"])
+        unpack_copy("fp", [0])
+        sigma(k)
+        unpack_copy("fp", [1, 2, 3])
         for t in range(4):
-            out, src = T.zt[:, t:4 * C:4], T.fp[:, C * t:C * (t + 1)].indirect(T["rl%d" % k][:])
-            rd = ["fp%d" % t, "rl%d" % k]
-            if t == 0:
-                V(cp(out, src), rd, ["zt%d" % t])
-            else:
-                op("s", act(out, src, ACT.Copy), rd, ["zt%d" % t])
-        if not last:
-            candidates_own(1)
-        quant("qz", "zt", ["zt%d" % t for t in range(4)], C)
+            gather(T.zt[:, t:4 * C:4], T.fp[:, C * t:C * (t + 1)], T["rl%d" % k][:], ["fp%d" % t, "rl%d" % k], "zt%d" % t, "vs"[t % 2])
+        new_p(k)
+        quant("qz", "zt", ["zt%d" % t for t in range(4)], 0, C)
         for b in range(4):
             mm("b%d" % (4 + b), C, "wq", "wqs", 128 * b, "qz", "qzs", 0, ["wq", "wqs", "qz"])
         for b in range(4):
-            op("s", act(T.hs[:, C * b:C * (b + 1)], T["b%d" % (4 + b)][:, 0:C], ACT.Copy, scale=0.03125), ["b%d" % (4 + b)], ["hs%d" % b])
+            S(T.hs[:, C * b:C * (b + 1)], T["b%d" % (4 + b)][:, 0:C], ACT.Copy, ["b%d" % (4 + b)], "hs%d" % b, scale=0.03125)
         if not last:
-            candidates(2, k + 1)
-            candidates_own(2)
-        for b in range(4):
-            V(tt(T["x%d" % (k + 1)][:, b::4], T.hs[:, C * b:C * (b + 1)].indirect(T["al%d" % k][:]), T.fo[:, C * b:C * (b + 1)], A.add),
-              ["hs%d" % b, "al%d" % k, "fo%d" % b], ["x%d_%d" % (k + 1, b)])
+            cand_v(1, "pw%d" % (1 - k % 2), 0)
+            wrap_v(1)
+        else:
+            quant("qv", "vt", ["vt"], 0, 128)
+        a, x = "al%d" % k, "x%d" % (k + 1)
+        S(T.ks[:], T.hs[:, 3 * C:4 * C].indirect(T[a][:]), ACT.Copy, ["hs3", a], "ks")
+        for b in range(3):
+            V(tt(T[x][:, b::4], T.hs[:, C * b:C * (b + 1)].indirect(T[a][:]), T.fo[:, C * b:C * (b + 1)], A.add), ["hs%d" % b, a, "fo%d" % b], ["%s_%d" % (x, b)])
+        V(tt(T[x][:, 3::4], T.b2[:, 0:C], T.ks[:], A.add), ["b2", "ks"], [x + "_3"])
 
-    quant("qv", "vt", ["vt"], 128)
-    op("s", act(T.plo[:, 0:C], T.flat[:].indirect(T.al2[:]), ACT.Copy), ["flat", "al2"], ["plo0"])
-    op("s", act(T.plo[:, C:2 * C], T.pw1[:], ACT.Copy, bias=float(HALF)), ["pw1"], ["plo1"])
-    quant("qx3", "x3", ["x3_%d" % b for b in range(4)], C)
+    S(T.plo[:, 0:C], T.flat[:].indirect(T.al2[:]), ACT.Copy, ["flat", "flat2", "al2"], "plo0")
+    S(T.plo[:, C:2 * C], T.pw1[:], ACT.Copy, ["pw1"], "plo1", bias=float(HALF))
+    quant("qx3", "x3", ["x3_%d" % b for b in range(4)], 0, C)
     for h in range(2):
-        mm("b%d" % h, C // 2, "qv", "qvs", 0, "qx3", "sx3", C // 2 * h, ["qv", "qx3"])
-    dma("y", "d_op", T.pl[:], T.plo[0::16, :], ["plo0", "plo1"], [])
+        mm("b%d" % (2 * h), C // 2, "qv", "qvs", 0, "qx3", "sx3", C // 2 * h, ["qv", "qx3"])
     dma("y", "d_oc", T.oc[:], T.qx3[:].bitcast(dt.uint8), ["qx3"], [])
     for i in range(4):
         dma("y", "d_os", T.osc[4 * i:4 * i + 4, :], T.sx3[32 * i:32 * i + 4, :], ["qx3"], [])
+    dma("y", "d_op", T.pl[:], T.plo[0::16, :], ["plo0", "plo1"], [])
     V(cp(T.yo[:, 0:C // 2], T.b0[:, 0:C // 2]), ["b0"], ["yo0"])
-    op("s", act(T.yo[:, C // 2:C], T.b1[:, 0:C // 2], ACT.Copy), ["b1"], ["yo1"])
+    S(T.yo[:, C // 2:C], T.b2[:, 0:C // 2], ACT.Copy, ["b2"], "yo1")
     dma("s", "d_oy", T.y[:], T.yo[:], ["yo0", "yo1"], [])
     for s, v in cnt.items():
         g.wait_ge(T.sem[s], v)

@@ -5,7 +5,6 @@ from concourse.mybir import dt, AluOpType, AxisListType, ActivationFunctionType
 C = 320
 STEPS = [1, 2, 4]
 HALF = 160
-VIEW = [0, 128, 192]
 BIG, TINY = 2.0 ** 96, 2.0 ** -100
 
 SCRATCH = {}
@@ -31,23 +30,24 @@ for _k in range(2):
 for _n, _c, _d in [
     ("ut", 512, "bfloat16"), ("vt", 512, "bfloat16"), ("zt", 4 * C, "bfloat16"),
     ("gt", 4 * C, "bfloat16"), ("st", 656, "bfloat16"), ("kt", 544, "bfloat16"), ("et", 2048, "bfloat16"), ("rt", 1024, "bfloat16"),
-    ("pint", C, "int32"), ("l32", 60, "int32"), ("pl16", 20, "uint16"), ("p2", C, "bfloat16"),
+    ("pint", C, "int32"), ("l32", 60, "int32"), ("p2", C, "bfloat16"),
     ("ip", 1, "int32"), ("si", 4, "int32"), ("sc", 24, "float32"),
     ("i16c", C, "bfloat16"), ("flat", C, "float32"), ("i20", 20, "int32"), ("iu", 16, "int32"),
-    ("jw", 40, "float32"), ("mj", 20, "float32"), ("ro", 20, "uint16"), ("ml", 20, "uint16"), ("ul", 16, "uint16"),
+    ("pj", 40, "float32"), ("dj", 40, "float32"), ("ro", 20, "uint16"), ("ml", 20, "uint16"), ("ul", 16, "uint16"),
     ("dm", C, "bfloat16"), ("rm", C, "bfloat16"), ("kw", C, "bfloat16"), ("kd", C, "bfloat16"), ("ident", 128, "bfloat16"),
     ("ra", 16, "float32"), ("pr", 32, "float32"), ("eq", 32, "float32"), ("pa", 16, "float32"), ("pb", 16, "float32"), ("on", 12, "float32"),
     ("rowt", 32, "float32"), ("rsc", 32, "float32"), ("scl", 2, "uint16"),
     ("tk", 96, "float32"), ("ti", 96, "float32"), ("hk", 36, "float32"), ("pk", 36, "float32"),
     ("pd", 80, "int32"), ("bi", 36, "int32"), ("sv", 32, "int32"),
-    ("tb1", C, "bfloat16"), ("tb", C, "bfloat16"), ("vb", C, "bfloat16"), ("ym", C, "bfloat16"), ("ysc", 2 * C, "bfloat16"),
-    ("lm", C, "bfloat16"), ("lf", 2 * C, "bfloat16"), ("lsb", C, "bfloat16"), ("lsc", C, "float32"), ("lg", 80, "uint16"), ("lw", 80, "float32"),
+    ("tb1", C, "bfloat16"), ("tb", C, "bfloat16"), ("tbp", C, "bfloat16"), ("vb", C, "bfloat16"), ("ym", C, "bfloat16"), ("ysc", 2 * C, "bfloat16"),
+    ("lm", C, "bfloat16"), ("lf", 2 * C, "bfloat16"), ("lsb", C, "bfloat16"), ("lsc", C, "float32"), ("lsd", C, "float32"),
+    ("lg", 60, "uint16"), ("lw", 80, "float32"),
     ("mt", 80, "float32"), ("dd", 80, "float32"), ("af", 80, "float32"),
-    ("sf", 60, "float32"), ("sl", 20, "uint16"),
-    ("fo", 4 * C, "bfloat16"), ("fp", 4 * C, "bfloat16"), ("hs", 4 * C, "float32"), ("ks", C, "float32"), ("yo", C, "float32"), ("plo", 2 * C, "float32"),
+    ("sf", 120, "float32"), ("sl", 40, "uint16"),
+    ("fo", 3 * C, "bfloat16"), ("fp", 4 * C, "bfloat16"), ("hs", 4 * C, "float32"), ("ks", C, "float32"), ("yo", C, "float32"), ("plo", 2 * C, "float32"),
 ]:
     _sb(_n, _c, _d)
-for _n, _c in [("qu", 128), ("up", 256), ("qv", 128), ("wq", 512), ("qe", 512), ("qr", 256), ("qk", 136), ("qg", C), ("qs", 148), ("qz", C)]:
+for _n, _c in [("qu", 128), ("up", 256), ("qv", 128), ("wq", 512), ("qe", 512), ("qr", 256), ("qk", 136), ("qg", 256), ("qh", 128), ("qs", 148), ("qz", C)]:
     _sb(_n, _c, "float8_e4m3fn_x4")
     _sb(_n + "s", _c, "uint8")
 for _k in range(8):
@@ -58,6 +58,13 @@ SEMAPHORES += LOADS
 
 A = AluOpType
 ACT = ActivationFunctionType
+HALVES = ((0, HALF, "a"), (HALF, C, "b"))
+BLOCKS = (("qg", 0, 0), ("qg", 128, 128), ("qh", 192, 0))
+SCORE = (("b0", "b3"), ("b1", "b7"))
+
+
+def both(key):
+    return [key + "a", key + "b"]
 
 
 def rank_program(g, core, T, topo):
@@ -123,82 +130,119 @@ def rank_program(g, core, T, topo):
     def scan(out, a, b, o0, o1):
         return lambda: g.vector.tensor_tensor_scan(out, a, b, 0.0, o0, o1)
 
-    def S(out, i, f, reads, writes, **kw):
-        op("s", lambda: g.scalar.activation(out, i, f, **kw), reads, [writes] if isinstance(writes, str) else writes)
+    def S(out, i, f, reads, writes, free=(), **kw):
+        op("s", lambda: g.scalar.activation(out, i, f, **kw), reads, [writes], free)
 
-    def quant(q, src, tiles, lo, hi, key=None):
+    def quant(q, src, tiles, lo, hi, key=None, at=None):
         sc = (q + "s") if q[:2] != "qx" else "sx" + q[2:]
-        V(lambda: g.vector.quantize_mx(T[q][:, lo:hi], T[sc][:, lo:hi], T[src][:, 4 * lo:4 * hi]), tiles, [key or q])
+        at = lo if at is None else at
+        V(lambda: g.vector.quantize_mx(T[q][:, at:at + hi - lo], T[sc][:, at:at + hi - lo], T[src][:, 4 * lo:4 * hi]), tiles, [key or q])
 
     def mm(bank, n, w, ws, wa, x, xs, xa, reads, start=True, stop=True):
         op("t", lambda: g.tensor.matmul_mx(T[bank][:, 0:n], T[w][:, wa:wa + 128], T[ws][:, wa:wa + 128], T[x][:, xa:xa + n], T[xs][:, xa:xa + n], start, stop),
            reads, [bank], [] if start else [bank])
 
-    def iota(out, pattern, base, reads, key, cm=0):
-        op("g", lambda: g.iota(out, pattern, base, cm, allow_small_or_imprecise_dtypes=True), reads, [key])
+    def iota(key, parts, cm=0):
+        for out, pattern, base in parts:
+            op("g", lambda: g.iota(out, pattern, base, cm, allow_small_or_imprecise_dtypes=True), [], [key], [key])
 
+    kg32, pg32, mg32 = T.l32[:, 0:20], T.l32[:, 20:40], T.l32[:, 40:60]
     for r in range(16):
         dma("y" if r % 2 else "s", "d_dp", T.pint[r::16, :], T.pg[:], [], ["pint"], ["pint"])
-    dma("s", "d_dg", T.l32[:, 20:40], T.pg[:], [], ["pg32"])
-    dma("y", "d_dk", T.l32[:, 0:20], T.kg[:], [], ["kg32"])
+    dma("s", "d_dg", pg32, T.pg[:], [], ["pg32"])
+    dma("y", "d_dk", kg32, T.kg[:], [], ["kg32"])
     dma("s", "d_du", T.ut[:], T.u[:], [], ["ut"])
     dma("y", "d_dx", T.x0[:], T.x[:], [], ["x0"])
-    dma("y", "d_dm", T.l32[:, 40:60], T.mg[:], [], ["mg32"])
+    dma("y", "d_dm", mg32, T.mg[:], [], ["mg32"])
     dma("y", "d_dw", T.wq[:].bitcast(dt.uint8), T.wc[:], [], ["wq"])
     dma("y", "d_dws", T.wqs[:], T.ws[:], [], ["wqs"])
     dma("y", "d_dv", T.vt[:], T.v[:], [], ["vt"])
-    kg32, pg32, mg32 = T.l32[:, 0:20], T.l32[:, 20:40], T.l32[:, 40:60]
 
-    iota(T.ip[:], [[0, 1]], 0, [], "ip", 1)
-    iota(T.i20[:], [[1, 20]], 0, [], "i20")
-    iota(T.flat[:, 0:128], [[1, 128]], 0, [], "flat")
-    iota(T.i16c[:], [[0, 20], [1, 16]], 0, [], "i16c")
-    iota(T.iu[:], [[0, 2], [16, 8]], 0, [], "iu")
-    def pieces(key, parts):
-        for out, pattern, base in parts:
-            op("g", lambda: g.iota(out, pattern, base, 0, allow_small_or_imprecise_dtypes=True), [], [key], [key])
+    iota("ip", [(T.ip[:], [[0, 1]], 0)], 1)
+    iota("i20", [(T.i20[:], [[1, 20]], 0)])
+    iota("flat", [(T.flat[:, 0:128], [[1, 128]], 0)])
+    iota("i16c", [(T.i16c[:], [[0, 20], [1, 16]], 0)])
+    iota("iu", [(T.iu[:], [[0, 2], [16, 8]], 0)])
+    iota("ra", [(T.ra[:, 0:2], [[-15, 2]], 15), (T.ra[:, 2:4], [[-3855, 2]], 3840), (T.ra[:, 4:6], [[-225, 2]], 240), (T.ra[:, 6:16], [[0, 10]], 0)])
+    iota("on", [(T.on[:, 0:4], [[0, 4]], 1)])
+    iota("pa", [(T.pa[:, 0::2], [[0, 4], [-6, 2]], 8), (T.pa[:, 1::2], [[0, 4], [-3, 2]], 4)])
+    iota("tk", [(T.tk[:, 0:36:2], [[0, 9], [4368, 2]], 1), (T.tk[:, 1:36:2], [[0, 18]], 15), (T.tk[:, 36:60], [[0, 24]], 1),
+                (T.tk[:, 60:84], [[-4354, 2], [0, 12]], 4369), (T.tk[:, 84:96], [[0, 12]], 4369)])
+    iota("hk", [(T.hk[:, 0::2], [[0, 9], [16, 2]], 0), (T.hk[:, 1::2], [[0, 18]], 16)])
+    iota("rowt", [(T.rowt[:, 0:24:3], [[80, 2], [1, 4]], 0), (T.rowt[:, 1:24:3], [[80, 2], [1, 4]], 32),
+                  (T.rowt[:, 2:24:3], [[80, 2], [1, 4]], 48), (T.rowt[:, 24:32], [[1, 8]], 608)])
 
-    pieces("ra", [(T.ra[:, 0:2], [[-15, 2]], 15), (T.ra[:, 2:4], [[-3855, 2]], 3840), (T.ra[:, 4:6], [[-225, 2]], 240), (T.ra[:, 6:16], [[0, 10]], 0)])
-    pieces("on", [(T.on[:, 0:4], [[0, 4]], 1)])
-    pieces("pa", [(T.pa[:, 0::2], [[0, 4], [-6, 2]], 8), (T.pa[:, 1::2], [[0, 4], [-3, 2]], 4)])
-    PA = ["pa"]
-    pieces("tk", [(T.tk[:, 0:36:2], [[0, 9], [4368, 2]], 1), (T.tk[:, 1:36:2], [[0, 18]], 15), (T.tk[:, 36:60], [[0, 24]], 1),
-                  (T.tk[:, 60:84], [[-4354, 2], [0, 12]], 4369), (T.tk[:, 84:96], [[0, 12]], 4369)])
-    pieces("hk", [(T.hk[:, 0::2], [[0, 9], [16, 2]], 0), (T.hk[:, 1::2], [[0, 18]], 16)])
-    pieces("rowt", [(T.rowt[:, 0:24:3], [[80, 2], [1, 4]], 0), (T.rowt[:, 1:24:3], [[80, 2], [1, 4]], 32),
-                    (T.rowt[:, 2:24:3], [[80, 2], [1, 4]], 48), (T.rowt[:, 24:32], [[1, 8]], 608)])
-
+    V(ms(T.kt[:], 0.0), [], ["ktz"])
     V(ms(T.et[:], 0.0), [], ["etz"])
-    names = ("rf", "gf", "of", "pf", "ge2", "r20", "lt4", "thr", "fix", "fx2", "ev", "lt6", "b3", "b", "lo", "a", "hi", "t0", "t1", "t2", "t3", "g4")
+    names = ("rf", "gf", "of", "pf", "ge2", "r20", "lt4", "thr", "fix", "ev", "lt6", "b3", "b", "lo", "a", "hi", "t0", "t1", "t2", "t3", "g4")
     one = {n: T.sc[:, i:i + 1] for i, n in enumerate(names)}
+    V(cp(one["pf"], T.ip[:]), ["ip"], ["pf"])
     V(ts(T.si[:, 0:1], T.ip[:], 15, None, A.bitwise_and), ["ip"], ["si0"])
     V(ts(T.si[:, 1:2], T.ip[:], 4, None, A.arith_shift_right), ["ip"], ["si1"])
     V(ts(T.si[:, 2:3], T.ip[:], 1, None, A.bitwise_and), ["ip"], ["si2"])
-    V(cp(one["pf"], T.ip[:]), ["ip"], ["pf"])
-    V(cp(T.sc[:, 0:3], T.si[:, 0:3]), ["si0", "si1", "si2"], ["rf"])
     V(ts(T.ident[:], T.flat[:, 0:128], one["pf"], None, A.is_equal), ["flat", "pf"], ["ident"])
+    V(cp(T.sc[:, 0:3], T.si[:, 0:3]), ["si0", "si1", "si2"], ["rf"])
+    V(cp(T.ul[:, 0:8], T.iu[:, 0:8]), ["iu"], ["ul0"])
     V(ts(one["r20"], one["rf"], 20.0, None, A.mult), ["rf"], ["r20"])
     V(ts(one["ge2"], one["rf"], 2.0, None, A.is_ge), ["rf"], ["ge2"])
     V(ts(one["lt4"], one["rf"], 4.0, BIG, A.is_lt, A.mult), ["rf"], ["lt4"])
-    V(ts(T.ro[:], T.i20[:], one["r20"], None, A.add), ["i20", "r20"], ["ro"])
     V(ts(T.dm[:], T.i16c[:], one["rf"], None, A.is_equal), ["i16c", "rf"], ["dm"])
-    V(ts(T.rm[:], T.i16c[:], 1.0, None, A.min), ["i16c"], ["rm"])
-    V(ts(one["thr"], one["lt4"], TINY, None, A.max), ["lt4"], ["thr"])
-    V(cp(T.ul[:, 0:8], T.iu[:, 0:8]), ["iu"], ["ul0"])
+    V(ts(T.ro[:], T.i20[:], one["r20"], None, A.add), ["i20", "r20"], ["ro"])
     V(ts(T.ul[:, 8:16], T.iu[:, 8:16], one["ge2"], None, A.add), ["iu", "ge2"], ["ul1"])
+    V(ts(one["thr"], one["lt4"], TINY, None, A.max), ["lt4"], ["thr"])
     V(ts(one["lt6"], one["rf"], 6.0, None, A.is_lt), ["rf"], ["lt6"])
     V(ts(T.eq[:, 0:8], T.flat[:, 0:8], one["gf"], None, A.is_equal), ["flat", "rf"], ["eq"])
-    V(ts(T.kw[:], T.dm[:], 8704.0, -512.0, A.mult, A.add), ["dm"], ["kw"])
+    V(tt(T.pr[:, 0:16], T.dm[:, 0:16], T.ra[:], A.mult), ["dm", "ra"], ["pr"])
 
-    S(T.kt[:], T.et[:, 0:544], ACT.Copy, ["etz"], "ktz")
-    for b in range(4):
-        S(T.et[:, 512 * b + b:512 * (b + 1):4], T.ident[:], ACT.Copy, ["ident", "etz", "ktz"], "et%d" % b)
-    ETK = ["et%d" % b for b in range(4)] + ["etz"]
-    S(one["fix"], one["rf"], ACT.Copy, ["rf"], "fix", scale=-512.0, bias=7680.0 + HALF)
     for h in range(2):
-        op("s", lambda: g.scalar.activation(T.rt[:, 512 * h:512 * (h + 1)], T.kt[:, 0:512], ACT.Copy), ["ktz"], ["rtz"], ["rtz"])
-    quant("qe", "et", ETK, 0, 512)
+        S(T.rt[:, 512 * h:512 * (h + 1)], T.kt[:, 0:512], ACT.Copy, ["ktz"], "rtz", ["rtz"])
+    for b in range(4):
+        S(T.et[:, 512 * b + b:512 * (b + 1):4], T.ident[:], ACT.Copy, ["ident", "etz"], "et%d" % b)
+    quant("qe", "et", ["et%d" % b for b in range(4)] + ["etz"], 0, 512)
+    S(T.rm[:], T.i16c[:], ACT.Sign, ["i16c"], "rm")
+    S(T.kw[:], T.dm[:], ACT.Copy, ["dm"], "kw", scale=8704.0, bias=-512.0)
+    S(one["fix"], one["rf"], ACT.Copy, ["rf"], "fix", scale=-512.0, bias=7680.0 + HALF)
 
+    def row_weights():
+        S(one["b3"], one["ge2"], ACT.Copy, ["ge2"], "b3", scale=2.0, bias=1.0)
+        S(one["ev"], one["of"], ACT.Copy, ["rf"], "ev", scale=-1.0, bias=1.0)
+        S(T.pr[:, 16:32], T.pr[:, 0:16], ACT.Copy, ["pr"], "a", accum_out=one["a"])
+        S(T.on[:, 8:12], T.on[:, 0:4], ACT.Copy, ["on", "rf"], "od4", scale=one["of"])
+        S(one["b"], one["b3"], ACT.Copy, ["b3", "lt6"], "b", scale=one["lt6"])
+        S(T.on[:, 4:8], T.on[:, 0:4], ACT.Copy, ["on", "ev"], "ev4", scale=one["ev"])
+
+    def tables_tile():
+        S(T.eq[:, 8:16], T.eq[:, 0:8], ACT.Copy, ["eq", "a"], "ag", scale=one["a"])
+        S(one["lo"], one["b"], ACT.Copy, ["b", "ev"], "lo", scale=one["ev"])
+        S(T.eq[:, 16:24], T.eq[:, 0:8], ACT.Copy, ["eq", "b"], "bg", scale=one["b"])
+        for n in range(4):
+            S(T.pb[:, n::4], T.on[:, 4:8] if n < 2 else T.on[:, 8:12], ACT.Copy, ["ev4", "od4"], "pb", ["pb"], scale=float(16 ** (3 - n)))
+        S(T.eq[:, 24:32], T.eq[:, 0:8], ACT.Copy, ["eq", "lo"], "lg", scale=one["lo"])
+        ag, bg, lg = [[T.eq[:, o + i:o + i + 1] for i in range(8)] for o in (8, 16, 24)]
+        fills = [(T.kt[:, 36:40], T.pa[:, 0:4], ag[1], "ag"), (T.kt[:, 44:48], T.pa[:, 0:4], ag[3], "ag"),
+                 (T.kt[:, 176:196:5], T.on[:, 0:4], ag[4], "ag"), (T.kt[:, 320:336], T.pa[:], ag[5], "ag"),
+                 (T.kt[:, 40:44], T.pb[:, 0:4], bg[2], "bg"), (T.kt[:, 33:34], T.on[:, 0:1], lg[0], "lg"),
+                 (T.kt[:, 272:288], T.pb[:], bg[5], "bg"), (T.kt[:, 368:384], T.pb[:], bg[6], "bg"), (T.kt[:, 224:244:5], T.on[:, 0:4], lg[4], "lg")]
+        for i, (out, src, f, key) in enumerate(fills):
+            S(out, src, ACT.Copy, ["pa", "on", key, "ktz", "rtz"] + (["pb"] if key == "bg" else []), "kt%d" % i, scale=f)
+        for i in (1, 2):
+            S(T.kt[:, 32 + 48 * i:48 + 48 * i], T.kt[:, 32:48], ACT.Copy, ["kt0", "kt1", "kt4", "kt5", "ktz"], "kt%d" % (8 + i))
+        return ["ktz"] + ["kt%d" % i for i in range(11)]
+
+    def way_back_constants():
+        S(T.rowt[0:64, 2:24:3], T.flat[0:64, 0:8], ACT.Copy, ["flat"], "rowt", bias=600.0)
+        S(one["g4"], one["gf"], ACT.Copy, ["rf"], "g4", scale=4.0)
+        for gg in range(7):
+            o = 512 * (gg // 4) + 64 * (gg + 1) + gg % 4
+            S(T.rt[:, o:o + 61:4], T.dm[:, 0:16], ACT.Copy, ["dm", "rtz"], "rt", ["rt"])
+        S(one["hi"], T.eq[:, 2:3], ACT.Identity, ["eq"], "hi", bias=T.eq[:, 4:5])
+        S(one["t0"], T.eq[:, 0:1], ACT.Copy, ["eq"], "t0", scale=-2.0, bias=2.0)
+        S(T.kd[:], T.dm[:], ACT.Copy, ["dm"], "kd", scale=34.0, bias=-2.0)
+        S(one["t1"], one["hi"], ACT.Copy, ["hi"], "t1", scale=4088.0, bias=8.0)
+        S(one["t2"], one["hi"], ACT.Copy, ["hi"], "t2", scale=252.0, bias=4.0)
+        S(one["t3"], one["hi"], ACT.Identity, ["hi", "t0"], "t3", scale=14.0, bias=one["t0"])
+
+    row_weights()
     partner = [rank ^ s for s in STEPS]
 
     def send(k, pairs, sem):
@@ -212,27 +256,36 @@ def rank_program(g, core, T, topo):
             cnt[sem] = cnt.get(sem, 0) + len(eng)
 
     def send_state(k):
-        need("g", ["qx%d" % k], [])
+        need("g", both("qx%d" % k), [])
         send(k, [(T["rq%d" % k][:].bitcast(dt.uint8), T["qx%d" % k][:].bitcast(dt.uint8)), (T["rs%d" % k][:], T["sx%d" % k][:])], "aq%d" % k)
-        done([], ["rq%d" % k], "aq%d" % k, cnt["aq%d" % k])
+        done([], both("rq%d" % k), "aq%d" % k, cnt["aq%d" % k])
 
     def send_list(k):
         need("g", ["al%d" % k], [])
         send(k, [(T["rl%d" % k][:], T["al%d" % k][:])], "ar%d" % k)
         done([], ["rl%d" % k], "ar%d" % k, cnt["ar%d" % k])
 
+    def quant_state(k):
+        for lo, hi, h in HALVES:
+            quant("qx%d" % k, "x%d" % k, ["x%d_%d" % (k, b) for b in range(3)] + ["x%d_3%s" % (k, h)] if k else ["x0"], lo, hi, "qx%d%s" % (k, h))
+
     def signs_mm(k):
         q, s = "qx%d" % k, "sx%d" % k
-        mm("b0", C, "up", "ups", 0, q, s, 0, ["up", "ups", q])
-        mm("b1", C, "up", "ups", 128, q, s, 0, ["up", "ups", q])
+        for i in range(2):
+            for (lo, hi, h), bank in zip(HALVES, SCORE[i]):
+                mm(bank, HALF, "up", "ups", 128 * i, q, s, lo, ["up", "ups", q + h])
 
-    def signs_table():
-        V(ts(T.tb1[:], T.b0[:, 0:C], 0.0, one["thr"], A.is_le, A.mult), ["b0", "thr"], ["tb1"])
-        V(tt(T.tb[:], T.b1[:, 0:C], T.tb1[:], A.is_gt), ["b1", "tb1"], ["tb"])
+    def signs_table(fill):
+        for i, ((lo, hi, h), bank) in enumerate(zip(HALVES, SCORE[0])):
+            V(ts(T.tb1[:, lo:hi], T[bank][:, 0:HALF], 0.0, one["thr"], A.is_le, A.mult), [bank, "thr"], ["tb1" + h])
+            fill(i)
+        for i, ((lo, hi, h), bank) in enumerate(zip(HALVES, SCORE[1])):
+            V(tt(T.tb[:, lo:hi], T[bank][:, 0:HALF], T.tb1[:, lo:hi], A.is_gt), [bank, "tb1" + h], ["tb" + h])
+            fill(2 + i)
 
-    def unpack_mm(codes, scales, key, parts, banks):
+    def unpack_mm(codes, scales, parts, banks):
         for b, bank in zip(parts, banks):
-            mm(bank, C, "qe", "qes", 128 * b, codes, scales, 0, ["qe", key])
+            mm(bank, C, "qe", "qes", 128 * b, codes, scales, 0, ["qe"] + both(codes))
 
     def unpack_copy(dst, parts):
         for b in parts:
@@ -241,103 +294,75 @@ def rank_program(g, core, T, topo):
     def lgn(n):
         return T.lg[:, 20 * n:20 * n + 20]
 
-    def cand_v(n, table, src):
-        V(tt(T.lm[:], T[table][:].indirect(lgn(src)), T.dm[:], A.mult), [table, "dm", "lg%d" % src], ["lm"])
+    def first_list(step, table=None):
+        if step == 0:
+            V(tt(T.lm[:], T[table][:].indirect(lgn(0)), T.dm[:], A.mult), [table, "dm", "lg0"], ["lm"])
+        elif step == 1:
+            V(scan(T.lsb[:], T.rm[:], T.lm[:], A.mult, A.add), ["rm", "lm"], ["lsb"])
+        else:
+            V(ts(lgn(1), T.lsb[:, 15::16], float(HALF), None, A.add), ["lsb"], ["lg1"])
 
-    def wrap_v(n):
-        V(scan(T.lsb[:], T.rm[:], T.lm[:], A.mult, A.add), ["rm", "lm"], ["lsb"])
-        V(ts(lgn(n), T.lsb[:, 15::16], float(HALF), None, A.add), ["lsb"], ["lg%d" % n])
+    def flat_list(n, table, lst, key):
+        S(T.lf[:, C * n:C * (n + 1)], T[table][:].indirect(lst), ACT.Copy, [table, key], "lf%d" % n)
 
-    def cand_s(n, table, src):
-        S(T.lf[:, C * (n % 2):C * (n % 2 + 1)], T[table][:].indirect(lgn(src)), ACT.Copy, [table, "lg%d" % src], "lf%d" % (n % 2))
+    def hold(out, n):
+        V(scan(T[out][:], T.kw[:], T.lf[:, C * n:C * (n + 1)], A.add, A.min), ["kw", "lf%d" % n], [out])
 
-    def wrap_s(n):
-        V(scan(T.lsc[:], T.kw[:], T.lf[:, C * (n % 2):C * (n % 2 + 1)], A.add, A.min), ["kw", "lf%d" % (n % 2)], ["lsc"])
-        V(ts(lgn(n), T.lsc[:, 15::16], one["fix"], None, A.add), ["lsc", "fix"], ["lg%d" % n])
+    def second_list():
+        V(ts(lgn(2), T.lsc[:, 15::16], one["fix"], None, A.add), ["lsc", "fix"], ["lg2"])
 
-    def gather(out, window, lst, rd, key, q, f=ACT.Copy):
+    def gather(out, window, lst, rd, key, q):
         if q == "v":
             V(cp(out, window.indirect(lst)), rd, [key])
         else:
-            S(out, window.indirect(lst), f, rd, key)
+            S(out, window.indirect(lst), ACT.Copy, rd, key)
 
-    def signs_at(n, q):
-        gather(T.gt[:, n:4 * C:4], T.tb[:], lgn(n), ["tb", "lg%d" % n], "gt%d" % n, q)
+    def signs_at(n, table, src, q, lo=0, hi=C):
+        keys = both("tb") if table == "tb" else [table]
+        gather(T.gt[:, 4 * lo + n:4 * hi:4], T[table][:], T.lg[:, 20 * src + lo // 16:20 * src + hi // 16], keys + ["lg%d" % src], "gt%d_%d" % (n, lo), q)
+
+    def signs_of_candidates():
+        S(T.tbp[:], T.tb[:].indirect(T.sl[:, 20:40]), ACT.Copy, both("tb") + ["pl"], "tbp")
+        signs_at(0, "tb", 0, "v")
+        signs_at(2, "tb", 2, "s", HALF, C)
+        signs_at(1, "tb", 1, "v")
+        signs_at(3, "tbp", 2, "s")
+        signs_at(2, "tb", 2, "v", 0, HALF)
+        return ["gt0_0", "gt1_0", "gt2_0", "gt2_%d" % HALF, "gt3_0"]
 
     V(ts(T.pw0[:], T.pint[:].indirect(T.ro[:]), -float(HALF), None, A.add), ["pint", "ro"], ["pw0"])
-    V(cp(T.pl16[:], pg32), ["pg32"], ["pl16"])
+    V(cp(T.sl[:, 20:40], pg32), ["pg32"], ["pl"])
     V(cp(lgn(0), kg32), ["kg32"], ["lg0"])
-    S(T.p2[:], T.pw0[:].indirect(T.pl16[:]), ACT.Copy, ["pw0", "pl16"], "p2")
+    S(T.p2[:], T.pw0[:].indirect(T.sl[:, 20:40]), ACT.Copy, ["pw0", "pl"], "p2")
     quant("qu", "ut", ["ut"], 0, 128)
-    cand_v(1, "pw0", 0)
-    quant("qx0", "x0", ["x0"], 0, C)
-    send_state(0)
-    wrap_v(1)
     ULK = ["ul0", "ul1"]
     S(T.ups[:], T.qus[:].indirect(T.ul[:]), ACT.Copy, ["qu"] + ULK, "ups")
+    flat_list(0, "p2", lgn(0), "lg0")
+    first_list(0, "pw0")
     V(cp(T.up[:].bitcast(dt.uint32), T.qu[:].bitcast(dt.uint32).indirect(T.ul[:])), ["qu"] + ULK, ["up"])
+    quant_state(0)
+    send_state(0)
     signs_mm(0)
-    cand_s(2, "p2", 0)
-    cand_s(3, "p2", 1)
-    V(tt(T.pr[:, 0:16], T.dm[:, 0:16], T.ra[:], A.mult), ["dm", "ra"], ["pr"])
-    wrap_s(2)
-    signs_table()
-    wrap_s(3)
-    iota(T.st[:], [[0, 656]], 0, [], "st")
-    iota(T.flat[:, 128:C], [[1, C - 128]], 128, [], "flat2")
-
-    def tables_tile():
-        S(T.pr[:, 16:32], T.pr[:, 0:16], ACT.Copy, ["pr"], "a", accum_out=one["a"])
-        S(one["b3"], one["ge2"], ACT.Copy, ["ge2"], "b3", scale=2.0, bias=1.0)
-        S(one["ev"], one["of"], ACT.Copy, ["rf"], "ev", scale=-1.0, bias=1.0)
-        S(T.on[:, 8:12], T.on[:, 0:4], ACT.Copy, ["on", "rf"], "od4", scale=one["of"])
-        S(one["b"], one["b3"], ACT.Copy, ["b3", "lt6"], "b", scale=one["lt6"])
-        S(T.on[:, 4:8], T.on[:, 0:4], ACT.Copy, ["on", "ev"], "ev4", scale=one["ev"])
-        S(T.eq[:, 8:16], T.eq[:, 0:8], ACT.Copy, ["eq", "a"], "ag", scale=one["a"])
-        S(one["lo"], one["b"], ACT.Copy, ["b", "ev"], "lo", scale=one["ev"])
-        S(T.eq[:, 16:24], T.eq[:, 0:8], ACT.Copy, ["eq", "b"], "bg", scale=one["b"])
-        for n in range(4):
-            S(T.pb[:, n::4], T.on[:, 4:8] if n < 2 else T.on[:, 8:12], ACT.Copy, ["ev4", "od4"], "pb%d" % n, scale=float(16 ** (3 - n)))
-        PB = ["pb%d" % n for n in range(4)]
-        S(T.eq[:, 24:32], T.eq[:, 0:8], ACT.Copy, ["eq", "lo"], "lg", scale=one["lo"])
-        ag, bg, lg = [[T.eq[:, o + i:o + i + 1] for i in range(8)] for o in (8, 16, 24)]
-        fills = [(T.kt[:, 36:40], T.pa[:, 0:4], ag[1]), (T.kt[:, 44:48], T.pa[:, 0:4], ag[3]), (T.kt[:, 40:44], T.pb[:, 0:4], bg[2]), (T.kt[:, 33:34], T.on[:, 0:1], lg[0]),
-                 (T.kt[:, 176:196:5], T.on[:, 0:4], ag[4]), (T.kt[:, 224:244:5], T.on[:, 0:4], lg[4]),
-                 (T.kt[:, 272:288], T.pb[:], bg[5]), (T.kt[:, 320:336], T.pa[:], ag[5]), (T.kt[:, 368:384], T.pb[:], bg[6])]
-        for i, (out, src, f) in enumerate(fills):
-            S(out, src, ACT.Copy, PA + PB + ["on", "ag", "bg", "lg", "ktz", "rtz"], "kt%d" % i, scale=f)
-        for i in (1, 2):
-            S(T.kt[:, 32 + 48 * i:48 + 48 * i], T.kt[:, 32:48], ACT.Copy, ["kt0", "kt1", "kt2", "kt3", "ktz"], "kt%d" % (8 + i))
-        return ["ktz"] + ["kt%d" % i for i in range(11)]
-
+    first_list(1)
     KTK = tables_tile()
+    signs_table(lambda i: [lambda: hold("lsc", 0), lambda: first_list(2), second_list, lambda: quant("qk", "kt", KTK, 0, 136)][i]())
+    iota("st", [(T.st[:], [[0, 656]], 0)])
+    iota("flat2", [(T.flat[:, 128:C], [[1, C - 128]], 128)])
 
-    def way_back_constants():
-        keys = ["rtz"]
-        S(T.rowt[0:64, 2:24:3], T.flat[0:64, 0:8], ACT.Copy, ["flat"], "rowt", bias=600.0)
-        S(one["g4"], one["gf"], ACT.Copy, ["rf"], "g4", scale=4.0)
-        for gg in range(7):
-            o = 512 * (gg // 4) + 64 * (gg + 1) + gg % 4
-            keys.append("rt%d" % gg)
-            S(T.rt[:, o:o + 61:4], T.dm[:, 0:16], ACT.Copy, ["dm", "rtz"], keys[-1])
-        S(one["hi"], T.eq[:, 2:3], ACT.Identity, ["eq"], "hi", bias=T.eq[:, 4:5])
-        S(one["t0"], T.eq[:, 0:1], ACT.Copy, ["eq"], "t0", scale=-2.0, bias=2.0)
-        S(one["t1"], one["hi"], ACT.Copy, ["hi"], "t1", scale=4088.0, bias=8.0)
-        S(one["t2"], one["hi"], ACT.Copy, ["hi"], "t2", scale=252.0, bias=4.0)
-        S(one["t3"], one["hi"], ACT.Identity, ["hi", "t0"], "t3", scale=14.0, bias=one["t0"])
-        return keys
+    def differences(step):
+        if step == 0:
+            V(cp(T.lw[:, 20:60], T.lg[:, 20:60]), ["lg1", "lg2"], ["lw"])
+            V(ts(T.lw[:, 60:80], lgn(2), one["fix"], None, A.subtract), ["lg2", "fix"], ["lw3"])
+        elif step == 1:
+            for i in (1, 2):
+                V(tt(T.dd[:, i::4], T.lw[:, 20 * (3 - i):20 * (4 - i)], T.lw[:, 20 * (2 - i):20 * (3 - i)], A.subtract), ["lw", "lw0"], ["dd%d" % i])
+        else:
+            V(tt(T.dd[:, 0::4], T.lsd[:, 15::16], T.lw[:, 60:80], A.subtract), ["lsd", "lw3"], ["dd0"])
 
-    def differences(first):
-        lo = 0 if first else 20
-        V(cp(T.lw[:, lo:80], T.lg[:, lo:80]), ["lg%d" % n for n in range(4)], ["lw"])
-        if first:
-            V(cp(T.dd[:, 3::4], T.lg[:, 0:20]), ["lg0"], ["dd3"])
-        for i in range(3):
-            V(tt(T.dd[:, i::4], T.lw[:, 20 * (3 - i):20 * (4 - i)], T.lw[:, 20 * (2 - i):20 * (3 - i)], A.subtract), ["lw"], ["dd%d" % i])
-
-    def chain(k, freed, fill):
+    def chain(freed, fill):
         V(tt(T.ti[:], T.b2[:, 0:96], T.tk[:], A.add), ["b2", "tk"], ["tia", "tib", "t5", "t6"])
         freed()
+        fill(0)
         UP, DOWN = (3, 0x1111), (12, 15)
 
         def times(out, table, state, rd, key):
@@ -346,23 +371,28 @@ def rank_program(g, core, T, topo):
         def pick(out, src, kind, rd, wr):
             V(ts(out, src, kind[0], kind[1], A.arith_shift_right, A.bitwise_and), rd, wr)
 
-        times(T.pd[:, 0:9], T.ti[:, 1:36:4], T.ti[:, 0:36:4], ["tia"], "pd1")
         times(T.pd[:, 40:64], T.ti[:, 60:84], T.ti[:, 36:60], ["tib", "t5"], "pe1")
-        pick(T.sv[:, 3:12], T.pd[:, 0:9], UP, ["pd1"], ["s1", "s2", "s3"])
-        pick(T.bi[:, 24:36], T.pd[:, 52:64], UP, ["pe1"], ["bh"])
-        times(T.pd[:, 9:18], T.ti[:, 2:36:4], T.sv[:, 3:12], ["tia", "s1", "s2", "s3"], "pd2")
-        times(T.pd[:, 64:76], T.ti[:, 84:96], T.bi[:, 24:36], ["t6", "bh"], "pe2")
-        pick(T.sv[:, 6:15], T.pd[:, 9:18], DOWN, ["pd2"], ["s2", "s3", "s4"])
-        pick(T.bi[:, 0:12], T.pd[:, 40:52], DOWN, ["pe1"], ["b5l"])
-        pick(T.bi[:, 12:24], T.pd[:, 64:76], DOWN, ["pe2"], ["b6l"])
-        times(T.pd[:, 18:27], T.ti[:, 3:36:4], T.sv[:, 6:15], ["tia", "s2", "s3", "s4"], "pd3")
-        V(cp(T.ti[:, 60:84], T.bi[:, 0:24]), ["b5l", "b6l"], ["t5"])
-        pick(T.sv[:, 9:18], T.pd[:, 18:27], UP, ["pd3"], ["s3", "s4", "s5"])
-        V(scan(T.pk[:], T.hk[:], T.ti[:, 48:84], A.mult, A.add), ["hk", "tib", "t5"], ["pk"])
+        times(T.pd[:, 0:9], T.ti[:, 1:36:4], T.ti[:, 0:36:4], ["tia"], "pd1")
         V(cp(T.sv[:, 0:3], T.ti[:, 0:12:4]), ["tia"], ["s0"])
+        pick(T.bi[:, 24:36], T.pd[:, 52:64], UP, ["pe1"], ["bh"])
+        pick(T.sv[:, 3:12], T.pd[:, 0:9], UP, ["pd1"], ["s1", "s2", "s3"])
+        pick(T.bi[:, 0:12], T.pd[:, 40:52], DOWN, ["pe1"], ["b5l"])
+        times(T.pd[:, 64:76], T.ti[:, 84:96], T.bi[:, 24:36], ["t6", "bh"], "pe2")
+        times(T.pd[:, 9:18], T.ti[:, 2:36:4], T.sv[:, 3:12], ["tia", "s1", "s2", "s3"], "pd2")
+        fill(1)
+        pick(T.bi[:, 12:24], T.pd[:, 64:76], DOWN, ["pe2"], ["b6l"])
+        pick(T.sv[:, 6:15], T.pd[:, 9:18], DOWN, ["pd2"], ["s2", "s3", "s4"])
+        fill(2)
+        V(cp(T.ti[:, 60:84], T.bi[:, 0:24]), ["b5l", "b6l"], ["t5"])
+        times(T.pd[:, 18:27], T.ti[:, 3:36:4], T.sv[:, 6:15], ["tia", "s2", "s3", "s4"], "pd3")
+        fill(3)
+        V(scan(T.pk[:], T.hk[:], T.ti[:, 48:84], A.mult, A.add), ["hk", "tib", "t5"], ["pk"])
+        pick(T.sv[:, 9:18], T.pd[:, 18:27], UP, ["pd3"], ["s3", "s4", "s5"])
+        fill(4)
         times(T.pd[:, 27:36], T.pk[:, 3::4], T.sv[:, 9:18], ["pk", "s3", "s4", "s5"], "pd4")
-        fill()
+        fill(5)
         pick(T.sv[:, 12:21], T.pd[:, 27:36], DOWN, ["pd4"], ["s4", "s5", "s6"])
+        fill(6)
         V(cp(T.st[:].indirect(T.scl[:]), T.sv[:]), ["s%d" % i for i in range(8)] + ["scl"], ["st"])
         quant("qs", "st", ["st"], 0, 148)
         for h in range(2):
@@ -375,106 +405,126 @@ def rank_program(g, core, T, topo):
         V(cp(T["al%d" % k][:], T.af[:, 3::4]), ["af"], ["al%d" % k])
 
     def sigma(k):
-        a = "al%d" % k
-        V(ts(T.vb[:, 0:HALF], T.tb1[:].indirect(T[a][:, 0:10]), 0.0, None, A.is_gt), ["tb1", a], ["vb0"])
-        S(T.vb[:, HALF:C], T.tb1[:].indirect(T[a][:, 10:20]), ACT.Sign, ["tb1", a], "vb1")
+        a, n = "al%d" % k, 40 if k < 2 else 20
+        V(ts(T.vb[:, 0:HALF], T.tb1[:].indirect(T[a][:, 0:10]), 0.0, None, A.is_gt), both("tb1") + [a], ["vb0"])
+        S(T.vb[:, HALF:C], T.tb1[:].indirect(T[a][:, 10:20]), ACT.Sign, both("tb1") + [a], "vb1")
         for h in range(2):
             gather(T.ym[:, HALF * h:HALF * (h + 1)], T.vb[:], T.ml[:, 10 * h:10 * h + 10], ["vb0", "vb1", "ml"], "ym%d" % h, "vs"[h])
         V(scan(T.ysc[:, 0:C], T.kd[:], T.vb[:], A.add, A.min), ["kd", "vb0", "vb1"], ["ysc0"])
         V(scan(T.ysc[:, C:2 * C], T.kd[:], T.ym[:], A.add, A.min), ["kd", "ym0", "ym1"], ["ysc1"])
-        V(tt(T.sf[:, 40:60], T.ysc[:, 15:C:16], T.ysc[:, C + 15::16], A.not_equal), ["ysc0", "ysc1"], ["df"])
-        V(tt(T.sf[:, 0:20], T.sf[:, 40:60], T.mj[:], A.mult), ["df", "mj"], ["sf0"])
-        V(tt(T.sf[:, 20:40], T.sf[:, 0:20], T.jw[:, 0:20], A.add), ["sf0", "jw"], ["sf1"])
-        V(cp(T.sl[:], T.sf[:, 20:40]), ["sf1"], ["sl"])
+        for o in range(0, n, 20):
+            V(tt(T.sf[:, o:o + 20], T.ysc[:, 15:C:16], T.ysc[:, C + 15::16], A.not_equal), ["ysc0", "ysc1"], ["df%d" % o])
+        V(tt(T.sf[:, 40:40 + n], T.sf[:, 0:n], T.dj[:, 0:n], A.mult), ["df0", "df20", "mj", "dl"], ["sf0"])
+        V(tt(T.sf[:, 80:80 + n], T.sf[:, 40:40 + n], T.pj[:, 0:n], A.add), ["sf0", "jw", "pp"], ["sf1"])
+        return lambda: V(cp(T.sl[:, 0:n], T.sf[:, 80:80 + n]), ["sf1"], ["sl", "pl"])
 
-    def new_p(k):
-        old, new = "pw%d" % (k % 2), "pw%d" % (1 - k % 2)
-        S(T[new][:], T[old][:].indirect(T.sl[:]), ACT.Copy, [old, "sl"], new)
+    def carry(step):
+        if step == 0:
+            V(cp(T.pj[:, 20:40], T.sf[:, 100:120]), ["sf1"], ["pp"])
+            V(ts(T.sf[:, 0:20], T.sf[:, 60:80], -2.0, None, A.mult), ["sf0"], ["df0"])
+        else:
+            V(tt(T.dj[:, 20:40], T.dj[:, 20:40], T.sf[:, 0:20], A.add), ["df0"], ["dl"])
+
+    FIRST = {
+        1: [(tt(T.pr[:], T.dm[:, 0:32], T.rowt[:], A.mult), ["dm", "rowt", "a"], ["pr", "prs"]), (ms(T.sv[:, 21:32], 0), [], ["s7"])],
+        2: [(scan(T.rsc[:], T.rm[:, 0:32], T.pr[:], A.mult, A.add), ["rm", "prs"], ["rsc"]), (cp(T.ml[:], mg32), ["mg32"], ["ml"])],
+        3: [(ts(T.scl[:], T.rsc[:, 15::16], one["g4"], None, A.add), ["rsc", "g4"], ["scl"]), (ms(T.mt[:, 0::4], 0.0), [], ["mt0"])],
+        4: [(cp(T.dd[:, 3::4], lgn(0)), ["lg0"], ["dd3"]), (ts(T.pj[:, 0:20], T.i20[:], 16.0, one["rf"], A.mult, A.add), ["i20", "rf"], ["jw"])],
+        0: [(cp(T.pj[:, 20:40], pg32), ["pg32"], ["pp"])],
+        6: [(ts(T.sf[:, 80:100], pg32, one["fix"], None, A.subtract), ["pg32", "fix"], ["sf1"]), (tt(T.dj[:, 0:20], mg32, T.pj[:, 0:20], A.subtract), ["mg32", "jw"], ["mj"])],
+    }
 
     for k in range(3):
         qx, sx, first, last = "qx%d" % k, "sx%d" % k, k == 0, k == 2
-        pw = "pw%d" % (k % 2)
+        pw, nxt = "pw%d" % (k % 2), "pw%d" % (1 - k % 2)
         if k:
-            cand_s(2, pw, 1)
-            quant(qx, "x%d" % k, ["x%d_%d" % (k, b) for b in range(4)], 0, C)
+            flat_list(0, pw, lgn(1), "lg1")
+            quant_state(k)
             send_state(k)
             signs_mm(k)
-            wrap_s(2)
-            cand_s(3, pw, 2)
-            signs_table()
-            signs_at(1, "s")
-            wrap_s(3)
-            signs_at(2, "s")
-            signs_at(0, "v")
-            signs_at(3, "v")
-        else:
-            signs_at(0, "v")
-            signs_at(1, "s")
-            signs_at(2, "s")
-            signs_at(3, "v")
-        unpack_mm(qx, sx, qx, [0, 1, 2], ["b4", "b5", "b6"])
-        GT = ["gt%d" % n for n in range(4)]
+            hold("lsc", 0)
+            signs_table(lambda i: second_list() if i == 0 else None)
+        GT = signs_of_candidates()
+        unpack_mm(qx, sx, [0, 1, 2], ["b4", "b5", "b6"])
+        flat_list(1, pw, lgn(2), "lg2")
+        for b, (q, lo, at) in enumerate(BLOCKS):
+            quant(q, "gt", GT, lo, lo + 128, "qg%d" % b, at)
+            mm("b2", 128, q, q + "s", at, "qk", "qks", 8 - 4 * b, ["qg%d" % b, "qk"], b == 0, b == 2)
         if first:
-            quant("qk", "kt", KTK, 0, 136)
-        quant("qg", "gt", GT, 0, 128, "qga")
-        quant("qg", "gt", GT, 128, C, "qgb")
-        for b in range(3):
-            mm("b2", 128, "qg", "qgs", VIEW[b], "qk", "qks", 8 - 4 * b, ["qga" if b == 0 else "qgb", "qk"], b == 0, b == 2)
-        own_last = lambda: unpack_mm(qx, sx, qx, [3], ["b2"])
-        if first:
-            RTK = way_back_constants()
-            V(tt(T.pr[:], T.dm[:, 0:32], T.rowt[:], A.mult), ["dm", "rowt", "a"], ["pr", "prs"])
-            V(scan(T.rsc[:], T.rm[:, 0:32], T.pr[:], A.mult, A.add), ["rm", "prs"], ["rsc"])
-            V(ms(T.sv[:, 21:32], 0), [], ["s7"])
-            V(ts(T.scl[:], T.rsc[:, 15::16], one["g4"], None, A.add), ["rsc", "g4"], ["scl"])
-        else:
-            differences(False)
+            way_back_constants()
+            V(cp(T.lw[:, 0:20], lgn(0)), ["lg0"], ["lw0"])
+        differences(0)
+        hold("lsd", 1)
         unpack_copy("fo", [0, 1, 2])
-        chain(k, own_last, (lambda: quant("qr", "rt", RTK, 0, 256)) if first else (lambda: None))
+
+        def fill(i):
+            if i == 0:
+                differences(1)
+            if i == (5 if k else 6):
+                differences(2)
+            if first:
+                for call in FIRST.get(i, []):
+                    V(*call)
+                if i == 2:
+                    flat_list(0, pw, T.ml[:], "ml")
+                if i == 5:
+                    quant("qr", "rt", ["rt", "rtz"], 0, 256)
+            if k == 1 and i in (1, 2):
+                carry(i - 1)
+
+        chain(lambda: unpack_mm(qx, sx, [3], ["b2"]), fill)
         if first:
-            V(ms(T.mt[:, 0::4], 0.0), [], ["mt0"])
-            differences(True)
-        unpack_mm("rq%d" % k, "rs%d" % k, "rq%d" % k, [0, 1, 2, 3], ["b4", "b5", "b6", "b7"])
+            hold("lsc", 0)
+        unpack_mm("rq%d" % k, "rs%d" % k, [0, 1, 2, 3], ["b4", "b5", "b6", "b7"])
         select(k)
         send_list(k)
         if first:
-            V(ts(T.jw[:, 0:20], T.i20[:], 16.0, one["rf"], A.mult, A.add), ["i20", "rf"], ["jw"])
-            V(cp(T.ml[:], mg32), ["mg32"], ["ml"])
-            V(tt(T.mj[:], mg32, T.jw[:, 0:20], A.subtract), ["mg32", "jw"], ["mj"])
-            V(ts(T.kd[:], T.dm[:], 34.0, -2.0, A.mult, A.add), ["dm"], ["kd"])
+            V(tt(T.dj[:, 20:40], T.lsc[:, 15::16], T.sf[:, 80:100], A.subtract), ["lsc", "sf1"], ["dl"])
         unpack_copy("fp", [0])
-        sigma(k)
+        as_list = sigma(k)
         unpack_copy("fp", [1, 2, 3])
         for t in range(4):
             gather(T.zt[:, t:4 * C:4], T.fp[:, C * t:C * (t + 1)], T["rl%d" % k][:], ["fp%d" % t, "rl%d" % k], "zt%d" % t, "vs"[t % 2])
-        new_p(k)
-        quant("qz", "zt", ["zt%d" % t for t in range(4)], 0, C)
-        for b in range(4):
-            mm("b%d" % (4 + b), C, "wq", "wqs", 128 * b, "qz", "qzs", 0, ["wq", "wqs", "qz"])
-        for b in range(4):
+            if t == 0:
+                as_list()
+        if last:
+            S(T.plo[:, 0:C], T.flat[:].indirect(T.al2[:]), ACT.Copy, ["flat", "flat2", "al2"], "plo0")
+        else:
+            S(T[nxt][:], T[pw][:].indirect(T.sl[:, 0:20]), ACT.Copy, [pw, "sl"], nxt)
+        for lo, hi, h in HALVES:
+            quant("qz", "zt", ["zt%d" % t for t in range(4)], lo, hi, "qz" + h)
+        for (lo, hi, h), bank in zip(HALVES, ("b4", "b0")):
+            mm(bank, HALF, "wq", "wqs", 0, "qz", "qzs", lo, ["wq", "wqs", "qz" + h])
+            S(T.hs[:, lo:hi], T[bank][:, 0:HALF], ACT.Copy, [bank], "hs0" + h, scale=0.03125)
+        for b in (1, 3, 2):
+            mm("b%d" % (4 + b), C, "wq", "wqs", 128 * b, "qz", "qzs", 0, ["wq", "wqs"] + both("qz"))
             S(T.hs[:, C * b:C * (b + 1)], T["b%d" % (4 + b)][:, 0:C], ACT.Copy, ["b%d" % (4 + b)], "hs%d" % b, scale=0.03125)
+        a, x = "al%d" % k, "x%d" % (k + 1)
+        for lo, hi, h in HALVES:
+            S(T.ks[:, lo:hi], T.hs[:, 3 * C:4 * C].indirect(T[a][:, lo // 16:hi // 16]), ACT.Copy, ["hs3", a], "ks" + h)
         if not last:
-            cand_v(1, "pw%d" % (1 - k % 2), 0)
-            wrap_v(1)
+            first_list(0, nxt)
+            first_list(1)
         else:
             quant("qv", "vt", ["vt"], 0, 128)
-        a, x = "al%d" % k, "x%d" % (k + 1)
-        S(T.ks[:], T.hs[:, 3 * C:4 * C].indirect(T[a][:]), ACT.Copy, ["hs3", a], "ks")
         for b in range(3):
-            V(tt(T[x][:, b::4], T.hs[:, C * b:C * (b + 1)].indirect(T[a][:]), T.fo[:, C * b:C * (b + 1)], A.add), ["hs%d" % b, a, "fo%d" % b], ["%s_%d" % (x, b)])
-        V(tt(T[x][:, 3::4], T.b2[:, 0:C], T.ks[:], A.add), ["b2", "ks"], [x + "_3"])
+            V(tt(T[x][:, b::4], T.hs[:, C * b:C * (b + 1)].indirect(T[a][:]), T.fo[:, C * b:C * (b + 1)], A.add),
+              (both("hs0") if b == 0 else ["hs%d" % b]) + [a, "fo%d" % b], ["%s_%d" % (x, b)])
+            if not last and b == 0:
+                first_list(2)
+        for lo, hi, h in HALVES:
+            V(tt(T[x][:, 4 * lo + 3:4 * hi:4], T.b2[:, lo:hi], T.ks[:, lo:hi], A.add), ["b2", "ks" + h], [x + "_3" + h])
 
-    S(T.plo[:, 0:C], T.flat[:].indirect(T.al2[:]), ACT.Copy, ["flat", "flat2", "al2"], "plo0")
-    S(T.plo[:, C:2 * C], T.pw1[:], ACT.Copy, ["pw1"], "plo1", bias=float(HALF))
-    quant("qx3", "x3", ["x3_%d" % b for b in range(4)], 0, C)
-    for h in range(2):
-        mm("b%d" % (2 * h), C // 2, "qv", "qvs", 0, "qx3", "sx3", C // 2 * h, ["qv", "qx3"])
-    dma("y", "d_oc", T.oc[:], T.qx3[:].bitcast(dt.uint8), ["qx3"], [])
+    S(T.plo[:, C:2 * C], T.pw0[:].indirect(T.sl[:, 0:20]), ACT.Copy, ["pw0", "sl"], "plo1", bias=float(HALF))
+    dma("s", "d_op", T.pl[:], T.plo[0::16, :], ["plo0", "plo1"], [])
+    quant_state(3)
+    for (lo, hi, h), bank in zip(HALVES, ("b0", "b1")):
+        mm(bank, HALF, "qv", "qvs", 0, "qx3", "sx3", lo, ["qv", "qx3" + h])
+        dma("y", "d_oc", T.oc[:, 4 * lo:4 * hi], T.qx3[:, lo:hi].bitcast(dt.uint8), ["qx3" + h], [])
     for i in range(4):
-        dma("y", "d_os", T.osc[4 * i:4 * i + 4, :], T.sx3[32 * i:32 * i + 4, :], ["qx3"], [])
-    dma("y", "d_op", T.pl[:], T.plo[0::16, :], ["plo0", "plo1"], [])
-    V(cp(T.yo[:, 0:C // 2], T.b0[:, 0:C // 2]), ["b0"], ["yo0"])
-    S(T.yo[:, C // 2:C], T.b2[:, 0:C // 2], ACT.Copy, ["b2"], "yo1")
-    dma("s", "d_oy", T.y[:], T.yo[:], ["yo0", "yo1"], [])
+        dma("y", "d_os", T.osc[4 * i:4 * i + 4, :], T.sx3[32 * i:32 * i + 4, :], both("qx3"), [])
+    for (lo, hi, h), bank in zip(HALVES, ("b0", "b1")):
+        V(cp(T.yo[:, lo:hi], T[bank][:, 0:HALF]), [bank], ["yo" + h])
+        dma("s", "d_oy", T.y[:, lo:hi], T.yo[:, lo:hi], ["yo" + h], [])
     for s, v in cnt.items():
         g.wait_ge(T.sem[s], v)

@@ -29,36 +29,36 @@ for _k in range(2):
     _sb("pw%d" % _k, C, "bfloat16")
 for _n, _c, _d in [
     ("ut", 512, "bfloat16"), ("vt", 512, "bfloat16"), ("zt", 4 * C, "bfloat16"),
-    ("gt", 4 * C, "bfloat16"), ("st", 656, "bfloat16"), ("kt", 544, "bfloat16"), ("et", 2048, "bfloat16"), ("rt", 1024, "bfloat16"),
+    ("gt", 4 * C, "bfloat16"), ("st", 656, "bfloat16"), ("kt", 560, "bfloat16"), ("et", 2048, "bfloat16"), ("rt", 1024, "bfloat16"),
     ("pint", C, "int32"), ("l32", 60, "int32"), ("p2", C, "bfloat16"),
     ("ip", 1, "int32"), ("si", 4, "int32"), ("sc", 24, "float32"),
     ("i16c", C, "bfloat16"), ("flat", C, "float32"), ("i20", 20, "int32"), ("iu", 16, "int32"),
     ("pj", 40, "float32"), ("dj", 40, "float32"), ("ro", 20, "uint16"), ("ml", 20, "uint16"), ("ul", 16, "uint16"),
-    ("dm", C, "bfloat16"), ("rm", C, "bfloat16"), ("kw", C, "bfloat16"), ("kd", C, "bfloat16"), ("ident", 128, "bfloat16"),
+    ("dm", C, "bfloat16"), ("kw", C, "bfloat16"), ("kd", C, "bfloat16"), ("ident", 128, "bfloat16"),
     ("ra", 16, "float32"), ("pr", 32, "float32"), ("eq", 32, "float32"), ("pa", 16, "float32"), ("pb", 16, "float32"), ("on", 12, "float32"),
     ("rowt", 32, "float32"), ("rsc", 32, "float32"), ("scl", 2, "uint16"),
-    ("tk", 96, "float32"), ("ti", 96, "float32"), ("hk", 36, "float32"), ("pk", 36, "float32"),
-    ("pd", 80, "int32"), ("bi", 36, "int32"), ("sv", 32, "int32"),
+    ("tk", 126, "float32"), ("w", 270, "int32"), ("pk", 72, "int32"), ("pd", 80, "int32"), ("e2", 36, "int32"),
     ("tb1", C, "bfloat16"), ("tb", C, "bfloat16"), ("tbp", C, "bfloat16"), ("vb", C, "bfloat16"), ("ym", C, "bfloat16"), ("ysc", 2 * C, "bfloat16"),
-    ("lm", C, "bfloat16"), ("lf", 2 * C, "bfloat16"), ("lsb", C, "bfloat16"), ("lsc", C, "float32"), ("lsd", C, "float32"),
-    ("lg", 60, "uint16"), ("lw", 80, "float32"),
+    ("lf", 4 * C, "bfloat16"), ("ls0", C, "float32"), ("ls1", C, "float32"), ("ls2", C, "float32"), ("ls3", C, "float32"),
+    ("lg", 60, "uint16"), ("lw", 20, "float32"),
     ("mt", 80, "float32"), ("dd", 80, "float32"), ("af", 80, "float32"),
     ("sf", 120, "float32"), ("sl", 40, "uint16"),
     ("fo", 3 * C, "bfloat16"), ("fp", 4 * C, "bfloat16"), ("hs", 4 * C, "float32"), ("ks", C, "float32"), ("yo", C, "float32"), ("plo", 2 * C, "float32"),
 ]:
     _sb(_n, _c, _d)
-for _n, _c in [("qu", 128), ("up", 256), ("qv", 128), ("wq", 512), ("qe", 512), ("qr", 256), ("qk", 136), ("qg", 256), ("qh", 128), ("qs", 148), ("qz", C)]:
+for _n, _c in [("qu", 128), ("up", 256), ("qv", 128), ("wq", 512), ("qe", 512), ("qr", 256), ("qk", 140), ("qg", 256), ("qh", 128), ("qs", 148), ("qz", C)]:
     _sb(_n, _c, "float8_e4m3fn_x4")
     _sb(_n + "s", _c, "uint8")
 for _k in range(8):
     SCRATCH["b%d" % _k] = ("psum", [128, 512], "float32")
-LOADS = ["dx", "du", "dp", "dk", "dm", "dg", "dw", "dws", "dv", "oy", "oc", "os", "op"]
+LOADS = ["dxa", "dxb", "du", "dp", "dk", "dm", "dg", "dw", "dws", "dv", "oy", "oc", "os", "op"]
 LOADS = ["d_" + _n for _n in LOADS]
 SEMAPHORES += LOADS
 
 A = AluOpType
 ACT = ActivationFunctionType
 HALVES = ((0, HALF, "a"), (HALF, C, "b"))
+RUNS = ((0, 192, "a"), (192, C, "b"))
 BLOCKS = (("qg", 0, 0), ("qg", 128, 128), ("qh", 192, 0))
 SCORE = (("b0", "b3"), ("b1", "b7"))
 
@@ -142,18 +142,19 @@ def rank_program(g, core, T, topo):
         op("t", lambda: g.tensor.matmul_mx(T[bank][:, 0:n], T[w][:, wa:wa + 128], T[ws][:, wa:wa + 128], T[x][:, xa:xa + n], T[xs][:, xa:xa + n], start, stop),
            reads, [bank], [] if start else [bank])
 
-    def iota(key, parts, cm=0):
+    def iota(key, parts, cm=0, after=()):
         for out, pattern, base in parts:
-            op("g", lambda: g.iota(out, pattern, base, cm, allow_small_or_imprecise_dtypes=True), [], [key], [key])
+            op("g", lambda: g.iota(out, pattern, base, cm, allow_small_or_imprecise_dtypes=True), list(after), [key], [key])
 
     kg32, pg32, mg32 = T.l32[:, 0:20], T.l32[:, 20:40], T.l32[:, 40:60]
-    for r in range(16):
-        dma("y" if r % 2 else "s", "d_dp", T.pint[r::16, :], T.pg[:], [], ["pint"], ["pint"])
-    dma("s", "d_dg", pg32, T.pg[:], [], ["pg32"])
-    dma("y", "d_dk", kg32, T.kg[:], [], ["kg32"])
     dma("s", "d_du", T.ut[:], T.u[:], [], ["ut"])
-    dma("y", "d_dx", T.x0[:], T.x[:], [], ["x0"])
+    dma("y", "d_dg", pg32, T.pg[:], [], ["pg32"])
+    dma("y", "d_dk", kg32, T.kg[:], [], ["kg32"])
+    for r in range(16):
+        dma("y" if r % 2 and r < 15 else "s", "d_dp", T.pint[r::16, :], T.pg[:], [], ["pint"], ["pint"])
     dma("y", "d_dm", mg32, T.mg[:], [], ["mg32"])
+    for lo, hi, h in HALVES:
+        dma("y", "d_dx" + h, T.x0[:, 4 * lo:4 * hi], T.x[:, 4 * lo:4 * hi], [], ["x0" + h])
     dma("y", "d_dw", T.wq[:].bitcast(dt.uint8), T.wc[:], [], ["wq"])
     dma("y", "d_dws", T.wqs[:], T.ws[:], [], ["wqs"])
     dma("y", "d_dv", T.vt[:], T.v[:], [], ["vt"])
@@ -166,15 +167,15 @@ def rank_program(g, core, T, topo):
     iota("ra", [(T.ra[:, 0:2], [[-15, 2]], 15), (T.ra[:, 2:4], [[-3855, 2]], 3840), (T.ra[:, 4:6], [[-225, 2]], 240), (T.ra[:, 6:16], [[0, 10]], 0)])
     iota("on", [(T.on[:, 0:4], [[0, 4]], 1)])
     iota("pa", [(T.pa[:, 0::2], [[0, 4], [-6, 2]], 8), (T.pa[:, 1::2], [[0, 4], [-3, 2]], 4)])
-    iota("tk", [(T.tk[:, 0:36:2], [[0, 9], [4368, 2]], 1), (T.tk[:, 1:36:2], [[0, 18]], 15), (T.tk[:, 36:60], [[0, 24]], 1),
-                (T.tk[:, 60:84], [[-4354, 2], [0, 12]], 4369), (T.tk[:, 84:96], [[0, 12]], 4369)])
-    iota("hk", [(T.hk[:, 0::2], [[0, 9], [16, 2]], 0), (T.hk[:, 1::2], [[0, 18]], 16)])
-    iota("rowt", [(T.rowt[:, 0:24:3], [[80, 2], [1, 4]], 0), (T.rowt[:, 1:24:3], [[80, 2], [1, 4]], 32),
-                  (T.rowt[:, 2:24:3], [[80, 2], [1, 4]], 48), (T.rowt[:, 24:32], [[1, 8]], 608)])
+    iota("tk0", [(T.tk[:, 0:54], [[0, 54]], 1), (T.tk[:, 54:126], [[0, 2], [-4354, 2], [0, 18]], 4369)])
+    iota("hk0", [(T.w[:, 0:54], [[0, 54]], 2), (T.w[:, 54:72], [[0, 18]], 16)])
+    iota("tk", [(T.tk[:, 22:108:6], [[0, 15]], 0), (T.tk[:, 23::6], [[0, 18]], 0), (T.tk[:, 5:18:6], [[0, 3]], 15), (T.tk[:, 112::6], [[0, 3]], 4369)], after=["tk0"])
+    iota("hk", [(T.w[:, 0:72:6], [[0, 12]], 0), (T.w[:, 5:72:6], [[0, 12]], 1)], after=["hk0"])
+    iota("rowt", [(T.rowt[:, 0:24:3], [[80, 2], [1, 4]], 64), (T.rowt[:, 1:24:3], [[80, 2], [1, 4]], 96),
+                  (T.rowt[:, 2:24:3], [[80, 2], [1, 4]], 112), (T.rowt[:, 24:32], [[1, 8]], 8)])
 
-    V(ms(T.kt[:], 0.0), [], ["ktz"])
     V(ms(T.et[:], 0.0), [], ["etz"])
-    names = ("rf", "gf", "of", "pf", "ge2", "r20", "lt4", "thr", "fix", "ev", "lt6", "b3", "b", "lo", "a", "hi", "t0", "t1", "t2", "t3", "g4")
+    names = ("rf", "gf", "of", "pf", "ge2", "r20", "lt4", "thr", "fix", "ev", "lt6", "b3", "b", "lo", "a", "hi", "t0", "t1", "t2", "t3", "g4", "fx0", "h5")
     one = {n: T.sc[:, i:i + 1] for i, n in enumerate(names)}
     V(cp(one["pf"], T.ip[:]), ["ip"], ["pf"])
     V(ts(T.si[:, 0:1], T.ip[:], 15, None, A.bitwise_and), ["ip"], ["si0"])
@@ -194,13 +195,11 @@ def rank_program(g, core, T, topo):
     V(ts(T.eq[:, 0:8], T.flat[:, 0:8], one["gf"], None, A.is_equal), ["flat", "rf"], ["eq"])
     V(tt(T.pr[:, 0:16], T.dm[:, 0:16], T.ra[:], A.mult), ["dm", "ra"], ["pr"])
 
-    for h in range(2):
-        S(T.rt[:, 512 * h:512 * (h + 1)], T.kt[:, 0:512], ACT.Copy, ["ktz"], "rtz", ["rtz"])
+    S(T.kt[:], T.et[:, 0:560], ACT.Copy, ["etz"], "ktz")
     for b in range(4):
-        S(T.et[:, 512 * b + b:512 * (b + 1):4], T.ident[:], ACT.Copy, ["ident", "etz"], "et%d" % b)
-    quant("qe", "et", ["et%d" % b for b in range(4)] + ["etz"], 0, 512)
-    S(T.rm[:], T.i16c[:], ACT.Sign, ["i16c"], "rm")
-    S(T.kw[:], T.dm[:], ACT.Copy, ["dm"], "kw", scale=8704.0, bias=-512.0)
+        S(T.et[:, 512 * b + b:512 * (b + 1):4], T.ident[:], ACT.Copy, ["ident", "etz", "ktz"], "et%d" % b)
+    ETK = ["et%d" % b for b in range(4)] + ["etz"]
+    V(ts(T.kw[:], T.dm[:], 8704.0, -512.0, A.mult, A.add), ["dm"], ["kw"])
     S(one["fix"], one["rf"], ACT.Copy, ["rf"], "fix", scale=-512.0, bias=7680.0 + HALF)
 
     def row_weights():
@@ -210,34 +209,43 @@ def rank_program(g, core, T, topo):
         S(T.on[:, 8:12], T.on[:, 0:4], ACT.Copy, ["on", "rf"], "od4", scale=one["of"])
         S(one["b"], one["b3"], ACT.Copy, ["b3", "lt6"], "b", scale=one["lt6"])
         S(T.on[:, 4:8], T.on[:, 0:4], ACT.Copy, ["on", "ev"], "ev4", scale=one["ev"])
-
-    def tables_tile():
         S(T.eq[:, 8:16], T.eq[:, 0:8], ACT.Copy, ["eq", "a"], "ag", scale=one["a"])
         S(one["lo"], one["b"], ACT.Copy, ["b", "ev"], "lo", scale=one["ev"])
         S(T.eq[:, 16:24], T.eq[:, 0:8], ACT.Copy, ["eq", "b"], "bg", scale=one["b"])
         for n in range(4):
             S(T.pb[:, n::4], T.on[:, 4:8] if n < 2 else T.on[:, 8:12], ACT.Copy, ["ev4", "od4"], "pb", ["pb"], scale=float(16 ** (3 - n)))
         S(T.eq[:, 24:32], T.eq[:, 0:8], ACT.Copy, ["eq", "lo"], "lg", scale=one["lo"])
+
+    def tables_tile():
         ag, bg, lg = [[T.eq[:, o + i:o + i + 1] for i in range(8)] for o in (8, 16, 24)]
-        fills = [(T.kt[:, 36:40], T.pa[:, 0:4], ag[1], "ag"), (T.kt[:, 44:48], T.pa[:, 0:4], ag[3], "ag"),
-                 (T.kt[:, 176:196:5], T.on[:, 0:4], ag[4], "ag"), (T.kt[:, 320:336], T.pa[:], ag[5], "ag"),
-                 (T.kt[:, 40:44], T.pb[:, 0:4], bg[2], "bg"), (T.kt[:, 33:34], T.on[:, 0:1], lg[0], "lg"),
-                 (T.kt[:, 272:288], T.pb[:], bg[5], "bg"), (T.kt[:, 368:384], T.pb[:], bg[6], "bg"), (T.kt[:, 224:244:5], T.on[:, 0:4], lg[4], "lg")]
-        for i, (out, src, f, key) in enumerate(fills):
-            S(out, src, ACT.Copy, ["pa", "on", key, "ktz", "rtz"] + (["pb"] if key == "bg" else []), "kt%d" % i, scale=f)
-        for i in (1, 2):
-            S(T.kt[:, 32 + 48 * i:48 + 48 * i], T.kt[:, 32:48], ACT.Copy, ["kt0", "kt1", "kt4", "kt5", "ktz"], "kt%d" % (8 + i))
-        return ["ktz"] + ["kt%d" % i for i in range(11)]
+
+        def each(q):
+            o = 4 * (12 + 18 * q)
+            return T.kt[:, o:o + 16:5]
+
+        def table(q, slot, n):
+            o = 4 * (12 + 18 * q + slot)
+            return T.kt[:, o:o + 4 * n]
+
+        fills = [(each(0), T.on[:, 0:4], ag[2]), (each(1), T.on[:, 0:4], ag[4]), (each(2), T.on[:, 0:4], lg[4]),
+                 (table(3, 0, 4), T.pb[:], bg[5]), (table(4, 0, 4), T.pa[:], ag[5]), (table(5, 0, 4), T.pb[:], bg[3]), (table(6, 0, 4), T.pa[:], ag[6]),
+                 (table(6, 4, 1), T.pb[:, 0:4], bg[2]), (table(0, 5, 1), T.pa[:, 0:4], ag[1]), (T.kt[:, 65:66], T.on[:, 0:1], lg[0])]
+        for out, src, f in fills:
+            S(out, src, ACT.Copy, ["pa", "pb", "on", "ag", "bg", "lg", "ktz"], "kt", ["kt"], scale=f)
+        S(T.rowt[0:64, 2:24:3], T.flat[0:64, 0:8], ACT.Copy, ["flat"], "rowt")
+        S(one["fx0"], one["fix"], ACT.Copy, ["fix"], "fx0", bias=-float(HALF))
+        return ["ktz", "kt"]
 
     def way_back_constants():
-        S(T.rowt[0:64, 2:24:3], T.flat[0:64, 0:8], ACT.Copy, ["flat"], "rowt", bias=600.0)
-        S(one["g4"], one["gf"], ACT.Copy, ["rf"], "g4", scale=4.0)
-        for gg in range(7):
-            o = 512 * (gg // 4) + 64 * (gg + 1) + gg % 4
+        S(one["g4"], one["gf"], ACT.Identity, ["rf", "fx0"], "g4", scale=4.0, bias=one["fx0"])
+        S(T.rt[:], T.et[:, 0:1024], ACT.Copy, ETK, "rtz", scale=0.0)
+        for i, gg in enumerate((3, 1, 2, 4, 5, 6, 0)):
+            o = 512 * (i // 4) + 64 * (gg + 1) + i % 4
             S(T.rt[:, o:o + 61:4], T.dm[:, 0:16], ACT.Copy, ["dm", "rtz"], "rt", ["rt"])
-        S(one["hi"], T.eq[:, 2:3], ACT.Identity, ["eq"], "hi", bias=T.eq[:, 4:5])
-        S(one["t0"], T.eq[:, 0:1], ACT.Copy, ["eq"], "t0", scale=-2.0, bias=2.0)
+        S(T.pr[:, 0:3], T.eq[:, 5:8], ACT.Copy, ["eq", "a"], "h5", accum_out=one["h5"])
         S(T.kd[:], T.dm[:], ACT.Copy, ["dm"], "kd", scale=34.0, bias=-2.0)
+        S(one["hi"], T.eq[:, 2:3], ACT.Identity, ["eq", "h5"], "hi", bias=one["h5"])
+        S(one["t0"], T.eq[:, 0:1], ACT.Copy, ["eq"], "t0", scale=-2.0, bias=2.0)
         S(one["t1"], one["hi"], ACT.Copy, ["hi"], "t1", scale=4088.0, bias=8.0)
         S(one["t2"], one["hi"], ACT.Copy, ["hi"], "t2", scale=252.0, bias=4.0)
         S(one["t3"], one["hi"], ACT.Identity, ["hi", "t0"], "t3", scale=14.0, bias=one["t0"])
@@ -248,7 +256,7 @@ def rank_program(g, core, T, topo):
     def send(k, pairs, sem):
         dst = T.cores[partner[k]]
         rid, pid, _ = topo.addr(dst)
-        eng = topo.engines(core, dst)[:8]
+        eng = topo.engines(core, dst)
         m = sum(1 << e for e in eng)
         for out, in_ in pairs:
             g.remote_dma(out, in_, T.sem[sem], T.sem.lsem, pid, rid, m)
@@ -267,25 +275,28 @@ def rank_program(g, core, T, topo):
 
     def quant_state(k):
         for lo, hi, h in HALVES:
-            quant("qx%d" % k, "x%d" % k, ["x%d_%d" % (k, b) for b in range(3)] + ["x%d_3%s" % (k, h)] if k else ["x0"], lo, hi, "qx%d%s" % (k, h))
+            quant("qx%d" % k, "x%d" % k, ["x%d_%d" % (k, b) for b in range(3)] + ["x%d_3%s" % (k, h)] if k else ["x0" + h], lo, hi, "qx%d%s" % (k, h))
 
     def signs_mm(k):
         q, s = "qx%d" % k, "sx%d" % k
         for i in range(2):
             for (lo, hi, h), bank in zip(HALVES, SCORE[i]):
-                mm(bank, HALF, "up", "ups", 128 * i, q, s, lo, ["up", "ups", q + h])
+                mm(bank, hi - lo, "up", "ups", 128 * i, q, s, lo, ["up", "ups", q + h])
 
     def signs_table(fill):
         for i, ((lo, hi, h), bank) in enumerate(zip(HALVES, SCORE[0])):
-            V(ts(T.tb1[:, lo:hi], T[bank][:, 0:HALF], 0.0, one["thr"], A.is_le, A.mult), [bank, "thr"], ["tb1" + h])
+            V(ts(T.tb1[:, lo:hi], T[bank][:, 0:hi - lo], 0.0, one["thr"], A.is_le, A.mult), [bank, "thr"], ["tb1" + h])
             fill(i)
         for i, ((lo, hi, h), bank) in enumerate(zip(HALVES, SCORE[1])):
-            V(tt(T.tb[:, lo:hi], T[bank][:, 0:HALF], T.tb1[:, lo:hi], A.is_gt), [bank, "tb1" + h], ["tb" + h])
+            V(tt(T.tb[:, lo:hi], T[bank][:, 0:hi - lo], T.tb1[:, lo:hi], A.is_gt), [bank, "tb1" + h], ["tb" + h])
             fill(2 + i)
 
     def unpack_mm(codes, scales, parts, banks):
         for b, bank in zip(parts, banks):
-            mm(bank, C, "qe", "qes", 128 * b, codes, scales, 0, ["qe"] + both(codes))
+            mm(bank, C, "qe", "qes", 128 * b, codes, scales, 0, ["qe%d" % b] + both(codes))
+
+    def unpack_tile(b):
+        quant("qe", "et", ETK, 128 * b, 128 * (b + 1), "qe%d" % b)
 
     def unpack_copy(dst, parts):
         for b in parts:
@@ -294,22 +305,14 @@ def rank_program(g, core, T, topo):
     def lgn(n):
         return T.lg[:, 20 * n:20 * n + 20]
 
-    def first_list(step, table=None):
-        if step == 0:
-            V(tt(T.lm[:], T[table][:].indirect(lgn(0)), T.dm[:], A.mult), [table, "dm", "lg0"], ["lm"])
-        elif step == 1:
-            V(scan(T.lsb[:], T.rm[:], T.lm[:], A.mult, A.add), ["rm", "lm"], ["lsb"])
-        else:
-            V(ts(lgn(1), T.lsb[:, 15::16], float(HALF), None, A.add), ["lsb"], ["lg1"])
-
     def flat_list(n, table, lst, key):
         S(T.lf[:, C * n:C * (n + 1)], T[table][:].indirect(lst), ACT.Copy, [table, key], "lf%d" % n)
 
-    def hold(out, n):
-        V(scan(T[out][:], T.kw[:], T.lf[:, C * n:C * (n + 1)], A.add, A.min), ["kw", "lf%d" % n], [out])
+    def hold(n):
+        V(scan(T["ls%d" % n][:], T.kw[:], T.lf[:, C * n:C * (n + 1)], A.add, A.min), ["kw", "lf%d" % n], ["ls%d" % n])
 
     def second_list():
-        V(ts(lgn(2), T.lsc[:, 15::16], one["fix"], None, A.add), ["lsc", "fix"], ["lg2"])
+        V(ts(lgn(2), T.ls2[:, 15::16], one["fix"], None, A.add), ["ls2", "fix"], ["lg2"])
 
     def gather(out, window, lst, rd, key, q):
         if q == "v":
@@ -325,42 +328,37 @@ def rank_program(g, core, T, topo):
         S(T.tbp[:], T.tb[:].indirect(T.sl[:, 20:40]), ACT.Copy, both("tb") + ["pl"], "tbp")
         signs_at(0, "tb", 0, "v")
         signs_at(2, "tb", 2, "s", HALF, C)
-        signs_at(1, "tb", 1, "v")
-        signs_at(3, "tbp", 2, "s")
         signs_at(2, "tb", 2, "v", 0, HALF)
-        return ["gt0_0", "gt1_0", "gt2_0", "gt2_%d" % HALF, "gt3_0"]
+        signs_at(3, "tbp", 2, "s", 0, 256)
+        signs_at(1, "tbp", 0, "v")
+        signs_at(3, "tbp", 2, "s", 256, C)
+        keys = ["gt0_0", "gt1_0", "gt2_0", "gt2_%d" % HALF, "gt3_0"]
+        return [keys, keys, keys + ["gt3_256"]]
 
-    V(ts(T.pw0[:], T.pint[:].indirect(T.ro[:]), -float(HALF), None, A.add), ["pint", "ro"], ["pw0"])
+    quant("qu", "ut", ["ut"], 0, 128)
     V(cp(T.sl[:, 20:40], pg32), ["pg32"], ["pl"])
     V(cp(lgn(0), kg32), ["kg32"], ["lg0"])
-    S(T.p2[:], T.pw0[:].indirect(T.sl[:, 20:40]), ACT.Copy, ["pw0", "pl"], "p2")
-    quant("qu", "ut", ["ut"], 0, 128)
+    unpack_tile(0)
+    unpack_tile(1)
+    V(ts(T.pw0[:], T.pint[:].indirect(T.ro[:]), -float(HALF), None, A.add), ["pint", "ro"], ["pw0"])
     ULK = ["ul0", "ul1"]
     S(T.ups[:], T.qus[:].indirect(T.ul[:]), ACT.Copy, ["qu"] + ULK, "ups")
-    flat_list(0, "p2", lgn(0), "lg0")
-    first_list(0, "pw0")
+    S(T.p2[:], T.pw0[:].indirect(T.sl[:, 20:40]), ACT.Copy, ["pw0", "pl"], "p2")
     V(cp(T.up[:].bitcast(dt.uint32), T.qu[:].bitcast(dt.uint32).indirect(T.ul[:])), ["qu"] + ULK, ["up"])
-    quant_state(0)
-    send_state(0)
-    signs_mm(0)
-    first_list(1)
-    KTK = tables_tile()
-    signs_table(lambda i: [lambda: hold("lsc", 0), lambda: first_list(2), second_list, lambda: quant("qk", "kt", KTK, 0, 136)][i]())
-    iota("st", [(T.st[:], [[0, 656]], 0)])
-    iota("flat2", [(T.flat[:, 128:C], [[1, C - 128]], 128)])
 
-    def differences(step):
-        if step == 0:
-            V(cp(T.lw[:, 20:60], T.lg[:, 20:60]), ["lg1", "lg2"], ["lw"])
-            V(ts(T.lw[:, 60:80], lgn(2), one["fix"], None, A.subtract), ["lg2", "fix"], ["lw3"])
-        elif step == 1:
-            for i in (1, 2):
-                V(tt(T.dd[:, i::4], T.lw[:, 20 * (3 - i):20 * (4 - i)], T.lw[:, 20 * (2 - i):20 * (3 - i)], A.subtract), ["lw", "lw0"], ["dd%d" % i])
-        else:
-            V(tt(T.dd[:, 0::4], T.lsd[:, 15::16], T.lw[:, 60:80], A.subtract), ["lsd", "lw3"], ["dd0"])
+    def held(n):
+        return T["ls%d" % n][:, 15::16]
+
+    def differences(*steps):
+        for i in steps:
+            hi, lo = (held(3 - i), held(2 - i) if i < 2 else T.lw[:])
+            V(tt(T.dd[:, i::4], hi, lo, A.subtract), ["ls%d" % (3 - i), "ls%d" % (2 - i) if i < 2 else "lw"], ["dd%d" % i])
 
     def chain(freed, fill):
-        V(tt(T.ti[:], T.b2[:, 0:96], T.tk[:], A.add), ["b2", "tk"], ["tia", "tib", "t5", "t6"])
+        def run(q, n=1, slot=None):
+            return T.w[:, 18 * q:18 * (q + n)] if slot is None else T.w[:, 18 * q + slot:18 * (q + n):6]
+
+        V(tt(run(8, 7), T.b2[:, 0:126], T.tk[:], A.add), ["b2", "tk", "tk0"], ["ti", "e5", "e6"])
         freed()
         fill(0)
         UP, DOWN = (3, 0x1111), (12, 15)
@@ -371,36 +369,35 @@ def rank_program(g, core, T, topo):
         def pick(out, src, kind, rd, wr):
             V(ts(out, src, kind[0], kind[1], A.arith_shift_right, A.bitwise_and), rd, wr)
 
-        times(T.pd[:, 40:64], T.ti[:, 60:84], T.ti[:, 36:60], ["tib", "t5"], "pe1")
-        times(T.pd[:, 0:9], T.ti[:, 1:36:4], T.ti[:, 0:36:4], ["tia"], "pd1")
-        V(cp(T.sv[:, 0:3], T.ti[:, 0:12:4]), ["tia"], ["s0"])
-        pick(T.bi[:, 24:36], T.pd[:, 52:64], UP, ["pe1"], ["bh"])
-        pick(T.sv[:, 3:12], T.pd[:, 0:9], UP, ["pd1"], ["s1", "s2", "s3"])
-        pick(T.bi[:, 0:12], T.pd[:, 40:52], DOWN, ["pe1"], ["b5l"])
-        times(T.pd[:, 64:76], T.ti[:, 84:96], T.bi[:, 24:36], ["t6", "bh"], "pe2")
-        times(T.pd[:, 9:18], T.ti[:, 2:36:4], T.sv[:, 3:12], ["tia", "s1", "s2", "s3"], "pd2")
+        times(T.pd[:, 0:18], run(13), run(8), ["ti"], "p3")
+        times(T.pd[:, 18:21], run(8, 1, 5), run(8, 1, 4), ["ti"], "p1")
+        times(T.pd[:, 24:60], run(11, 2), run(9, 2), ["ti", "e5", "e6"], "p5")
+        pick(T.e2[:, 18:36], T.pd[:, 0:18], DOWN, ["p3"], ["e3"])
+        pick(run(3, 1, 4), T.pd[:, 18:21], UP, ["p1", "hk0"], ["s1"])
+        pick(T.e2[:, 0:18], T.pd[:, 24:42], DOWN, ["p5"], ["e5l"])
+        pick(run(10), T.pd[:, 42:60], UP, ["p5"], ["e5"])
+        V(scan(T.pk[:, 0:18], run(3), T.e2[:, 18:36], A.mult, A.add), ["hk", "s1", "e3"], ["q3"])
+        times(T.pd[:, 60:78], run(14), T.e2[:, 0:18], ["ti", "e5l"], "p6")
+        times(T.pd[:, 21:24], run(14, 1, 4), run(3, 1, 4), ["ti", "s1"], "p2")
+        for i in range(3):
+            pick(run(i, 1, 4), T.pk[:, 5:18:6], DOWN, ["q3", "hk0"], ["s3%d" % i])
+        pick(run(11), T.pd[:, 60:78], UP, ["p6"], ["e6"])
+        pick(run(4, 1, 4), T.pd[:, 21:24], DOWN, ["p2"], ["s2"])
         fill(1)
-        pick(T.bi[:, 12:24], T.pd[:, 64:76], DOWN, ["pe2"], ["b6l"])
-        pick(T.sv[:, 6:15], T.pd[:, 9:18], DOWN, ["pd2"], ["s2", "s3", "s4"])
+        V(scan(T.pk[:, 18:72], run(0, 3), run(9, 3), A.mult, A.add), ["hk", "s30", "s31", "s32", "ti", "e5", "e6"], ["q6"])
         fill(2)
-        V(cp(T.ti[:, 60:84], T.bi[:, 0:24]), ["b5l", "b6l"], ["t5"])
-        times(T.pd[:, 18:27], T.ti[:, 3:36:4], T.sv[:, 6:15], ["tia", "s2", "s3", "s4"], "pd3")
+        pick(run(5, 3, 4), T.pk[:, 23:72:6], UP, ["q6"], ["s4"])
         fill(3)
-        V(scan(T.pk[:], T.hk[:], T.ti[:, 48:84], A.mult, A.add), ["hk", "tib", "t5"], ["pk"])
-        pick(T.sv[:, 9:18], T.pd[:, 18:27], UP, ["pd3"], ["s3", "s4", "s5"])
+        V(cp(T.st[:].indirect(T.scl[:]), T.w[:, 40:232:6]), ["ti", "e5", "e6", "s1", "s2", "s32", "s4", "scl"], ["st"])
         fill(4)
-        times(T.pd[:, 27:36], T.pk[:, 3::4], T.sv[:, 9:18], ["pk", "s3", "s4", "s5"], "pd4")
-        fill(5)
-        pick(T.sv[:, 12:21], T.pd[:, 27:36], DOWN, ["pd4"], ["s4", "s5", "s6"])
-        fill(6)
-        V(cp(T.st[:].indirect(T.scl[:]), T.sv[:]), ["s%d" % i for i in range(8)] + ["scl"], ["st"])
-        quant("qs", "st", ["st"], 0, 148)
+        quant("qs", "st", ["st"], 16, 164, at=0)
         for h in range(2):
             mm("b3", 128, "qr", "qrs", 128 * h, "qs", "qss", 20 * h, ["qr", "qs"], h == 0, h == 1)
 
-    def select(k):
+    def select(k, fill):
         for i in (1, 2, 3):
             V(ts(T.mt[:, i::4], T.b3[:, 0:20], one["t%d" % i], None, A.is_ge), ["b3", "t%d" % i], ["mt%d" % i])
+        fill(5)
         V(scan(T.af[:], T.mt[:], T.dd[:], A.mult, A.add), ["mt%d" % i for i in range(4)] + ["dd%d" % i for i in range(4)], ["af"])
         V(cp(T["al%d" % k][:], T.af[:, 3::4]), ["af"], ["al%d" % k])
 
@@ -410,13 +407,15 @@ def rank_program(g, core, T, topo):
         S(T.vb[:, HALF:C], T.tb1[:].indirect(T[a][:, 10:20]), ACT.Sign, both("tb1") + [a], "vb1")
         for h in range(2):
             gather(T.ym[:, HALF * h:HALF * (h + 1)], T.vb[:], T.ml[:, 10 * h:10 * h + 10], ["vb0", "vb1", "ml"], "ym%d" % h, "vs"[h])
-        V(scan(T.ysc[:, 0:C], T.kd[:], T.vb[:], A.add, A.min), ["kd", "vb0", "vb1"], ["ysc0"])
-        V(scan(T.ysc[:, C:2 * C], T.kd[:], T.ym[:], A.add, A.min), ["kd", "ym0", "ym1"], ["ysc1"])
+            if k == 0 and h == 0:
+                V(tt(T.dj[:, 20:40], held(0), T.sf[:, 80:100], A.subtract), ["ls0", "sf1"], ["dl"])
+        calls = [(scan(T.ysc[:, 0:C], T.kd[:], T.vb[:], A.add, A.min), ["kd", "vb0", "vb1"], ["ysc0"]),
+                 (scan(T.ysc[:, C:2 * C], T.kd[:], T.ym[:], A.add, A.min), ["kd", "ym0", "ym1"], ["ysc1"])]
         for o in range(0, n, 20):
-            V(tt(T.sf[:, o:o + 20], T.ysc[:, 15:C:16], T.ysc[:, C + 15::16], A.not_equal), ["ysc0", "ysc1"], ["df%d" % o])
-        V(tt(T.sf[:, 40:40 + n], T.sf[:, 0:n], T.dj[:, 0:n], A.mult), ["df0", "df20", "mj", "dl"], ["sf0"])
-        V(tt(T.sf[:, 80:80 + n], T.sf[:, 40:40 + n], T.pj[:, 0:n], A.add), ["sf0", "jw", "pp"], ["sf1"])
-        return lambda: V(cp(T.sl[:, 0:n], T.sf[:, 80:80 + n]), ["sf1"], ["sl", "pl"])
+            calls.append((tt(T.sf[:, o:o + 20], T.ysc[:, 15:C:16], T.ysc[:, C + 15::16], A.not_equal), ["ysc0", "ysc1"], ["df%d" % o]))
+        return calls + [(tt(T.sf[:, 40:40 + n], T.sf[:, 0:n], T.dj[:, 0:n], A.mult), ["df0", "df20", "mj", "dl"], ["sf0"]),
+                        (tt(T.sf[:, 80:80 + n], T.sf[:, 40:40 + n], T.pj[:, 0:n], A.add), ["sf0", "jw", "pp"], ["sf1"]),
+                        (cp(T.sl[:, 0:n], T.sf[:, 80:80 + n]), ["sf1"], ["sl", "pl"])]
 
     def carry(step):
         if step == 0:
@@ -426,76 +425,97 @@ def rank_program(g, core, T, topo):
             V(tt(T.dj[:, 20:40], T.dj[:, 20:40], T.sf[:, 0:20], A.add), ["df0"], ["dl"])
 
     FIRST = {
-        1: [(tt(T.pr[:], T.dm[:, 0:32], T.rowt[:], A.mult), ["dm", "rowt", "a"], ["pr", "prs"]), (ms(T.sv[:, 21:32], 0), [], ["s7"])],
-        2: [(scan(T.rsc[:], T.rm[:, 0:32], T.pr[:], A.mult, A.add), ["rm", "prs"], ["rsc"]), (cp(T.ml[:], mg32), ["mg32"], ["ml"])],
-        3: [(ts(T.scl[:], T.rsc[:, 15::16], one["g4"], None, A.add), ["rsc", "g4"], ["scl"]), (ms(T.mt[:, 0::4], 0.0), [], ["mt0"])],
-        4: [(cp(T.dd[:, 3::4], lgn(0)), ["lg0"], ["dd3"]), (ts(T.pj[:, 0:20], T.i20[:], 16.0, one["rf"], A.mult, A.add), ["i20", "rf"], ["jw"])],
-        0: [(cp(T.pj[:, 20:40], pg32), ["pg32"], ["pp"])],
-        6: [(ts(T.sf[:, 80:100], pg32, one["fix"], None, A.subtract), ["pg32", "fix"], ["sf1"]), (tt(T.dj[:, 0:20], mg32, T.pj[:, 0:20], A.subtract), ["mg32", "jw"], ["mj"])],
+        -1: [(scan(T.rsc[:], T.kw[:, 0:32], T.rowt[:], A.add, A.min), ["kw", "rowt"], ["rsc"]), (cp(T.ml[:], mg32), ["mg32"], ["ml"])],
+        0: [(ts(T.scl[:], T.rsc[:, 15::16], one["g4"], None, A.add), ["rsc", "g4"], ["scl"]), (ts(T.lw[:], lgn(0), one["fix"], None, A.subtract), ["lg0", "fix"], ["lw"]),
+            (cp(T.pj[:, 20:40], pg32), ["pg32"], ["pp"])],
+        2: [(ms(T.mt[:, 0::4], 0.0), [], ["mt0"])],
+        3: [(cp(T.dd[:, 3::4], lgn(0)), ["lg0"], ["dd3"]), (ts(T.pj[:, 0:20], T.i20[:], 16.0, one["rf"], A.mult, A.add), ["i20", "rf"], ["jw"]),
+            (ts(T.sf[:, 80:100], pg32, one["fix"], None, A.subtract), ["pg32", "fix"], ["sf1"])],
+        5: [(tt(T.dj[:, 0:20], mg32, T.pj[:, 0:20], A.subtract), ["mg32", "jw"], ["mj"])],
     }
 
     for k in range(3):
         qx, sx, first, last = "qx%d" % k, "sx%d" % k, k == 0, k == 2
         pw, nxt = "pw%d" % (k % 2), "pw%d" % (1 - k % 2)
-        if k:
-            flat_list(0, pw, lgn(1), "lg1")
-            quant_state(k)
-            send_state(k)
-            signs_mm(k)
-            hold("lsc", 0)
+        flat_list(2, "p2", lgn(0), "lg0")
+        if first:
+            KTK = tables_tile()
+        quant_state(k)
+        send_state(k)
+        signs_mm(k)
+        if first:
+            iota("st", [(T.st[:], [[0, 656]], 0)])
+            iota("flat2", [(T.flat[:, 128:C], [[1, C - 128]], 128)])
+            unpack_tile(2)
+            signs_table(lambda i: [lambda: unpack_tile(3), lambda: hold(2), lambda: None, second_list][i]())
+            quant("qk", "kt", KTK, 0, 140)
+        else:
+            hold(2)
             signs_table(lambda i: second_list() if i == 0 else None)
         GT = signs_of_candidates()
         unpack_mm(qx, sx, [0, 1, 2], ["b4", "b5", "b6"])
-        flat_list(1, pw, lgn(2), "lg2")
-        for b, (q, lo, at) in enumerate(BLOCKS):
-            quant(q, "gt", GT, lo, lo + 128, "qg%d" % b, at)
-            mm("b2", 128, q, q + "s", at, "qk", "qks", 8 - 4 * b, ["qg%d" % b, "qk"], b == 0, b == 2)
+        flat_list(1, pw, lgn(0), "lg0")
         if first:
             way_back_constants()
-            V(cp(T.lw[:, 0:20], lgn(0)), ["lg0"], ["lw0"])
-        differences(0)
-        hold("lsd", 1)
-        unpack_copy("fo", [0, 1, 2])
+        flat_list(3, pw, lgn(2), "lg2")
+        for b, (q, lo, at) in enumerate(BLOCKS):
+            quant(q, "gt", GT[b], lo, lo + 128, "qg%d" % b, at)
+            mm("b2", 128, q, q + "s", at, "qk", "qks", 12 - 6 * b, ["qg%d" % b, "qk"], b == 0, b == 2)
 
         def fill(i):
-            if i == 0:
-                differences(1)
-            if i == (5 if k else 6):
-                differences(2)
+            if i == (2 if first else 3):
+                differences(1, 2)
             if first:
                 for call in FIRST.get(i, []):
                     V(*call)
-                if i == 2:
-                    flat_list(0, pw, T.ml[:], "ml")
-                if i == 5:
+                if i == 4:
                     quant("qr", "rt", ["rt", "rtz"], 0, 256)
-            if k == 1 and i in (1, 2):
-                carry(i - 1)
+            if k == 1 and i in (4, 5):
+                carry(i - 4)
 
-        chain(lambda: unpack_mm(qx, sx, [3], ["b2"]), fill)
+        fill(-1)
+        hold(1)
+        unpack_copy("fo", [0, 1, 2])
         if first:
-            hold("lsc", 0)
-        unpack_mm("rq%d" % k, "rs%d" % k, [0, 1, 2, 3], ["b4", "b5", "b6", "b7"])
-        select(k)
+            flat_list(0, pw, T.ml[:], "ml")
+        early = 0 if first else 2
+
+        def unpack_arrived(parts):
+            unpack_mm("rq%d" % k, "rs%d" % k, parts, ["b%d" % (4 + b) for b in parts])
+
+        chain(lambda: (unpack_mm(qx, sx, [3], ["b2"]), unpack_arrived(range(early)), unpack_copy("fp", range(early))), fill)
+        hold(3)
+        differences(0)
+        unpack_arrived(range(early, 4))
+        select(k, fill)
         send_list(k)
         if first:
-            V(tt(T.dj[:, 20:40], T.lsc[:, 15::16], T.sf[:, 80:100], A.subtract), ["lsc", "sf1"], ["dl"])
-        unpack_copy("fp", [0])
-        as_list = sigma(k)
-        unpack_copy("fp", [1, 2, 3])
-        for t in range(4):
-            gather(T.zt[:, t:4 * C:4], T.fp[:, C * t:C * (t + 1)], T["rl%d" % k][:], ["fp%d" % t, "rl%d" % k], "zt%d" % t, "vs"[t % 2])
-            if t == 0:
-                as_list()
+            hold(0)
+        unpack_copy("fp", [early])
+        later = sigma(k)
+
+        def go_on(n):
+            for _ in range(n):
+                V(*later.pop(0))
+
+        go_on(len(later) - (3 if last else 2))
+        unpack_copy("fp", range(early + 1, 4))
+        rl = "rl%d" % k
+        for t in (0, 1):
+            gather(T.zt[:, t:4 * C:4], T.fp[:, C * t:C * (t + 1)], T[rl][:], ["fp%d" % t, rl], "zt%d" % t, "vs"[t])
+        for lo, hi, h in RUNS:
+            go_on(0 if last else 1)
+            for t in (2, 3):
+                gather(T.zt[:, 4 * lo + t:4 * hi:4], T.fp[:, C * t:C * (t + 1)], T[rl][:, lo // 16:hi // 16], ["fp%d" % t, rl], "zt%d%s" % (t, h), "vs"[t % 2])
         if last:
             S(T.plo[:, 0:C], T.flat[:].indirect(T.al2[:]), ACT.Copy, ["flat", "flat2", "al2"], "plo0")
         else:
             S(T[nxt][:], T[pw][:].indirect(T.sl[:, 0:20]), ACT.Copy, [pw, "sl"], nxt)
-        for lo, hi, h in HALVES:
-            quant("qz", "zt", ["zt%d" % t for t in range(4)], lo, hi, "qz" + h)
-        for (lo, hi, h), bank in zip(HALVES, ("b4", "b0")):
-            mm(bank, HALF, "wq", "wqs", 0, "qz", "qzs", lo, ["wq", "wqs", "qz" + h])
-            S(T.hs[:, lo:hi], T[bank][:, 0:HALF], ACT.Copy, [bank], "hs0" + h, scale=0.03125)
+        for lo, hi, h in RUNS:
+            quant("qz", "zt", ["zt0", "zt1", "zt2" + h, "zt3" + h], lo, hi, "qz" + h)
+        for (lo, hi, h), bank in zip(RUNS, ("b4", "b0")):
+            mm(bank, hi - lo, "wq", "wqs", 0, "qz", "qzs", lo, ["wq", "wqs", "qz" + h])
+            S(T.hs[:, lo:hi], T[bank][:, 0:hi - lo], ACT.Copy, [bank], "hs0" + h, scale=0.03125)
         for b in (1, 3, 2):
             mm("b%d" % (4 + b), C, "wq", "wqs", 128 * b, "qz", "qzs", 0, ["wq", "wqs"] + both("qz"))
             S(T.hs[:, C * b:C * (b + 1)], T["b%d" % (4 + b)][:, 0:C], ACT.Copy, ["b%d" % (4 + b)], "hs%d" % b, scale=0.03125)
@@ -503,15 +523,14 @@ def rank_program(g, core, T, topo):
         for lo, hi, h in HALVES:
             S(T.ks[:, lo:hi], T.hs[:, 3 * C:4 * C].indirect(T[a][:, lo // 16:hi // 16]), ACT.Copy, ["hs3", a], "ks" + h)
         if not last:
-            first_list(0, nxt)
-            first_list(1)
+            V(cp(T.p2[:], T[nxt][:].indirect(T.sl[:, 20:40])), [nxt, "pl"], ["p2"])
         else:
+            go_on(1)
             quant("qv", "vt", ["vt"], 0, 128)
+            go_on(2)
         for b in range(3):
             V(tt(T[x][:, b::4], T.hs[:, C * b:C * (b + 1)].indirect(T[a][:]), T.fo[:, C * b:C * (b + 1)], A.add),
               (both("hs0") if b == 0 else ["hs%d" % b]) + [a, "fo%d" % b], ["%s_%d" % (x, b)])
-            if not last and b == 0:
-                first_list(2)
         for lo, hi, h in HALVES:
             V(tt(T[x][:, 4 * lo + 3:4 * hi:4], T.b2[:, lo:hi], T.ks[:, lo:hi], A.add), ["b2", "ks" + h], [x + "_3" + h])
 
@@ -519,12 +538,12 @@ def rank_program(g, core, T, topo):
     dma("s", "d_op", T.pl[:], T.plo[0::16, :], ["plo0", "plo1"], [])
     quant_state(3)
     for (lo, hi, h), bank in zip(HALVES, ("b0", "b1")):
-        mm(bank, HALF, "qv", "qvs", 0, "qx3", "sx3", lo, ["qv", "qx3" + h])
+        mm(bank, hi - lo, "qv", "qvs", 0, "qx3", "sx3", lo, ["qv", "qx3" + h])
         dma("y", "d_oc", T.oc[:, 4 * lo:4 * hi], T.qx3[:, lo:hi].bitcast(dt.uint8), ["qx3" + h], [])
     for i in range(4):
         dma("y", "d_os", T.osc[4 * i:4 * i + 4, :], T.sx3[32 * i:32 * i + 4, :], both("qx3"), [])
     for (lo, hi, h), bank in zip(HALVES, ("b0", "b1")):
-        V(cp(T.yo[:, lo:hi], T[bank][:, 0:HALF]), [bank], ["yo" + h])
+        V(cp(T.yo[:, lo:hi], T[bank][:, 0:hi - lo]), [bank], ["yo" + h])
         dma("s", "d_oy", T.y[:, lo:hi], T.yo[:, lo:hi], ["yo" + h], [])
     for s, v in cnt.items():
         g.wait_ge(T.sem[s], v)

import numpy as np
from concourse.bass import DstId, RemoteDMATransfer
from concourse.mybir import dt, AluOpType, AxisListType, ActivationFunctionType

C = 320
STEPS = [1, 2, 4]
HALF = 160
BIG, TINY = 2.0 ** 96, 2.0 ** -100

SCRATCH = {}
SEMAPHORES = ["vs", "ss", "ts", "gs", "lsem"]


def _sb(name, cols, d):
    SCRATCH[name] = ("sbuf", [128, cols], d)


for _k in range(4):
    _sb("x%d" % _k, 4 * C, "bfloat16")
    _sb("qx%d" % _k, C, "float8_e4m3fn_x4")
    _sb("sx%d" % _k, C, "uint8")
for _k in range(3):
    _sb("rq%d" % _k, C, "float8_e4m3fn_x4")
    _sb("rs%d" % _k, C, "uint8")
    _sb("al%d" % _k, 20, "uint16")
    _sb("rl%d" % _k, 20, "uint16")
    SEMAPHORES += ["aq%d" % _k, "ar%d" % _k]
for _k in range(2):
    _sb("pw%d" % _k, C, "bfloat16")
for _n, _c, _d in [
    ("ut", 512, "bfloat16"), ("vt", 512, "bfloat16"), ("zt", 4 * C, "bfloat16"),
    ("gt", 4 * C, "bfloat16"), ("st", 656, "bfloat16"), ("kt", 560, "bfloat16"), ("et", 2048, "bfloat16"), ("rt", 1024, "bfloat16"),
    ("pint", C, "int32"), ("l32", 60, "int32"), ("p2", C, "bfloat16"),
    ("ip", 1, "int32"), ("si", 4, "int32"), ("sc", 24, "float32"),
    ("i16c", C, "bfloat16"), ("flat", C, "float32"), ("i20", 20, "int32"), ("iu", 16, "int32"),
    ("pj", 40, "float32"), ("dj", 40, "float32"), ("ro", 20, "uint16"), ("ml", 20, "uint16"), ("ul", 16, "uint16"),
    ("dm", C, "bfloat16"), ("kw", C, "bfloat16"), ("kd", C, "bfloat16"), ("ident", 128, "bfloat16"),
    ("ra", 16, "float32"), ("pr", 32, "float32"), ("eq", 32, "float32"), ("pa", 16, "float32"), ("pb", 16, "float32"), ("on", 12, "float32"),
    ("rowt", 32, "float32"), ("rsc", 32, "float32"), ("scl", 2, "uint16"),
    ("tk", 126, "float32"), ("w", 270, "int32"), ("pk", 72, "int32"), ("pd", 80, "int32"), ("e2", 36, "int32"),
    ("tb1", C, "bfloat16"), ("tb", C, "bfloat16"), ("tbp", C, "bfloat16"), ("vb", C, "bfloat16"), ("ym", C, "bfloat16"), ("ysc", 2 * C, "bfloat16"),
    ("lf", 4 * C, "bfloat16"), ("ls0", C, "float32"), ("ls1", C, "float32"), ("ls2", C, "float32"), ("ls3", C, "float32"),
    ("lg", 60, "uint16"), ("lw", 20, "float32"),
    ("mt", 80, "float32"), ("dd", 80, "float32"), ("af", 80, "float32"),
    ("sf", 120, "float32"), ("sl", 40, "uint16"),
    ("fo", 3 * C, "bfloat16"), ("fp", 4 * C, "bfloat16"), ("hs", 4 * C, "float32"), ("ks", C, "float32"), ("yo", C, "float32"), ("plo", 2 * C, "float32"),
]:
    _sb(_n, _c, _d)
for _n, _c in [("qu", 128), ("up", 256), ("qv", 128), ("wq", 512), ("qe", 512), ("qr", 256), ("qk", 140), ("qg", 256), ("qh", 128), ("qs", 148), ("qz", C)]:
    _sb(_n, _c, "float8_e4m3fn_x4")
    _sb(_n + "s", _c, "uint8")
for _k in range(8):
    SCRATCH["b%d" % _k] = ("psum", [128, 512], "float32")
LOADS = ["dxa", "dxb", "du", "dp", "dk", "dm", "dg", "dw", "dws", "dv", "oy", "oc", "os", "op"]
LOADS = ["d_" + _n for _n in LOADS]
SEMAPHORES += LOADS

A = AluOpType
ACT = ActivationFunctionType
HALVES = ((0, HALF, "a"), (HALF, C, "b"))
RUNS = ((0, 192, "a"), (192, C, "b"))
BLOCKS = (("qg", 0, 0), ("qg", 128, 128), ("qh", 192, 0))
SCORE = (("b0", "b3"), ("b1", "b7"))


def both(key):
    return [key + "a", key + "b"]


def rank_program(g, core, T, topo):
    rank = T.rank_of(core)
    if rank is None:
        return
    queues = {"v": (g.vector, "vs"), "s": (g.scalar, "ss"), "t": (g.tensor, "ts"), "g": (g, "gs"), "y": (g.sync, None)}
    cnt, seen, lastw, readers = {}, {}, {}, {}

    def need(qn, reads, writes, free=()):
        out = {}
        for k in list(reads) + list(writes):
            for s, v in lastw.get(k, []):
                if k in writes and k in free:
                    continue
                out[s] = max(out.get(s, 0), v)
        for k in writes:
            for s, v in readers.get(k, []):
                out[s] = max(out.get(s, 0), v)
        for s, v in out.items():
            if seen.get((qn, s), 0) < v:
                queues[qn][0].wait_ge(T.sem[s], v)
                seen[(qn, s)] = v

    def done(reads, writes, s, v, free=()):
        for k in reads:
            readers.setdefault(k, []).append((s, v))
        for k in writes:
            if k in free:
                lastw.setdefault(k, []).append((s, v))
            else:
                lastw[k] = [(s, v)]
                readers[k] = []

    def op(qn, fn, reads, writes, free=()):
        need(qn, reads, writes, free)
        s = queues[qn][1]
        cnt[s] = cnt.get(s, 0) + 1
        fn().then_inc(T.sem[s], 1)
        done(reads, writes, s, cnt[s], free)

    def dma(qn, s, out, in_, reads, writes, free=()):
        need(qn, reads, writes, free)
        cnt[s] = cnt.get(s, 0) + 16
        queues[qn][0].dma_start(out, in_).then_inc(T.sem[s], 16)
        done(reads, writes, s, cnt[s], free)

    def V(fn, reads, writes, free=()):
        op("v", fn, reads, writes, free)

    def ts(out, i, s1, s2, *ops):
        return lambda: g.vector.tensor_scalar(out, i, s1, s2, *ops)

    def tt(out, a, b, o):
        return lambda: g.vector.tensor_tensor(out, a, b, o)

    def cp(out, i):
        return lambda: g.vector.tensor_copy(out, i)

    def ms(ap, c):
        return lambda: g.vector.memset(ap, c)

    def scan(out, a, b, o0, o1):
        return lambda: g.vector.tensor_tensor_scan(out, a, b, 0.0, o0, o1)

    def S(out, i, f, reads, writes, free=(), **kw):
        op("s", lambda: g.scalar.activation(out, i, f, **kw), reads, [writes], free)

    def quant(q, src, tiles, lo, hi, key=None, at=None):
        sc = (q + "s") if q[:2] != "qx" else "sx" + q[2:]
        at = lo if at is None else at
        V(lambda: g.vector.quantize_mx(T[q][:, at:at + hi - lo], T[sc][:, at:at + hi - lo], T[src][:, 4 * lo:4 * hi]), tiles, [key or q])

    def mm(bank, n, w, ws, wa, x, xs, xa, reads, start=True, stop=True):
        op("t", lambda: g.tensor.matmul_mx(T[bank][:, 0:n], T[w][:, wa:wa + 128], T[ws][:, wa:wa + 128], T[x][:, xa:xa + n], T[xs][:, xa:xa + n], start, stop),
           reads, [bank], [] if start else [bank])

    def iota(key, parts, cm=0, after=()):
        for out, pattern, base in parts:
            op("g", lambda: g.iota(out, pattern, base, cm, allow_small_or_imprecise_dtypes=True), list(after), [key], [key])

    kg32, pg32, mg32 = T.l32[:, 0:20], T.l32[:, 20:40], T.l32[:, 40:60]
    dma("s", "d_du", T.ut[:], T.u[:], [], ["ut"])
    dma("y", "d_dg", pg32, T.pg[:], [], ["pg32"])
    dma("y", "d_dk", kg32, T.kg[:], [], ["kg32"])
    for r in range(16):
        dma("y" if r % 2 and r < 15 else "s", "d_dp", T.pint[r::16, :], T.pg[:], [], ["pint"], ["pint"])
    dma("y", "d_dm", mg32, T.mg[:], [], ["mg32"])
    for lo, hi, h in HALVES:
        dma("y", "d_dx" + h, T.x0[:, 4 * lo:4 * hi], T.x[:, 4 * lo:4 * hi], [], ["x0" + h])
    dma("y", "d_dw", T.wq[:].bitcast(dt.uint8), T.wc[:], [], ["wq"])
    dma("y", "d_dws", T.wqs[:], T.ws[:], [], ["wqs"])
    dma("y", "d_dv", T.vt[:], T.v[:], [], ["vt"])

    iota("ip", [(T.ip[:], [[0, 1]], 0)], 1)
    iota("i20", [(T.i20[:], [[1, 20]], 0)])
    iota("flat", [(T.flat[:, 0:128], [[1, 128]], 0)])
    iota("i16c", [(T.i16c[:], [[0, 20], [1, 16]], 0)])
    iota("iu", [(T.iu[:], [[0, 2], [16, 8]], 0)])
    iota("ra", [(T.ra[:, 0:2], [[-15, 2]], 15), (T.ra[:, 2:4], [[-3855, 2]], 3840), (T.ra[:, 4:6], [[-225, 2]], 240), (T.ra[:, 6:16], [[0, 10]], 0)])
    iota("on", [(T.on[:, 0:4], [[0, 4]], 1)])
    iota("pa", [(T.pa[:, 0::2], [[0, 4], [-6, 2]], 8), (T.pa[:, 1::2], [[0, 4], [-3, 2]], 4)])
    iota("tk0", [(T.tk[:, 0:54], [[0, 54]], 1), (T.tk[:, 54:126], [[0, 2], [-4354, 2], [0, 18]], 4369)])
    iota("hk0", [(T.w[:, 0:54], [[0, 54]], 2), (T.w[:, 54:72], [[0, 18]], 16)])
    iota("tk", [(T.tk[:, 22:108:6], [[0, 15]], 0), (T.tk[:, 23::6], [[0, 18]], 0), (T.tk[:, 5:18:6], [[0, 3]], 15), (T.tk[:, 112::6], [[0, 3]], 4369)], after=["tk0"])
    iota("hk", [(T.w[:, 0:72:6], [[0, 12]], 0), (T.w[:, 5:72:6], [[0, 12]], 1)], after=["hk0"])
    iota("rowt", [(T.rowt[:, 0:24:3], [[80, 2], [1, 4]], 64), (T.rowt[:, 1:24:3], [[80, 2], [1, 4]], 96),
                  (T.rowt[:, 2:24:3], [[80, 2], [1, 4]], 112), (T.rowt[:, 24:32], [[1, 8]], 8)])

    V(ms(T.et[:], 0.0), [], ["etz"])
    names = ("rf", "gf", "of", "pf", "ge2", "r20", "lt4", "thr", "fix", "ev", "lt6", "b3", "b", "lo", "a", "hi", "t0", "t1", "t2", "t3", "g4", "fx0", "h5")
    one = {n: T.sc[:, i:i + 1] for i, n in enumerate(names)}
    V(cp(one["pf"], T.ip[:]), ["ip"], ["pf"])
    V(ts(T.si[:, 0:1], T.ip[:], 15, None, A.bitwise_and), ["ip"], ["si0"])
    V(ts(T.si[:, 1:2], T.ip[:], 4, None, A.arith_shift_right), ["ip"], ["si1"])
    V(ts(T.si[:, 2:3], T.ip[:], 1, None, A.bitwise_and), ["ip"], ["si2"])
    V(ts(T.ident[:], T.flat[:, 0:128], one["pf"], None, A.is_equal), ["flat", "pf"], ["ident"])
    V(cp(T.sc[:, 0:3], T.si[:, 0:3]), ["si0", "si1", "si2"], ["rf"])
    V(cp(T.ul[:, 0:8], T.iu[:, 0:8]), ["iu"], ["ul0"])
    V(ts(one["r20"], one["rf"], 20.0, None, A.mult), ["rf"], ["r20"])
    V(ts(one["ge2"], one["rf"], 2.0, None, A.is_ge), ["rf"], ["ge2"])
    V(ts(one["lt4"], one["rf"], 4.0, BIG, A.is_lt, A.mult), ["rf"], ["lt4"])
    V(ts(T.dm[:], T.i16c[:], one["rf"], None, A.is_equal), ["i16c", "rf"], ["dm"])
    V(ts(T.ro[:], T.i20[:], one["r20"], None, A.add), ["i20", "r20"], ["ro"])
    V(ts(T.ul[:, 8:16], T.iu[:, 8:16], one["ge2"], None, A.add), ["iu", "ge2"], ["ul1"])
    V(ts(one["thr"], one["lt4"], TINY, None, A.max), ["lt4"], ["thr"])
    V(ts(one["lt6"], one["rf"], 6.0, None, A.is_lt), ["rf"], ["lt6"])
    V(ts(T.eq[:, 0:8], T.flat[:, 0:8], one["gf"], None, A.is_equal), ["flat", "rf"], ["eq"])
    V(tt(T.pr[:, 0:16], T.dm[:, 0:16], T.ra[:], A.mult), ["dm", "ra"], ["pr"])

    S(T.kt[:], T.et[:, 0:560], ACT.Copy, ["etz"], "ktz")
    for b in range(4):
        S(T.et[:, 512 * b + b:512 * (b + 1):4], T.ident[:], ACT.Copy, ["ident", "etz", "ktz"], "et%d" % b)
    ETK = ["et%d" % b for b in range(4)] + ["etz"]
    V(ts(T.kw[:], T.dm[:], 8704.0, -512.0, A.mult, A.add), ["dm"], ["kw"])
    S(one["fix"], one["rf"], ACT.Copy, ["rf"], "fix", scale=-512.0, bias=7680.0 + HALF)

    def row_weights():
        S(one["b3"], one["ge2"], ACT.Copy, ["ge2"], "b3", scale=2.0, bias=1.0)
        S(one["ev"], one["of"], ACT.Copy, ["rf"], "ev", scale=-1.0, bias=1.0)
        S(T.pr[:, 16:32], T.pr[:, 0:16], ACT.Copy, ["pr"], "a", accum_out=one["a"])
        S(T.on[:, 8:12], T.on[:, 0:4], ACT.Copy, ["on", "rf"], "od4", scale=one["of"])
        S(one["b"], one["b3"], ACT.Copy, ["b3", "lt6"], "b", scale=one["lt6"])
        S(T.on[:, 4:8], T.on[:, 0:4], ACT.Copy, ["on", "ev"], "ev4", scale=one["ev"])
        S(T.eq[:, 8:16], T.eq[:, 0:8], ACT.Copy, ["eq", "a"], "ag", scale=one["a"])
        S(one["lo"], one["b"], ACT.Copy, ["b", "ev"], "lo", scale=one["ev"])
        S(T.eq[:, 16:24], T.eq[:, 0:8], ACT.Copy, ["eq", "b"], "bg", scale=one["b"])
        for n in range(4):
            S(T.pb[:, n::4], T.on[:, 4:8] if n < 2 else T.on[:, 8:12], ACT.Copy, ["ev4", "od4"], "pb", ["pb"], scale=float(16 ** (3 - n)))
        S(T.eq[:, 24:32], T.eq[:, 0:8], ACT.Copy, ["eq", "lo"], "lg", scale=one["lo"])

    def tables_tile():
        ag, bg, lg = [[T.eq[:, o + i:o + i + 1] for i in range(8)] for o in (8, 16, 24)]

        def each(q):
            o = 4 * (12 + 18 * q)
            return T.kt[:, o:o + 16:5]

        def table(q, slot, n):
            o = 4 * (12 + 18 * q + slot)
            return T.kt[:, o:o + 4 * n]

        fills = [(each(0), T.on[:, 0:4], ag[2]), (each(1), T.on[:, 0:4], ag[4]), (each(2), T.on[:, 0:4], lg[4]),
                 (table(3, 0, 4), T.pb[:], bg[5]), (table(4, 0, 4), T.pa[:], ag[5]), (table(5, 0, 4), T.pb[:], bg[3]), (table(6, 0, 4), T.pa[:], ag[6]),
                 (table(6, 4, 1), T.pb[:, 0:4], bg[2]), (table(0, 5, 1), T.pa[:, 0:4], ag[1]), (T.kt[:, 65:66], T.on[:, 0:1], lg[0])]
        for out, src, f in fills:
            S(out, src, ACT.Copy, ["pa", "pb", "on", "ag", "bg", "lg", "ktz"], "kt", ["kt"], scale=f)
        S(T.rowt[0:64, 2:24:3], T.flat[0:64, 0:8], ACT.Copy, ["flat"], "rowt")
        S(one["fx0"], one["fix"], ACT.Copy, ["fix"], "fx0", bias=-float(HALF))
        return ["ktz", "kt"]

    def way_back_constants():
        S(one["g4"], one["gf"], ACT.Identity, ["rf", "fx0"], "g4", scale=4.0, bias=one["fx0"])
        S(T.rt[:], T.et[:, 0:1024], ACT.Copy, ETK, "rtz", scale=0.0)
        for i, gg in enumerate((3, 1, 2, 4, 5, 6, 0)):
            o = 512 * (i // 4) + 64 * (gg + 1) + i % 4
            S(T.rt[:, o:o + 61:4], T.dm[:, 0:16], ACT.Copy, ["dm", "rtz"], "rt", ["rt"])
        S(T.pr[:, 0:3], T.eq[:, 5:8], ACT.Copy, ["eq", "a"], "h5", accum_out=one["h5"])
        S(T.kd[:], T.dm[:], ACT.Copy, ["dm"], "kd", scale=34.0, bias=-2.0)
        S(one["hi"], T.eq[:, 2:3], ACT.Identity, ["eq", "h5"], "hi", bias=one["h5"])
        S(one["t0"], T.eq[:, 0:1], ACT.Copy, ["eq"], "t0", scale=-2.0, bias=2.0)
        S(one["t1"], one["hi"], ACT.Copy, ["hi"], "t1", scale=4088.0, bias=8.0)
        S(one["t2"], one["hi"], ACT.Copy, ["hi"], "t2", scale=252.0, bias=4.0)
        S(one["t3"], one["hi"], ACT.Identity, ["hi", "t0"], "t3", scale=14.0, bias=one["t0"])

    row_weights()
    partner = [rank ^ s for s in STEPS]

    def send(k, pairs, sem):
        dst = T.cores[partner[k]]
        rid, pid, _ = topo.addr(dst)
        eng = topo.engines(core, dst)
        m = sum(1 << e for e in eng)
        for out, in_ in pairs:
            g.remote_dma(out, in_, T.sem[sem], T.sem.lsem, pid, rid, m)
            cnt["lsem"] = cnt.get("lsem", 0) + len(eng)
            cnt[sem] = cnt.get(sem, 0) + len(eng)

    def send_state(k):
        need("g", both("qx%d" % k), [])
        send(k, [(T["rq%d" % k][:].bitcast(dt.uint8), T["qx%d" % k][:].bitcast(dt.uint8)), (T["rs%d" % k][:], T["sx%d" % k][:])], "aq%d" % k)
        done([], both("rq%d" % k), "aq%d" % k, cnt["aq%d" % k])

    def send_list(k):
        need("g", ["al%d" % k], [])
        send(k, [(T["rl%d" % k][:], T["al%d" % k][:])], "ar%d" % k)
        done([], ["rl%d" % k], "ar%d" % k, cnt["ar%d" % k])

    def quant_state(k):
        for lo, hi, h in HALVES:
            quant("qx%d" % k, "x%d" % k, ["x%d_%d" % (k, b) for b in range(3)] + ["x%d_3%s" % (k, h)] if k else ["x0" + h], lo, hi, "qx%d%s" % (k, h))

    def signs_mm(k):
        q, s = "qx%d" % k, "sx%d" % k
        for i in range(2):
            for (lo, hi, h), bank in zip(HALVES, SCORE[i]):
                mm(bank, hi - lo, "up", "ups", 128 * i, q, s, lo, ["up", "ups", q + h])

    def signs_table(fill):
        for i, ((lo, hi, h), bank) in enumerate(zip(HALVES, SCORE[0])):
            V(ts(T.tb1[:, lo:hi], T[bank][:, 0:hi - lo], 0.0, one["thr"], A.is_le, A.mult), [bank, "thr"], ["tb1" + h])
            fill(i)
        for i, ((lo, hi, h), bank) in enumerate(zip(HALVES, SCORE[1])):
            V(tt(T.tb[:, lo:hi], T[bank][:, 0:hi - lo], T.tb1[:, lo:hi], A.is_gt), [bank, "tb1" + h], ["tb" + h])
            fill(2 + i)

    def unpack_mm(codes, scales, parts, banks):
        for b, bank in zip(parts, banks):
            mm(bank, C, "qe", "qes", 128 * b, codes, scales, 0, ["qe%d" % b] + both(codes))

    def unpack_tile(b):
        quant("qe", "et", ETK, 128 * b, 128 * (b + 1), "qe%d" % b)

    def unpack_copy(dst, parts):
        for b in parts:
            S(T[dst][:, C * b:C * (b + 1)], T["b%d" % (4 + b)][:, 0:C], ACT.Copy, ["b%d" % (4 + b)], "%s%d" % (dst, b))

    def lgn(n):
        return T.lg[:, 20 * n:20 * n + 20]

    def flat_list(n, table, lst, key):
        S(T.lf[:, C * n:C * (n + 1)], T[table][:].indirect(lst), ACT.Copy, [table, key], "lf%d" % n)

    def hold(n):
        V(scan(T["ls%d" % n][:], T.kw[:], T.lf[:, C * n:C * (n + 1)], A.add, A.min), ["kw", "lf%d" % n], ["ls%d" % n])

    def second_list():
        V(ts(lgn(2), T.ls2[:, 15::16], one["fix"], None, A.add), ["ls2", "fix"], ["lg2"])

    def gather(out, window, lst, rd, key, q):
        if q == "v":
            V(cp(out, window.indirect(lst)), rd, [key])
        else:
            S(out, window.indirect(lst), ACT.Copy, rd, key)

    def signs_at(n, table, src, q, lo=0, hi=C):
        keys = both("tb") if table == "tb" else [table]
        gather(T.gt[:, 4 * lo + n:4 * hi:4], T[table][:], T.lg[:, 20 * src + lo // 16:20 * src + hi // 16], keys + ["lg%d" % src], "gt%d_%d" % (n, lo), q)

    def signs_of_candidates():
        S(T.tbp[:], T.tb[:].indirect(T.sl[:, 20:40]), ACT.Copy, both("tb") + ["pl"], "tbp")
        signs_at(0, "tb", 0, "v")
        signs_at(2, "tb", 2, "s", HALF, C)
        signs_at(2, "tb", 2, "v", 0, HALF)
        signs_at(3, "tbp", 2, "s", 0, 256)
        signs_at(1, "tbp", 0, "v")
        signs_at(3, "tbp", 2, "s", 256, C)
        keys = ["gt0_0", "gt1_0", "gt2_0", "gt2_%d" % HALF, "gt3_0"]
        return [keys, keys, keys + ["gt3_256"]]

    quant("qu", "ut", ["ut"], 0, 128)
    V(cp(T.sl[:, 20:40], pg32), ["pg32"], ["pl"])
    V(cp(lgn(0), kg32), ["kg32"], ["lg0"])
    unpack_tile(0)
    unpack_tile(1)
    V(ts(T.pw0[:], T.pint[:].indirect(T.ro[:]), -float(HALF), None, A.add), ["pint", "ro"], ["pw0"])
    ULK = ["ul0", "ul1"]
    S(T.ups[:], T.qus[:].indirect(T.ul[:]), ACT.Copy, ["qu"] + ULK, "ups")
    S(T.p2[:], T.pw0[:].indirect(T.sl[:, 20:40]), ACT.Copy, ["pw0", "pl"], "p2")
    V(cp(T.up[:].bitcast(dt.uint32), T.qu[:].bitcast(dt.uint32).indirect(T.ul[:])), ["qu"] + ULK, ["up"])

    def held(n):
        return T["ls%d" % n][:, 15::16]

    def differences(*steps):
        for i in steps:
            hi, lo = (held(3 - i), held(2 - i) if i < 2 else T.lw[:])
            V(tt(T.dd[:, i::4], hi, lo, A.subtract), ["ls%d" % (3 - i), "ls%d" % (2 - i) if i < 2 else "lw"], ["dd%d" % i])

    def chain(freed, fill):
        def run(q, n=1, slot=None):
            return T.w[:, 18 * q:18 * (q + n)] if slot is None else T.w[:, 18 * q + slot:18 * (q + n):6]

        V(tt(run(8, 7), T.b2[:, 0:126], T.tk[:], A.add), ["b2", "tk", "tk0"], ["ti", "e5", "e6"])
        freed()
        fill(0)
        UP, DOWN = (3, 0x1111), (12, 15)

        def times(out, table, state, rd, key):
            V(tt(out, table, state, A.mult), rd, [key])

        def pick(out, src, kind, rd, wr):
            V(ts(out, src, kind[0], kind[1], A.arith_shift_right, A.bitwise_and), rd, wr)

        times(T.pd[:, 0:18], run(13), run(8), ["ti"], "p3")
        times(T.pd[:, 18:21], run(8, 1, 5), run(8, 1, 4), ["ti"], "p1")
        times(T.pd[:, 24:60], run(11, 2), run(9, 2), ["ti", "e5", "e6"], "p5")
        pick(T.e2[:, 18:36], T.pd[:, 0:18], DOWN, ["p3"], ["e3"])
        pick(run(3, 1, 4), T.pd[:, 18:21], UP, ["p1", "hk0"], ["s1"])
        pick(T.e2[:, 0:18], T.pd[:, 24:42], DOWN, ["p5"], ["e5l"])
        pick(run(10), T.pd[:, 42:60], UP, ["p5"], ["e5"])
        V(scan(T.pk[:, 0:18], run(3), T.e2[:, 18:36], A.mult, A.add), ["hk", "s1", "e3"], ["q3"])
        times(T.pd[:, 60:78], run(14), T.e2[:, 0:18], ["ti", "e5l"], "p6")
        times(T.pd[:, 21:24], run(14, 1, 4), run(3, 1, 4), ["ti", "s1"], "p2")
        for i in range(3):
            pick(run(i, 1, 4), T.pk[:, 5:18:6], DOWN, ["q3", "hk0"], ["s3%d" % i])
        pick(run(11), T.pd[:, 60:78], UP, ["p6"], ["e6"])
        pick(run(4, 1, 4), T.pd[:, 21:24], DOWN, ["p2"], ["s2"])
        fill(1)
        V(scan(T.pk[:, 18:72], run(0, 3), run(9, 3), A.mult, A.add), ["hk", "s30", "s31", "s32", "ti", "e5", "e6"], ["q6"])
        fill(2)
        pick(run(5, 3, 4), T.pk[:, 23:72:6], UP, ["q6"], ["s4"])
        fill(3)
        V(cp(T.st[:].indirect(T.scl[:]), T.w[:, 40:232:6]), ["ti", "e5", "e6", "s1", "s2", "s32", "s4", "scl"], ["st"])
        fill(4)
        quant("qs", "st", ["st"], 16, 164, at=0)
        for h in range(2):
            mm("b3", 128, "qr", "qrs", 128 * h, "qs", "qss", 20 * h, ["qr", "qs"], h == 0, h == 1)

    def select(k, fill):
        for i in (1, 2, 3):
            V(ts(T.mt[:, i::4], T.b3[:, 0:20], one["t%d" % i], None, A.is_ge), ["b3", "t%d" % i], ["mt%d" % i])
        fill(5)
        V(scan(T.af[:], T.mt[:], T.dd[:], A.mult, A.add), ["mt%d" % i for i in range(4)] + ["dd%d" % i for i in range(4)], ["af"])
        V(cp(T["al%d" % k][:], T.af[:, 3::4]), ["af"], ["al%d" % k])

    def sigma(k):
        a, n = "al%d" % k, 40 if k < 2 else 20
        V(ts(T.vb[:, 0:HALF], T.tb1[:].indirect(T[a][:, 0:10]), 0.0, None, A.is_gt), both("tb1") + [a], ["vb0"])
        S(T.vb[:, HALF:C], T.tb1[:].indirect(T[a][:, 10:20]), ACT.Sign, both("tb1") + [a], "vb1")
        for h in range(2):
            gather(T.ym[:, HALF * h:HALF * (h + 1)], T.vb[:], T.ml[:, 10 * h:10 * h + 10], ["vb0", "vb1", "ml"], "ym%d" % h, "vs"[h])
            if k == 0 and h == 0:
                V(tt(T.dj[:, 20:40], held(0), T.sf[:, 80:100], A.subtract), ["ls0", "sf1"], ["dl"])
        calls = [(scan(T.ysc[:, 0:C], T.kd[:], T.vb[:], A.add, A.min), ["kd", "vb0", "vb1"], ["ysc0"]),
                 (scan(T.ysc[:, C:2 * C], T.kd[:], T.ym[:], A.add, A.min), ["kd", "ym0", "ym1"], ["ysc1"])]
        for o in range(0, n, 20):
            calls.append((tt(T.sf[:, o:o + 20], T.ysc[:, 15:C:16], T.ysc[:, C + 15::16], A.not_equal), ["ysc0", "ysc1"], ["df%d" % o]))
        return calls + [(tt(T.sf[:, 40:40 + n], T.sf[:, 0:n], T.dj[:, 0:n], A.mult), ["df0", "df20", "mj", "dl"], ["sf0"]),
                        (tt(T.sf[:, 80:80 + n], T.sf[:, 40:40 + n], T.pj[:, 0:n], A.add), ["sf0", "jw", "pp"], ["sf1"]),
                        (cp(T.sl[:, 0:n], T.sf[:, 80:80 + n]), ["sf1"], ["sl", "pl"])]

    def carry(step):
        if step == 0:
            V(cp(T.pj[:, 20:40], T.sf[:, 100:120]), ["sf1"], ["pp"])
            V(ts(T.sf[:, 0:20], T.sf[:, 60:80], -2.0, None, A.mult), ["sf0"], ["df0"])
        else:
            V(tt(T.dj[:, 20:40], T.dj[:, 20:40], T.sf[:, 0:20], A.add), ["df0"], ["dl"])

    FIRST = {
        -1: [(scan(T.rsc[:], T.kw[:, 0:32], T.rowt[:], A.add, A.min), ["kw", "rowt"], ["rsc"]), (cp(T.ml[:], mg32), ["mg32"], ["ml"])],
        0: [(ts(T.scl[:], T.rsc[:, 15::16], one["g4"], None, A.add), ["rsc", "g4"], ["scl"]), (ts(T.lw[:], lgn(0), one["fix"], None, A.subtract), ["lg0", "fix"], ["lw"]),
            (cp(T.pj[:, 20:40], pg32), ["pg32"], ["pp"])],
        2: [(ms(T.mt[:, 0::4], 0.0), [], ["mt0"])],
        3: [(cp(T.dd[:, 3::4], lgn(0)), ["lg0"], ["dd3"]), (ts(T.pj[:, 0:20], T.i20[:], 16.0, one["rf"], A.mult, A.add), ["i20", "rf"], ["jw"]),
            (ts(T.sf[:, 80:100], pg32, one["fix"], None, A.subtract), ["pg32", "fix"], ["sf1"])],
        5: [(tt(T.dj[:, 0:20], mg32, T.pj[:, 0:20], A.subtract), ["mg32", "jw"], ["mj"])],
    }

    for k in range(3):
        qx, sx, first, last = "qx%d" % k, "sx%d" % k, k == 0, k == 2
        pw, nxt = "pw%d" % (k % 2), "pw%d" % (1 - k % 2)
        flat_list(2, "p2", lgn(0), "lg0")
        if first:
            KTK = tables_tile()
        quant_state(k)
        send_state(k)
        signs_mm(k)
        if first:
            iota("st", [(T.st[:], [[0, 656]], 0)])
            iota("flat2", [(T.flat[:, 128:C], [[1, C - 128]], 128)])
            unpack_tile(2)
            signs_table(lambda i: [lambda: unpack_tile(3), lambda: hold(2), lambda: None, second_list][i]())
            quant("qk", "kt", KTK, 0, 140)
        else:
            hold(2)
            signs_table(lambda i: second_list() if i == 0 else None)
        GT = signs_of_candidates()
        unpack_mm(qx, sx, [0, 1, 2], ["b4", "b5", "b6"])
        flat_list(1, pw, lgn(0), "lg0")
        if first:
            way_back_constants()
        flat_list(3, pw, lgn(2), "lg2")
        for b, (q, lo, at) in enumerate(BLOCKS):
            quant(q, "gt", GT[b], lo, lo + 128, "qg%d" % b, at)
            mm("b2", 128, q, q + "s", at, "qk", "qks", 12 - 6 * b, ["qg%d" % b, "qk"], b == 0, b == 2)

        def fill(i):
            if i == (2 if first else 3):
                differences(1, 2)
            if first:
                for call in FIRST.get(i, []):
                    V(*call)
                if i == 4:
                    quant("qr", "rt", ["rt", "rtz"], 0, 256)
            if k == 1 and i in (4, 5):
                carry(i - 4)

        fill(-1)
        hold(1)
        unpack_copy("fo", [0, 1, 2])
        if first:
            flat_list(0, pw, T.ml[:], "ml")
        early = 0 if first else 2

        def unpack_arrived(parts):
            unpack_mm("rq%d" % k, "rs%d" % k, parts, ["b%d" % (4 + b) for b in parts])

        chain(lambda: (unpack_mm(qx, sx, [3], ["b2"]), unpack_arrived(range(early)), unpack_copy("fp", range(early))), fill)
        hold(3)
        differences(0)
        unpack_arrived(range(early, 4))
        select(k, fill)
        send_list(k)
        if first:
            hold(0)
        unpack_copy("fp", [early])
        later = sigma(k)

        def go_on(n):
            for _ in range(n):
                V(*later.pop(0))

        go_on(len(later) - (3 if last else 2))
        unpack_copy("fp", range(early + 1, 4))
        rl = "rl%d" % k
        for t in (0, 1):
            gather(T.zt[:, t:4 * C:4], T.fp[:, C * t:C * (t + 1)], T[rl][:], ["fp%d" % t, rl], "zt%d" % t, "vs"[t])
        for lo, hi, h in RUNS:
            go_on(0 if last else 1)
            for t in (2, 3):
                gather(T.zt[:, 4 * lo + t:4 * hi:4], T.fp[:, C * t:C * (t + 1)], T[rl][:, lo // 16:hi // 16], ["fp%d" % t, rl], "zt%d%s" % (t, h), "vs"[t % 2])
        if last:
            S(T.plo[:, 0:C], T.flat[:].indirect(T.al2[:]), ACT.Copy, ["flat", "flat2", "al2"], "plo0")
        else:
            S(T[nxt][:], T[pw][:].indirect(T.sl[:, 0:20]), ACT.Copy, [pw, "sl"], nxt)
        for lo, hi, h in RUNS:
            quant("qz", "zt", ["zt0", "zt1", "zt2" + h, "zt3" + h], lo, hi, "qz" + h)
        for (lo, hi, h), bank in zip(RUNS, ("b4", "b0")):
            mm(bank, hi - lo, "wq", "wqs", 0, "qz", "qzs", lo, ["wq", "wqs", "qz" + h])
            S(T.hs[:, lo:hi], T[bank][:, 0:hi - lo], ACT.Copy, [bank], "hs0" + h, scale=0.03125)
        for b in (1, 3, 2):
            mm("b%d" % (4 + b), C, "wq", "wqs", 128 * b, "qz", "qzs", 0, ["wq", "wqs"] + both("qz"))
            S(T.hs[:, C * b:C * (b + 1)], T["b%d" % (4 + b)][:, 0:C], ACT.Copy, ["b%d" % (4 + b)], "hs%d" % b, scale=0.03125)
        a, x = "al%d" % k, "x%d" % (k + 1)
        for lo, hi, h in HALVES:
            S(T.ks[:, lo:hi], T.hs[:, 3 * C:4 * C].indirect(T[a][:, lo // 16:hi // 16]), ACT.Copy, ["hs3", a], "ks" + h)
        if not last:
            V(cp(T.p2[:], T[nxt][:].indirect(T.sl[:, 20:40])), [nxt, "pl"], ["p2"])
        else:
            go_on(1)
            quant("qv", "vt", ["vt"], 0, 128)
            go_on(2)
        for b in range(3):
            V(tt(T[x][:, b::4], T.hs[:, C * b:C * (b + 1)].indirect(T[a][:]), T.fo[:, C * b:C * (b + 1)], A.add),
              (both("hs0") if b == 0 else ["hs%d" % b]) + [a, "fo%d" % b], ["%s_%d" % (x, b)])
        for lo, hi, h in HALVES:
            V(tt(T[x][:, 4 * lo + 3:4 * hi:4], T.b2[:, lo:hi], T.ks[:, lo:hi], A.add), ["b2", "ks" + h], [x + "_3" + h])

    S(T.plo[:, C:2 * C], T.pw0[:].indirect(T.sl[:, 0:20]), ACT.Copy, ["pw0", "sl"], "plo1", bias=float(HALF))
    dma("s", "d_op", T.pl[:], T.plo[0::16, :], ["plo0", "plo1"], [])
    quant_state(3)
    for (lo, hi, h), bank in zip(HALVES, ("b0", "b1")):
        mm(bank, hi - lo, "qv", "qvs", 0, "qx3", "sx3", lo, ["qv", "qx3" + h])
        dma("y", "d_oc", T.oc[:, 4 * lo:4 * hi], T.qx3[:, lo:hi].bitcast(dt.uint8), ["qx3" + h], [])
    for i in range(4):
        dma("y", "d_os", T.osc[4 * i:4 * i + 4, :], T.sx3[32 * i:32 * i + 4, :], both("qx3"), [])
    for (lo, hi, h), bank in zip(HALVES, ("b0", "b1")):
        V(cp(T.yo[:, lo:hi], T[bank][:, 0:hi - lo]), [bank], ["yo" + h])
        dma("s", "d_oy", T.y[:, lo:hi], T.yo[:, lo:hi], ["yo" + h], [])
    for s, v in cnt.items():
        g.wait_ge(T.sem[s], v)
